import numpy as np
import ml_dtypes


def mxq(x, axis, fmt="e4m3"):
    dtype, down = {"e4m3": (ml_dtypes.float8_e4m3fn, 7), "e5m2": (ml_dtypes.float8_e5m2, 14)}[fmt]
    v = np.moveaxis(np.asarray(x, np.float32).astype(ml_dtypes.bfloat16).astype(np.float64), axis, -1)
    blocks = v.reshape(v.shape[:-1] + (-1, 32))
    amax = np.abs(blocks).max(-1, keepdims=True)
    byte = np.maximum(np.where(amax > 0, np.frexp(amax)[1] - 1 + 127, 0) - down, 1)
    scale = np.exp2(byte - 127.0)
    codes = (blocks / scale).astype(np.float32).astype(dtype).astype(np.float64)
    return np.moveaxis((codes * scale).reshape(v.shape), -1, axis)


WIDE = False


def mx_kscale(k):
    if not WIDE:
        return np.ones(k)
    levels = np.array([10, -10, 5, -5, 0])
    if k % 512:
        return np.exp2(np.random.permutation(np.resize(levels, k // 32))).repeat(32)
    a = np.empty((k // 512, 16))
    for p in range(k // 512):
        a[p, :8] = np.random.permutation(np.resize(levels, 8))
        for g in range(8):
            far = levels[np.abs(levels - a[p, g]) >= 10]
            a[p, g + 8] = far[np.random.randint(len(far))]
    return np.exp2(a.ravel()).repeat(32)


def f64(x):
    return np.asarray(x).astype(np.float64)


def striped(idx):
    return np.tile(np.asarray(idx).reshape(-1, 16).T, (8, 1)).astype(np.uint16)


def unstriped(offs):
    return offs[:16].T.reshape(-1).astype(np.int64)


B, N, T, D, DV, NQ = 1, 512, 2048, 512, 256, 512


def setup_inputs():
    n = np.random.standard_normal
    idx = np.sort(np.random.permutation(T)[:B * N].reshape(B, N), axis=1).reshape(-1)
    s = mx_kscale(D)[:, None]
    u = np.ones(T)
    u[idx] = mx_kscale(B * N)
    r = np.random.uniform(0.5, 2.0, T)
    qidx = np.random.permutation(T)[:B * NQ]
    k = n((D, T)) / s
    v = n((DV, T)) / (u * r)
    return {
        "xq": (n((D, T)) * s * (0.80 / np.sqrt(D))).astype(np.float32),
        "kT": k.astype(np.float32),
        "vT": v.astype(np.float32),
        "vs": np.tile(u * r, (128, 1)).astype(np.float32),
        "offs": striped(idx),
        "qoffs": striped(qidx),
    }


def reference(xq, kT, vT, vs, offs, qoffs):
    idx = unstriped(offs)
    k = f64(kT)
    v = f64(vT)
    pick = lambda x: x[:, idx].reshape(x.shape[0], B, N).transpose(1, 0, 2)
    q = f64(xq)[:, unstriped(qoffs)].reshape(D, B, NQ).transpose(1, 0, 2)
    score = mxq(q, 1, "e4m3").transpose(0, 2, 1) @ mxq(pick(k), 1, "e4m3")
    m = score.max(-1, keepdims=True)
    p = np.exp(score - m)
    total = p.sum(-1, keepdims=True)
    w = p * pick(f64(vs))[:, :1, :]
    y = mxq(w, 2, "e4m3") @ mxq(pick(v).transpose(0, 2, 1), 1, "e4m3")
    y = y / total
    out = np.zeros((DV, T))
    out[:, unstriped(qoffs)] = y.transpose(2, 0, 1).reshape(-1, B * NQ)
    return out

@@ -1,0 +1,258 @@
+from contextlib import ExitStack
+
+import concourse.mybir as mybir
+from concourse.masks import make_identity
+
+F32 = mybir.dt.float32
+BF16 = mybir.dt.bfloat16
+U32 = mybir.dt.uint32
+U16 = mybir.dt.uint16
+U8 = mybir.dt.uint8
+FP8X4 = mybir.dt.float8_e4m3fn_x4
+COPY_OUT = "p t x -> p x t"
+EXP = mybir.ActivationFunctionType.Exp
+MULT = mybir.AluOpType.mult
+MAX = mybir.AluOpType.max
+AXIS_X = mybir.AxisListType.X
+
+P = 128
+PACK = 4
+T = 2048
+D = 512
+DV = 256
+N = 512
+NQ = 512
+PER_LIST_COLUMN = 16
+Q_CHUNKS = NQ // P
+V_CHUNKS = DV // P
+HALVES = 2
+HALF_Q = NQ // HALVES
+PSUM_BANKS = 8
+
+FLOPS = 2 * NQ * N * D + 2 * NQ * N * DV
+BYTES = 4 * (2 * D * T + DV * T + T + DV * T) + 2 * P * (N + NQ) // PER_LIST_COLUMN
+
+
+def tile_attend_mod_sorted_kernel(tc, xq, kT, vT, vs, offs, qoffs, out):
+    nc = tc.nc
+    with ExitStack() as ctx:
+        keep = ctx.enter_context(tc.tile_pool(name="keep", bufs=1))
+        psum = ctx.enter_context(tc.psum_pool(name="psum", bufs=PSUM_BANKS))
+
+        k_list = keep.tile([P, N // PER_LIST_COLUMN], U16, name="k_list")
+        q_list = keep.tile([P, NQ // PER_LIST_COLUMN], U16, name="q_list")
+        nc.sync.dma_start(k_list[:], offs)
+        nc.sync.dma_start(q_list[:], qoffs)
+
+        vs_window = keep.tile([P, T], F32, name="vs_window")
+        nc.vector.memset(vs_window[:], 0.0)
+        table_column = keep.tile([P, 1], F32, name="table_column")
+        nc.vector.memset(table_column[:], 0.0)
+        nc.scalar.activation(table_column[:], table_column[:], EXP)
+
+        ident = keep.tile([P, P], F32, name="ident")
+        make_identity(nc, ident[:])
+        ident_bf16 = keep.tile([P, P], BF16, name="ident_bf16")
+        nc.scalar.copy(ident_bf16[:], ident[:])
+        out_windows = [keep.tile([P, T], F32, name="out_window%d" % e) for e in range(V_CHUNKS)]
+        for window in out_windows:
+            nc.gpsimd.memset(window[:], 0.0)
+
+        def load(rows, name):
+            tile = keep.tile([P, T], F32, name=name)
+            nc.sync.dma_start(tile[:], rows)
+            return tile
+
+        k_rows = kT.rearrange("(p t) c -> p t c", t=PACK)
+        q_rows = xq.rearrange("(p t) c -> p t c", t=PACK)
+        k_tiles = [load(k_rows[:, 0, :], "k_tile0")]
+        nc.sync.dma_start(vs_window[0:1, :], vs[0:1, :])
+        k_tiles.extend([load(k_rows[:, t, :], "k_tile%d" % t) for t in range(1, PACK)])
+        q_tiles = [load(q_rows[:, t, :], "q_tile%d" % t) for t in range(PACK)]
+        v_tiles = [load(vT[e * P : (e + 1) * P, :], "v_tile%d" % e) for e in range(V_CHUNKS)]
+
+        def quantize(grouped, width, name):
+            codes = keep.tile([P, width], U32, align_bytes=64, name=name + "_codes")
+            scales = keep.tile([P, width], U8, align_bytes=64, name=name + "_scales")
+            nc.vector.quantize_mx(
+                out=codes[:].bitcast(FP8X4),
+                scales=scales[:],
+                in_=grouped.rearrange("p c t -> p (c t)"),
+            )
+            return codes, scales
+
+        k_grouped = keep.tile([P, N, PACK], BF16, align_bytes=64, name="k_grouped")
+        nc.vector.tensor_copy(k_grouped[:, :, 0], k_tiles[0][:].indirect(k_list[:]))
+
+        vs_picked = keep.tile([P, N], F32, name="vs_picked")
+        nc.vector.tensor_copy(vs_picked[:], vs_window[:].indirect(k_list[:]))
+        column_bank = psum.tile([P, PACK, P], F32, name="bank")
+        for t in range(PACK):
+            nc.tensor.transpose(column_bank[:, t, :], vs_picked[:, t::PACK], ident[:])
+        vs_column = keep.tile([P, PACK], F32, name="vs_column")
+        nc.scalar.copy(vs_column[:], column_bank[:, :, 0])
+        row_bank = psum.tile([P, PACK, P], F32, name="bank")
+        for t in range(PACK):
+            nc.tensor.transpose(row_bank[:, t, :], vs_column[:, t : t + 1].to_broadcast([P, P]), ident[:])
+        vs_row = keep.tile([P, PACK, P], F32, name="vs_row")
+        nc.scalar.copy(vs_row[:], row_bank[:])
+
+        for t in range(1, PACK):
+            nc.vector.tensor_copy(k_grouped[:, :, t], k_tiles[t][:].indirect(k_list[:]))
+        k_codes, k_scales = quantize(k_grouped[:], N, "k")
+
+        q_grouped = keep.tile([P, NQ, PACK], BF16, align_bytes=64, name="q_grouped")
+        for t in range(PACK - 1):
+            nc.vector.tensor_copy(q_grouped[:, :, t], q_tiles[t][:].indirect(q_list[:]))
+
+        half_queries = [slice(h * HALF_Q, (h + 1) * HALF_Q) for h in range(HALVES)]
+        half_lists = [
+            q_list[:, h * HALF_Q // PER_LIST_COLUMN : (h + 1) * HALF_Q // PER_LIST_COLUMN] for h in range(HALVES)
+        ]
+        neg_max = keep.tile([P, Q_CHUNKS], F32, name="neg_max")
+        total = keep.tile([P, Q_CHUNKS], F32, name="total")
+        inv_total = keep.tile([P, Q_CHUNKS], F32, name="inv_total")
+        w_grouped = [keep.tile([P, HALF_Q, PACK], BF16, align_bytes=64, name="w_grouped%d" % h) for h in range(HALVES)]
+
+        def gather_last_queries(h):
+            last = PACK - 1
+            nc.vector.tensor_copy(q_grouped[:, half_queries[h], last], q_tiles[last][:].indirect(half_lists[h]))
+
+        def quantize_queries(h):
+            return quantize(q_grouped[:, half_queries[h], :], HALF_Q, "q%d" % h)
+
+        def scores(b, codes, scales):
+            start = b * P % HALF_Q
+            bank = psum.tile([P, N], F32, name="bank")
+            nc.tensor.matmul_mx(
+                out=bank[:],
+                lhsT=codes[:, start : start + P].bitcast(FP8X4),
+                lhsT_scale=scales[:, start : start + P],
+                rhs=k_codes[:].bitcast(FP8X4),
+                rhs_scale=k_scales[:],
+                start=True,
+                stop=True,
+            )
+            return bank
+
+        def softmax(b, bank):
+            nc.vector.tensor_reduce(neg_max[:, b : b + 1], bank[:], AXIS_X, MAX, negate=True)
+            prob = keep.tile([P, PACK, P], F32, name="prob%d" % b)
+            nc.scalar.activation(
+                prob[:],
+                bank[:].rearrange("p (s t) -> p t s", t=PACK),
+                EXP,
+                bias=neg_max[:, b : b + 1],
+                accum_out=total[:, b : b + 1],
+            )
+            return prob
+
+        def w_columns(b):
+            h, i = divmod(b, Q_CHUNKS // HALVES)
+            return w_grouped[h][:, i * P : (i + 1) * P, :]
+
+        def multiply_on_gpsimd(b, prob):
+            weights = keep.tile([P, PACK, P], BF16, name="weights%d" % b)
+            nc.gpsimd.tensor_tensor(weights[:], prob[:], vs_row[:], MULT)
+            return weights
+
+        def turn_weights(b, weights):
+            bank = psum.tile([P, PACK, P], BF16, name="bank")
+            for t in range(PACK):
+                nc.tensor.transpose(bank[:, t, :], weights[:, t, :], ident_bf16[:])
+            nc.scalar.copy(w_columns(b), bank[:].rearrange(COPY_OUT))
+
+        def turn_probs(prob):
+            bank = psum.tile([P, PACK, P], F32, name="bank")
+            for t in range(PACK):
+                nc.tensor.transpose(bank[:, t, :], prob[:, t, :], ident[:])
+            return bank
+
+        def multiply_on_vector(b, bank):
+            nc.vector.tensor_tensor(
+                w_columns(b),
+                bank[:].rearrange(COPY_OUT),
+                vs_column[:].unsqueeze(1).to_broadcast([P, P, PACK]),
+                MULT,
+            )
+
+        def gather_values(e):
+            picked = keep.tile([P, N], F32, name="v_picked%d" % e)
+            nc.vector.tensor_copy(picked[:], v_tiles[e][:].indirect(k_list[:]))
+            return picked
+
+        def turn_values(e, picked):
+            bank = psum.tile([P, PACK, P], F32, name="bank")
+            for t in range(PACK):
+                nc.tensor.transpose(bank[:, t, :], picked[:, t::PACK], ident[:])
+            grouped = keep.tile([P, P, PACK], BF16, align_bytes=64, name="v_grouped%d" % e)
+            nc.scalar.copy(grouped[:], bank[:].rearrange(COPY_OUT))
+            return grouped
+
+        def products(values, halves, name):
+            v_codes, v_scales = values
+            bank = psum.tile([P, len(halves), HALF_Q], F32, name="bank")
+            for i, (w_codes, w_scales) in enumerate(halves):
+                nc.tensor.matmul_mx(
+                    out=bank[:, i, :],
+                    lhsT=v_codes[:].bitcast(FP8X4),
+                    lhsT_scale=v_scales[:],
+                    rhs=w_codes[:].bitcast(FP8X4),
+                    rhs_scale=w_scales[:],
+                    start=True,
+                    stop=True,
+                )
+            sums = keep.tile([P, len(halves) * HALF_Q], F32, name=name)
+            nc.scalar.copy(sums[:], bank[:].rearrange("p h q -> p (h q)"))
+            return sums
+
+        def inverse_totals():
+            nc.vector.reciprocal(inv_total[:], total[:])
+            bank = psum.tile([P, Q_CHUNKS, P], F32, name="bank")
+            for b in range(Q_CHUNKS):
+                nc.tensor.transpose(bank[:, b, :], inv_total[:, b : b + 1].to_broadcast([P, P]), ident[:])
+            inverse = keep.tile([P, NQ], F32, name="inverse")
+            nc.scalar.copy(inverse[:], bank[:].rearrange("p b q -> p (b q)"))
+            return inverse
+
+        def put_back(e, listed, sums, inverse):
+            nc.vector.tensor_tensor(out_windows[e][:].indirect(listed), sums[:], inverse, MULT)
+
+        gather_last_queries(0)
+        q_half0 = quantize_queries(0)
+        gather_last_queries(1)
+        score0 = scores(0, *q_half0)
+        score1 = scores(1, *q_half0)
+        prob0 = softmax(0, score0)
+        weights0 = multiply_on_gpsimd(0, prob0)
+        q_half1 = quantize_queries(1)
+        prob1 = softmax(1, score1)
+        weights1 = multiply_on_gpsimd(1, prob1)
+        score2 = scores(2, *q_half1)
+        score3 = scores(3, *q_half1)
+        prob2 = softmax(2, score2)
+        weights2 = multiply_on_gpsimd(2, prob2)
+        prob3 = softmax(3, score3)
+        turn_weights(0, weights0)
+        picked0 = gather_values(0)
+        grouped0 = turn_values(0, picked0)
+        turned3 = turn_probs(prob3)
+        turn_weights(1, weights1)
+        picked1 = gather_values(1)
+        values0 = quantize(grouped0[:], P, "v0")
+        w_half0 = quantize(w_grouped[0][:], HALF_Q, "w0")
+        inverse = inverse_totals()
+        turn_weights(2, weights2)
+        multiply_on_vector(3, turned3)
+        grouped1 = turn_values(1, picked1)
+        sums00 = products(values0, [w_half0], "sums00")
+        w_half1 = quantize(w_grouped[1][:], HALF_Q, "w1")
+        values1 = quantize(grouped1[:], P, "v1")
+        sums01 = products(values0, [w_half1], "sums01")
+        sums1 = products(values1, [w_half0, w_half1], "sums1")
+
+        put_back(0, half_lists[0], sums00, inverse[:, half_queries[0]])
+        put_back(0, half_lists[1], sums01, inverse[:, half_queries[1]])
+        nc.sync.dma_start(out[0:P, :], out_windows[0][:])
+        put_back(1, q_list[:], sums1, inverse[:])
+        nc.sync.dma_start(out[P:DV, :], out_windows[1][:])

@@ -41,7 +41,17 @@ def tile_attend_mod_sorted_kernel(tc, xq, kT, vT, vs, offs, qoffs, out):
 
         k_list = keep.tile([P, N // PER_LIST_COLUMN], U16, name="k_list")
         q_list = keep.tile([P, NQ // PER_LIST_COLUMN], U16, name="q_list")
+
+        def load(rows, name):
+            tile = keep.tile([P, T], F32, name=name)
+            nc.sync.dma_start(tile[:], rows)
+            return tile
+
+        k_rows = kT.rearrange("(p t) c -> p t c", t=PACK)
+        q_rows = xq.rearrange("(p t) c -> p t c", t=PACK)
+        k_tiles = [load(k_rows[:, 0, :], "k_tile0")]
         nc.sync.dma_start(k_list[:], offs)
+        k_tiles.append(load(k_rows[:, 1, :], "k_tile1"))
         nc.sync.dma_start(q_list[:], qoffs)
 
         vs_window = keep.tile([P, T], F32, name="vs_window")
@@ -58,16 +68,8 @@ def tile_attend_mod_sorted_kernel(tc, xq, kT, vT, vs, offs, qoffs, out):
         for window in out_windows:
             nc.gpsimd.memset(window[:], 0.0)
 
-        def load(rows, name):
-            tile = keep.tile([P, T], F32, name=name)
-            nc.sync.dma_start(tile[:], rows)
-            return tile
-
-        k_rows = kT.rearrange("(p t) c -> p t c", t=PACK)
-        q_rows = xq.rearrange("(p t) c -> p t c", t=PACK)
-        k_tiles = [load(k_rows[:, 0, :], "k_tile0")]
         nc.sync.dma_start(vs_window[0:1, :], vs[0:1, :])
-        k_tiles.extend([load(k_rows[:, t, :], "k_tile%d" % t) for t in range(1, PACK)])
+        k_tiles.extend([load(k_rows[:, t, :], "k_tile%d" % t) for t in range(2, PACK)])
         q_tiles = [load(q_rows[:, t, :], "q_tile%d" % t) for t in range(PACK)]
         v_tiles = [load(vT[e * P : (e + 1) * P, :], "v_tile%d" % e) for e in range(V_CHUNKS)]
 

@@ -52,7 +52,6 @@ def tile_attend_mod_sorted_kernel(tc, xq, kT, vT, vs, offs, qoffs, out):
         k_tiles = [load(k_rows[:, 0, :], "k_tile0")]
         nc.sync.dma_start(k_list[:], offs)
         k_tiles.append(load(k_rows[:, 1, :], "k_tile1"))
-        nc.sync.dma_start(q_list[:], qoffs)
 
         vs_window = keep.tile([P, T], F32, name="vs_window")
         nc.vector.memset(vs_window[:], 0.0)
@@ -68,8 +67,9 @@ def tile_attend_mod_sorted_kernel(tc, xq, kT, vT, vs, offs, qoffs, out):
         for window in out_windows:
             nc.gpsimd.memset(window[:], 0.0)
 
-        nc.sync.dma_start(vs_window[0:1, :], vs[0:1, :])
         k_tiles.extend([load(k_rows[:, t, :], "k_tile%d" % t) for t in range(2, PACK)])
+        nc.sync.dma_start(vs_window[0:1, :], vs[0:1, :])
+        nc.sync.dma_start(q_list[:], qoffs)
         q_tiles = [load(q_rows[:, t, :], "q_tile%d" % t) for t in range(PACK)]
         v_tiles = [load(vT[e * P : (e + 1) * P, :], "v_tile%d" % e) for e in range(V_CHUNKS)]
 

@@ -164,6 +164,13 @@ def tile_attend_mod_sorted_kernel(tc, xq, kT, vT, vs, offs, qoffs, out):
                 nc.tensor.transpose(bank[:, t, :], weights[:, t, :], ident_bf16[:])
             nc.scalar.copy(w_columns(b), bank[:].rearrange(COPY_OUT))
 
+        def turn_pairs(words, grouped):
+            bank = psum.tile([P, 2, P], F32, name="bank")
+            for u in range(2):
+                nc.tensor.transpose(bank[:, u, :], words[:, u, :], ident[:])
+            grouped_words = grouped.rearrange("p x t -> p (x t)").bitcast(F32).rearrange("p (x u) -> p x u", u=2)
+            nc.scalar.copy(grouped_words, bank[:].rearrange(COPY_OUT))
+
         def turn_probs(prob):
             bank = psum.tile([P, PACK, P], F32, name="bank")
             for t in range(PACK):
@@ -179,16 +186,13 @@ def tile_attend_mod_sorted_kernel(tc, xq, kT, vT, vs, offs, qoffs, out):
             )
 
         def gather_values(e):
-            picked = keep.tile([P, N], F32, name="v_picked%d" % e)
+            picked = keep.tile([P, N], BF16, name="v_picked%d" % e)
             nc.vector.tensor_copy(picked[:], v_tiles[e][:].indirect(k_list[:]))
             return picked
 
         def turn_values(e, picked):
-            bank = psum.tile([P, PACK, P], F32, name="bank")
-            for t in range(PACK):
-                nc.tensor.transpose(bank[:, t, :], picked[:, t::PACK], ident[:])
             grouped = keep.tile([P, P, PACK], BF16, align_bytes=64, name="v_grouped%d" % e)
-            nc.scalar.copy(grouped[:], bank[:].rearrange(COPY_OUT))
+            turn_pairs(picked[:].bitcast(F32).rearrange("p (s u) -> p u s", u=2), grouped[:])
             return grouped
 
         def products(values, halves, name):

@@ -27,7 +27,6 @@ Q_CHUNKS = NQ // P
 V_CHUNKS = DV // P
 HALVES = 2
 HALF_Q = NQ // HALVES
-PSUM_BANKS = 8
 
 FLOPS = 2 * NQ * N * D + 2 * NQ * N * DV
 BYTES = 4 * (2 * D * T + DV * T + T + DV * T) + 2 * P * (N + NQ) // PER_LIST_COLUMN
@@ -37,7 +36,7 @@ def tile_attend_mod_sorted_kernel(tc, xq, kT, vT, vs, offs, qoffs, out):
     nc = tc.nc
     with ExitStack() as ctx:
         keep = ctx.enter_context(tc.tile_pool(name="keep", bufs=1))
-        psum = ctx.enter_context(tc.psum_pool(name="psum", bufs=PSUM_BANKS))
+        psum = ctx.enter_context(tc.psum_pool(name="psum", bufs=1))
 
         k_list = keep.tile([P, N // PER_LIST_COLUMN], U16, name="k_list")
         q_list = keep.tile([P, NQ // PER_LIST_COLUMN], U16, name="q_list")
@@ -61,8 +60,6 @@ def tile_attend_mod_sorted_kernel(tc, xq, kT, vT, vs, offs, qoffs, out):
 
         ident = keep.tile([P, P], F32, name="ident")
         make_identity(nc, ident[:])
-        ident_bf16 = keep.tile([P, P], BF16, name="ident_bf16")
-        nc.scalar.copy(ident_bf16[:], ident[:])
         out_windows = [keep.tile([P, T], F32, name="out_window%d" % e) for e in range(V_CHUNKS)]
         for window in out_windows:
             nc.gpsimd.memset(window[:], 0.0)
@@ -84,23 +81,27 @@ def tile_attend_mod_sorted_kernel(tc, xq, kT, vT, vs, offs, qoffs, out):
             return codes, scales
 
         k_grouped = keep.tile([P, N, PACK], BF16, align_bytes=64, name="k_grouped")
-        nc.vector.tensor_copy(k_grouped[:, :, 0], k_tiles[0][:].indirect(k_list[:]))
+        k_by_slot = k_grouped[:].rearrange("p (u s e) t -> p s u e t", u=2, e=2)
+        nc.vector.tensor_copy(k_by_slot[:, :, :, :, 0], k_tiles[0][:].indirect(k_list[:]))
 
         vs_picked = keep.tile([P, N], F32, name="vs_picked")
         nc.vector.tensor_copy(vs_picked[:], vs_window[:].indirect(k_list[:]))
-        column_bank = psum.tile([P, PACK, P], F32, name="bank")
+        column_bank = psum.tile([P, PACK, P], F32, name="bank4")
         for t in range(PACK):
             nc.tensor.transpose(column_bank[:, t, :], vs_picked[:, t::PACK], ident[:])
         vs_column = keep.tile([P, PACK], F32, name="vs_column")
         nc.scalar.copy(vs_column[:], column_bank[:, :, 0])
-        row_bank = psum.tile([P, PACK, P], F32, name="bank")
+        row_bank = psum.tile([P, PACK, P], F32, name="bank5")
         for t in range(PACK):
             nc.tensor.transpose(row_bank[:, t, :], vs_column[:, t : t + 1].to_broadcast([P, P]), ident[:])
-        vs_row = keep.tile([P, PACK, P], F32, name="vs_row")
-        nc.scalar.copy(vs_row[:], row_bank[:])
+        vs_row = keep.tile([P, N], F32, name="vs_row")
+        nc.scalar.copy(
+            vs_row[:].rearrange("p (u s e) -> p u s e", u=2, e=2),
+            row_bank[:].rearrange("p (u e) s -> p u s e", e=2),
+        )
 
         for t in range(1, PACK):
-            nc.vector.tensor_copy(k_grouped[:, :, t], k_tiles[t][:].indirect(k_list[:]))
+            nc.vector.tensor_copy(k_by_slot[:, :, :, :, t], k_tiles[t][:].indirect(k_list[:]))
         k_codes, k_scales = quantize(k_grouped[:], N, "k")
 
         q_grouped = keep.tile([P, NQ, PACK], BF16, align_bytes=64, name="q_grouped")
@@ -125,7 +126,7 @@ def tile_attend_mod_sorted_kernel(tc, xq, kT, vT, vs, offs, qoffs, out):
 
         def scores(b, codes, scales):
             start = b * P % HALF_Q
-            bank = psum.tile([P, N], F32, name="bank")
+            bank = psum.tile([P, N], F32, name="bank%d" % b)
             nc.tensor.matmul_mx(
                 out=bank[:],
                 lhsT=codes[:, start : start + P].bitcast(FP8X4),
@@ -137,12 +138,12 @@ def tile_attend_mod_sorted_kernel(tc, xq, kT, vT, vs, offs, qoffs, out):
             )
             return bank
 
-        def softmax(b, bank):
+        def softmax(b, bank, paired=True):
             nc.vector.tensor_reduce(neg_max[:, b : b + 1], bank[:], AXIS_X, MAX, negate=True)
-            prob = keep.tile([P, PACK, P], F32, name="prob%d" % b)
+            prob = keep.tile([P, N], F32, name="prob%d" % b)
             nc.scalar.activation(
-                prob[:],
-                bank[:].rearrange("p (s t) -> p t s", t=PACK),
+                prob[:] if paired else prob[:].rearrange("p (u e s) -> p u e s", u=2, e=2),
+                bank[:] if paired else bank[:].rearrange("p (u s e) -> p u e s", u=2, e=2),
                 EXP,
                 bias=neg_max[:, b : b + 1],
                 accum_out=total[:, b : b + 1],
@@ -154,27 +155,24 @@ def tile_attend_mod_sorted_kernel(tc, xq, kT, vT, vs, offs, qoffs, out):
             return w_grouped[h][:, i * P : (i + 1) * P, :]
 
         def multiply_on_gpsimd(b, prob):
-            weights = keep.tile([P, PACK, P], BF16, name="weights%d" % b)
+            weights = keep.tile([P, N], BF16, name="weights%d" % b)
             nc.gpsimd.tensor_tensor(weights[:], prob[:], vs_row[:], MULT)
             return weights
 
-        def turn_weights(b, weights):
-            bank = psum.tile([P, PACK, P], BF16, name="bank")
-            for t in range(PACK):
-                nc.tensor.transpose(bank[:, t, :], weights[:, t, :], ident_bf16[:])
-            nc.scalar.copy(w_columns(b), bank[:].rearrange(COPY_OUT))
+        def turn_weights(b, weights, bank_name):
+            turn_pairs(weights[:].bitcast(F32).rearrange("p (u s) -> p u s", u=2), w_columns(b), bank_name)
 
-        def turn_pairs(words, grouped):
-            bank = psum.tile([P, 2, P], F32, name="bank")
+        def turn_pairs(words, grouped, bank_name):
+            bank = psum.tile([P, 2, P], F32, name=bank_name)
             for u in range(2):
                 nc.tensor.transpose(bank[:, u, :], words[:, u, :], ident[:])
             grouped_words = grouped.rearrange("p x t -> p (x t)").bitcast(F32).rearrange("p (x u) -> p x u", u=2)
             nc.scalar.copy(grouped_words, bank[:].rearrange(COPY_OUT))
 
         def turn_probs(prob):
-            bank = psum.tile([P, PACK, P], F32, name="bank")
+            bank = psum.tile([P, PACK, P], F32, name="bank6")
             for t in range(PACK):
-                nc.tensor.transpose(bank[:, t, :], prob[:, t, :], ident[:])
+                nc.tensor.transpose(bank[:, t, :], prob[:, t * P : (t + 1) * P], ident[:])
             return bank
 
         def multiply_on_vector(b, bank):
@@ -185,19 +183,20 @@ def tile_attend_mod_sorted_kernel(tc, xq, kT, vT, vs, offs, qoffs, out):
                 MULT,
             )
 
-        def gather_values(e):
-            picked = keep.tile([P, N], BF16, name="v_picked%d" % e)
-            nc.vector.tensor_copy(picked[:], v_tiles[e][:].indirect(k_list[:]))
+        def gather_values(e, name):
+            picked = keep.tile([P, N], BF16, align_bytes=64, name=name)
+            by_slot = picked[:].rearrange("p (u s e) -> p s u e", u=2, e=2)
+            nc.vector.tensor_copy(by_slot, v_tiles[e][:].indirect(k_list[:]))
             return picked
 
-        def turn_values(e, picked):
+        def turn_values(e, picked, bank_name):
             grouped = keep.tile([P, P, PACK], BF16, align_bytes=64, name="v_grouped%d" % e)
-            turn_pairs(picked[:].bitcast(F32).rearrange("p (s u) -> p u s", u=2), grouped[:])
+            turn_pairs(picked[:].bitcast(F32).rearrange("p (u s) -> p u s", u=2), grouped[:], bank_name)
             return grouped
 
-        def products(values, halves, name):
+        def products(values, halves, name, bank_name):
             v_codes, v_scales = values
-            bank = psum.tile([P, len(halves), HALF_Q], F32, name="bank")
+            bank = psum.tile([P, len(halves), HALF_Q], F32, name=bank_name)
             for i, (w_codes, w_scales) in enumerate(halves):
                 nc.tensor.matmul_mx(
                     out=bank[:, i, :],
@@ -212,14 +211,14 @@ def tile_attend_mod_sorted_kernel(tc, xq, kT, vT, vs, offs, qoffs, out):
             nc.scalar.copy(sums[:], bank[:].rearrange("p h q -> p (h q)"))
             return sums
 
-        def inverse_totals():
-            nc.vector.reciprocal(inv_total[:], total[:])
-            bank = psum.tile([P, Q_CHUNKS, P], F32, name="bank")
-            for b in range(Q_CHUNKS):
-                nc.tensor.transpose(bank[:, b, :], inv_total[:, b : b + 1].to_broadcast([P, P]), ident[:])
-            inverse = keep.tile([P, NQ], F32, name="inverse")
-            nc.scalar.copy(inverse[:], bank[:].rearrange("p b q -> p (b q)"))
-            return inverse
+        inverse = keep.tile([P, NQ], F32, name="inverse")
+
+        def spread_inverse(h, bank_name):
+            bank = psum.tile([P, Q_CHUNKS // HALVES, P], F32, name=bank_name)
+            for i in range(Q_CHUNKS // HALVES):
+                b = h * Q_CHUNKS // HALVES + i
+                nc.tensor.transpose(bank[:, i, :], inv_total[:, b : b + 1].to_broadcast([P, P]), ident[:])
+            nc.scalar.copy(inverse[:, half_queries[h]], bank[:].rearrange("p b q -> p (b q)"))
 
         def put_back(e, listed, sums, inverse):
             nc.vector.tensor_tensor(out_windows[e][:].indirect(listed), sums[:], inverse, MULT)
@@ -232,30 +231,32 @@ def tile_attend_mod_sorted_kernel(tc, xq, kT, vT, vs, offs, qoffs, out):
         prob0 = softmax(0, score0)
         weights0 = multiply_on_gpsimd(0, prob0)
         q_half1 = quantize_queries(1)
-        prob1 = softmax(1, score1)
-        weights1 = multiply_on_gpsimd(1, prob1)
+        prob1 = softmax(1, score1, paired=False)
+        turned1 = turn_probs(prob1)
         score2 = scores(2, *q_half1)
         score3 = scores(3, *q_half1)
         prob2 = softmax(2, score2)
         weights2 = multiply_on_gpsimd(2, prob2)
         prob3 = softmax(3, score3)
-        turn_weights(0, weights0)
-        picked0 = gather_values(0)
-        grouped0 = turn_values(0, picked0)
-        turned3 = turn_probs(prob3)
-        turn_weights(1, weights1)
-        picked1 = gather_values(1)
-        values0 = quantize(grouped0[:], P, "v0")
+        weights3 = multiply_on_gpsimd(3, prob3)
+        turn_weights(0, weights0, "bank4")
+        picked0 = gather_values(0, "q1_codes")
+        multiply_on_vector(1, turned1)
+        nc.vector.reciprocal(inv_total[:], total[:])
+        grouped0 = turn_values(0, picked0, "bank0")
+        turn_weights(2, weights2, "bank5")
+        picked1 = gather_values(1, "v_picked1")
         w_half0 = quantize(w_grouped[0][:], HALF_Q, "w0")
-        inverse = inverse_totals()
-        turn_weights(2, weights2)
-        multiply_on_vector(3, turned3)
-        grouped1 = turn_values(1, picked1)
-        sums00 = products(values0, [w_half0], "sums00")
-        w_half1 = quantize(w_grouped[1][:], HALF_Q, "w1")
+        values0 = quantize(grouped0[:], P, "v0")
+        spread_inverse(0, "bank0")
+        grouped1 = turn_values(1, picked1, "bank5")
+        turn_weights(3, weights3, "bank7")
+        sums00 = products(values0, [w_half0], "sums00", "bank1")
         values1 = quantize(grouped1[:], P, "v1")
-        sums01 = products(values0, [w_half1], "sums01")
-        sums1 = products(values1, [w_half0, w_half1], "sums1")
+        w_half1 = quantize(w_grouped[1][:], HALF_Q, "w1")
+        spread_inverse(1, "bank7")
+        sums01 = products(values0, [w_half1], "sums01", "bank2")
+        sums1 = products(values1, [w_half0, w_half1], "sums1", "bank3")
 
         put_back(0, half_lists[0], sums00, inverse[:, half_queries[0]])
         put_back(0, half_lists[1], sums01, inverse[:, half_queries[1]])

@@ -70,8 +70,8 @@ def tile_attend_mod_sorted_kernel(tc, xq, kT, vT, vs, offs, qoffs, out):
         q_tiles = [load(q_rows[:, t, :], "q_tile%d" % t) for t in range(PACK)]
         v_tiles = [load(vT[e * P : (e + 1) * P, :], "v_tile%d" % e) for e in range(V_CHUNKS)]
 
-        def quantize(grouped, width, name):
-            codes = keep.tile([P, width], U32, align_bytes=64, name=name + "_codes")
+        def quantize(grouped, width, name, codes_name=None):
+            codes = keep.tile([P, width], U32, align_bytes=64, name=codes_name or name + "_codes")
             scales = keep.tile([P, width], U8, align_bytes=64, name=name + "_scales")
             nc.vector.quantize_mx(
                 out=codes[:].bitcast(FP8X4),
@@ -140,7 +140,7 @@ def tile_attend_mod_sorted_kernel(tc, xq, kT, vT, vs, offs, qoffs, out):
 
         def softmax(b, bank, paired=True):
             nc.vector.tensor_reduce(neg_max[:, b : b + 1], bank[:], AXIS_X, MAX, negate=True)
-            prob = keep.tile([P, N], F32, name="prob%d" % b)
+            prob = keep.tile([P, N], F32, align_bytes=64, name="prob%d" % b)
             nc.scalar.activation(
                 prob[:] if paired else prob[:].rearrange("p (u e s) -> p u e s", u=2, e=2),
                 bank[:] if paired else bank[:].rearrange("p (u s e) -> p u e s", u=2, e=2),
@@ -246,7 +246,7 @@ def tile_attend_mod_sorted_kernel(tc, xq, kT, vT, vs, offs, qoffs, out):
         grouped0 = turn_values(0, picked0, "bank0")
         turn_weights(2, weights2, "bank5")
         picked1 = gather_values(1, "v_picked1")
-        w_half0 = quantize(w_grouped[0][:], HALF_Q, "w0")
+        w_half0 = quantize(w_grouped[0][:], HALF_Q, "w0", "prob3")
         values0 = quantize(grouped0[:], P, "v0")
         spread_inverse(0, "bank0")
         grouped1 = turn_values(1, picked1, "bank5")
@@ -254,8 +254,8 @@ def tile_attend_mod_sorted_kernel(tc, xq, kT, vT, vs, offs, qoffs, out):
         sums00 = products(values0, [w_half0], "sums00", "bank1")
         values1 = quantize(grouped1[:], P, "v1")
         w_half1 = quantize(w_grouped[1][:], HALF_Q, "w1")
-        spread_inverse(1, "bank7")
         sums01 = products(values0, [w_half1], "sums01", "bank2")
+        spread_inverse(1, "bank1")
         sums1 = products(values1, [w_half0, w_half1], "sums1", "bank3")
 
         put_back(0, half_lists[0], sums00, inverse[:, half_queries[0]])

@@ -169,8 +169,8 @@ def tile_attend_mod_sorted_kernel(tc, xq, kT, vT, vs, offs, qoffs, out):
             grouped_words = grouped.rearrange("p x t -> p (x t)").bitcast(F32).rearrange("p (x u) -> p x u", u=2)
             nc.scalar.copy(grouped_words, bank[:].rearrange(COPY_OUT))
 
-        def turn_probs(prob):
-            bank = psum.tile([P, PACK, P], F32, name="bank6")
+        def turn_probs(prob, bank_name):
+            bank = psum.tile([P, PACK, P], F32, name=bank_name)
             for t in range(PACK):
                 nc.tensor.transpose(bank[:, t, :], prob[:, t * P : (t + 1) * P], ident[:])
             return bank
@@ -207,11 +207,15 @@ def tile_attend_mod_sorted_kernel(tc, xq, kT, vT, vs, offs, qoffs, out):
                     start=True,
                     stop=True,
                 )
-            sums = keep.tile([P, len(halves) * HALF_Q], F32, name=name)
+            sums = keep.tile([P, len(halves) * HALF_Q], F32, align_bytes=64, name=name)
             nc.scalar.copy(sums[:], bank[:].rearrange("p h q -> p (h q)"))
             return sums
 
         inverse = keep.tile([P, NQ], F32, name="inverse")
+
+        def invert_totals(h):
+            chunks = slice(h * Q_CHUNKS // HALVES, (h + 1) * Q_CHUNKS // HALVES)
+            nc.vector.reciprocal(inv_total[:, chunks], total[:, chunks])
 
         def spread_inverse(h, bank_name):
             bank = psum.tile([P, Q_CHUNKS // HALVES, P], F32, name=bank_name)
@@ -232,33 +236,33 @@ def tile_attend_mod_sorted_kernel(tc, xq, kT, vT, vs, offs, qoffs, out):
         weights0 = multiply_on_gpsimd(0, prob0)
         q_half1 = quantize_queries(1)
         prob1 = softmax(1, score1, paired=False)
-        turned1 = turn_probs(prob1)
         score2 = scores(2, *q_half1)
         score3 = scores(3, *q_half1)
+        turned1 = turn_probs(prob1, "bank6")
         prob2 = softmax(2, score2)
         weights2 = multiply_on_gpsimd(2, prob2)
-        prob3 = softmax(3, score3)
-        weights3 = multiply_on_gpsimd(3, prob3)
+        prob3 = softmax(3, score3, paired=False)
+        invert_totals(0)
         turn_weights(0, weights0, "bank4")
+        spread_inverse(0, "bank5")
         picked0 = gather_values(0, "q1_codes")
         multiply_on_vector(1, turned1)
-        nc.vector.reciprocal(inv_total[:], total[:])
         grouped0 = turn_values(0, picked0, "bank0")
-        turn_weights(2, weights2, "bank5")
-        picked1 = gather_values(1, "v_picked1")
-        w_half0 = quantize(w_grouped[0][:], HALF_Q, "w0", "prob3")
+        turned3 = turn_probs(prob3, "bank7")
+        turn_weights(2, weights2, "bank4")
+        w_half0 = quantize(w_grouped[0][:], HALF_Q, "w0", "prob2")
         values0 = quantize(grouped0[:], P, "v0")
-        spread_inverse(0, "bank0")
-        grouped1 = turn_values(1, picked1, "bank5")
-        turn_weights(3, weights3, "bank7")
         sums00 = products(values0, [w_half0], "sums00", "bank1")
-        values1 = quantize(grouped1[:], P, "v1")
+        invert_totals(1)
+        multiply_on_vector(3, turned3)
+        picked1 = gather_values(1, "v_picked1")
         w_half1 = quantize(w_grouped[1][:], HALF_Q, "w1")
-        sums01 = products(values0, [w_half1], "sums01", "bank2")
-        spread_inverse(1, "bank1")
-        sums1 = products(values1, [w_half0, w_half1], "sums1", "bank3")
-
+        spread_inverse(1, "bank5")
+        grouped1 = turn_values(1, picked1, "bank1")
+        sums01 = products(values0, [w_half1], "v_picked1", "bank2")
         put_back(0, half_lists[0], sums00, inverse[:, half_queries[0]])
+        values1 = quantize(grouped1[:], P, "v1")
+        sums1 = products(values1, [w_half0, w_half1], "sums1", "bank3")
         put_back(0, half_lists[1], sums01, inverse[:, half_queries[1]])
         nc.sync.dma_start(out[0:P, :], out_windows[0][:])
         put_back(1, q_list[:], sums1, inverse[:])

@@ -10,6 +10,7 @@ U16 = mybir.dt.uint16
 U8 = mybir.dt.uint8
 FP8X4 = mybir.dt.float8_e4m3fn_x4
 COPY_OUT = "p t x -> p x t"
+COPY = mybir.ActivationFunctionType.Copy
 EXP = mybir.ActivationFunctionType.Exp
 MULT = mybir.AluOpType.mult
 MAX = mybir.AluOpType.max
@@ -27,6 +28,7 @@ Q_CHUNKS = NQ // P
 V_CHUNKS = DV // P
 HALVES = 2
 HALF_Q = NQ // HALVES
+V_PIECES = 4
 
 FLOPS = 2 * NQ * N * D + 2 * NQ * N * DV
 BYTES = 4 * (2 * D * T + DV * T + T + DV * T) + 2 * P * (N + NQ) // PER_LIST_COLUMN
@@ -68,7 +70,12 @@ def tile_attend_mod_sorted_kernel(tc, xq, kT, vT, vs, offs, qoffs, out):
         nc.sync.dma_start(vs_window[0:1, :], vs[0:1, :])
         nc.sync.dma_start(q_list[:], qoffs)
         q_tiles = [load(q_rows[:, t, :], "q_tile%d" % t) for t in range(PACK)]
-        v_tiles = [load(vT[e * P : (e + 1) * P, :], "v_tile%d" % e) for e in range(V_CHUNKS)]
+        v1_pieces = []
+        for c in range(V_PIECES):
+            piece = keep.tile([P, T // V_PIECES], F32, align_bytes=64, name="v1_piece%d" % c)
+            nc.sync.dma_start(piece[:], vT[P:DV, c * T // V_PIECES : (c + 1) * T // V_PIECES])
+            v1_pieces.append(piece)
+        v0_tile = load(vT[0:P, :], "v0_tile")
 
         def quantize(grouped, width, name, codes_name=None):
             codes = keep.tile([P, width], U32, align_bytes=64, name=codes_name or name + "_codes")
@@ -113,7 +120,6 @@ def tile_attend_mod_sorted_kernel(tc, xq, kT, vT, vs, offs, qoffs, out):
             q_list[:, h * HALF_Q // PER_LIST_COLUMN : (h + 1) * HALF_Q // PER_LIST_COLUMN] for h in range(HALVES)
         ]
         neg_max = keep.tile([P, Q_CHUNKS], F32, name="neg_max")
-        total = keep.tile([P, Q_CHUNKS], F32, name="total")
         inv_total = keep.tile([P, Q_CHUNKS], F32, name="inv_total")
         w_grouped = [keep.tile([P, HALF_Q, PACK], BF16, align_bytes=64, name="w_grouped%d" % h) for h in range(HALVES)]
 
@@ -138,9 +144,9 @@ def tile_attend_mod_sorted_kernel(tc, xq, kT, vT, vs, offs, qoffs, out):
             )
             return bank
 
-        def softmax(b, bank, paired=True):
+        def softmax(b, bank, paired=True, name=None):
             nc.vector.tensor_reduce(neg_max[:, b : b + 1], bank[:], AXIS_X, MAX, negate=True)
-            prob = keep.tile([P, N], F32, align_bytes=64, name="prob%d" % b)
+            prob = keep.tile([P, N], F32, align_bytes=64, name=name or "prob%d" % b)
             nc.scalar.activation(
                 prob[:] if paired else prob[:].rearrange("p (u e s) -> p u e s", u=2, e=2),
                 bank[:] if paired else bank[:].rearrange("p (u s e) -> p u e s", u=2, e=2),
@@ -155,7 +161,7 @@ def tile_attend_mod_sorted_kernel(tc, xq, kT, vT, vs, offs, qoffs, out):
             return w_grouped[h][:, i * P : (i + 1) * P, :]
 
         def multiply_on_gpsimd(b, prob):
-            weights = keep.tile([P, N], BF16, name="weights%d" % b)
+            weights = keep.tile([P, N], BF16, align_bytes=64, name="weights%d" % b)
             nc.gpsimd.tensor_tensor(weights[:], prob[:], vs_row[:], MULT)
             return weights
 
@@ -183,11 +189,26 @@ def tile_attend_mod_sorted_kernel(tc, xq, kT, vT, vs, offs, qoffs, out):
                 MULT,
             )
 
-        def gather_values(e, name):
+        def gather_values_on_vector(name):
             picked = keep.tile([P, N], BF16, align_bytes=64, name=name)
             by_slot = picked[:].rearrange("p (u s e) -> p s u e", u=2, e=2)
-            nc.vector.tensor_copy(by_slot, v_tiles[e][:].indirect(k_list[:]))
+            nc.vector.tensor_copy(by_slot, v0_tile[:].indirect(k_list[:]))
             return picked
+
+        def cast_values():
+            window = keep.tile([P, T], BF16, name="v1_window")
+            for c, piece in enumerate(v1_pieces):
+                nc.scalar.activation(window[:, c * T // V_PIECES : (c + 1) * T // V_PIECES], piece[:], COPY)
+            return window
+
+        def gather_values_on_scalar(window, picked, h):
+            by_slot = picked[:].rearrange("p (u s e) -> p s u e", u=2, e=2)
+            columns = N // PER_LIST_COLUMN // HALVES
+            nc.scalar.activation(
+                by_slot[:, h * P // HALVES : (h + 1) * P // HALVES],
+                window[:].indirect(k_list[:, h * columns : (h + 1) * columns]),
+                COPY,
+            )
 
         def turn_values(e, picked, bank_name):
             grouped = keep.tile([P, P, PACK], BF16, align_bytes=64, name="v_grouped%d" % e)
@@ -227,6 +248,8 @@ def tile_attend_mod_sorted_kernel(tc, xq, kT, vT, vs, offs, qoffs, out):
         def put_back(e, listed, sums, inverse):
             nc.vector.tensor_tensor(out_windows[e][:].indirect(listed), sums[:], inverse, MULT)
 
+        v1_window = cast_values()
+        total = keep.tile([P, Q_CHUNKS], F32, align_bytes=64, name="v1_piece3")
         gather_last_queries(0)
         q_half0 = quantize_queries(0)
         gather_last_queries(1)
@@ -245,21 +268,23 @@ def tile_attend_mod_sorted_kernel(tc, xq, kT, vT, vs, offs, qoffs, out):
         invert_totals(0)
         turn_weights(0, weights0, "bank4")
         spread_inverse(0, "bank5")
-        picked0 = gather_values(0, "q1_codes")
+        picked0 = gather_values_on_vector("q1_codes")
         multiply_on_vector(1, turned1)
         grouped0 = turn_values(0, picked0, "bank0")
         turned3 = turn_probs(prob3, "bank7")
         turn_weights(2, weights2, "bank4")
+        picked1 = keep.tile([P, N], BF16, align_bytes=64, name="weights2")
+        gather_values_on_scalar(v1_window, picked1, 0)
         w_half0 = quantize(w_grouped[0][:], HALF_Q, "w0", "prob2")
         values0 = quantize(grouped0[:], P, "v0")
         sums00 = products(values0, [w_half0], "sums00", "bank1")
+        gather_values_on_scalar(v1_window, picked1, 1)
         invert_totals(1)
         multiply_on_vector(3, turned3)
-        picked1 = gather_values(1, "v_picked1")
         w_half1 = quantize(w_grouped[1][:], HALF_Q, "w1")
         spread_inverse(1, "bank5")
         grouped1 = turn_values(1, picked1, "bank1")
-        sums01 = products(values0, [w_half1], "v_picked1", "bank2")
+        sums01 = products(values0, [w_half1], "weights2", "bank2")
         put_back(0, half_lists[0], sums00, inverse[:, half_queries[0]])
         values1 = quantize(grouped1[:], P, "v1")
         sums1 = products(values1, [w_half0, w_half1], "sums1", "bank3")

@@ -250,6 +250,8 @@ def tile_attend_mod_sorted_kernel(tc, xq, kT, vT, vs, offs, qoffs, out):
 
         v1_window = cast_values()
         total = keep.tile([P, Q_CHUNKS], F32, align_bytes=64, name="v1_piece3")
+        picked1 = keep.tile([P, N], BF16, align_bytes=64, name="v_picked1")
+        gather_values_on_scalar(v1_window, picked1, 0)
         gather_last_queries(0)
         q_half0 = quantize_queries(0)
         gather_last_queries(1)
@@ -273,8 +275,6 @@ def tile_attend_mod_sorted_kernel(tc, xq, kT, vT, vs, offs, qoffs, out):
         grouped0 = turn_values(0, picked0, "bank0")
         turned3 = turn_probs(prob3, "bank7")
         turn_weights(2, weights2, "bank4")
-        picked1 = keep.tile([P, N], BF16, align_bytes=64, name="weights2")
-        gather_values_on_scalar(v1_window, picked1, 0)
         w_half0 = quantize(w_grouped[0][:], HALF_Q, "w0", "prob2")
         values0 = quantize(grouped0[:], P, "v0")
         sums00 = products(values0, [w_half0], "sums00", "bank1")
@@ -284,7 +284,7 @@ def tile_attend_mod_sorted_kernel(tc, xq, kT, vT, vs, offs, qoffs, out):
         w_half1 = quantize(w_grouped[1][:], HALF_Q, "w1")
         spread_inverse(1, "bank5")
         grouped1 = turn_values(1, picked1, "bank1")
-        sums01 = products(values0, [w_half1], "weights2", "bank2")
+        sums01 = products(values0, [w_half1], "v_picked1", "bank2")
         put_back(0, half_lists[0], sums00, inverse[:, half_queries[0]])
         values1 = quantize(grouped1[:], P, "v1")
         sums1 = products(values1, [w_half0, w_half1], "sums1", "bank3")

@@ -66,8 +66,8 @@ def tile_attend_mod_sorted_kernel(tc, xq, kT, vT, vs, offs, qoffs, out):
         for window in out_windows:
             nc.gpsimd.memset(window[:], 0.0)
 
-        k_tiles.extend([load(k_rows[:, t, :], "k_tile%d" % t) for t in range(2, PACK)])
         nc.sync.dma_start(vs_window[0:1, :], vs[0:1, :])
+        k_tiles.extend([load(k_rows[:, t, :], "k_tile%d" % t) for t in range(2, PACK)])
         nc.sync.dma_start(q_list[:], qoffs)
         q_tiles = [load(q_rows[:, t, :], "q_tile%d" % t) for t in range(PACK)]
         v1_pieces = []

@@ -232,18 +232,13 @@ def tile_attend_mod_sorted_kernel(tc, xq, kT, vT, vs, offs, qoffs, out):
             nc.scalar.copy(sums[:], bank[:].rearrange("p h q -> p (h q)"))
             return sums
 
-        inverse = keep.tile([P, NQ], F32, name="inverse")
 
-        def invert_totals(h):
-            chunks = slice(h * Q_CHUNKS // HALVES, (h + 1) * Q_CHUNKS // HALVES)
-            nc.vector.reciprocal(inv_total[:, chunks], total[:, chunks])
-
-        def spread_inverse(h, bank_name):
+        def turn_inverse(h, bank_name):
             bank = psum.tile([P, Q_CHUNKS // HALVES, P], F32, name=bank_name)
             for i in range(Q_CHUNKS // HALVES):
                 b = h * Q_CHUNKS // HALVES + i
                 nc.tensor.transpose(bank[:, i, :], inv_total[:, b : b + 1].to_broadcast([P, P]), ident[:])
-            nc.scalar.copy(inverse[:, half_queries[h]], bank[:].rearrange("p b q -> p (b q)"))
+            return bank[:].rearrange("p b q -> p (b q)")
 
         def put_back(e, listed, sums, inverse):
             nc.vector.tensor_tensor(out_windows[e][:].indirect(listed), sums[:], inverse, MULT)
@@ -267,22 +262,22 @@ def tile_attend_mod_sorted_kernel(tc, xq, kT, vT, vs, offs, qoffs, out):
         prob2 = softmax(2, score2)
         weights2 = multiply_on_gpsimd(2, prob2)
         prob3 = softmax(3, score3, paired=False)
-        invert_totals(0)
         turn_weights(0, weights0, "bank4")
-        spread_inverse(0, "bank5")
         picked0 = gather_values_on_vector("q1_codes")
         multiply_on_vector(1, turned1)
+        nc.vector.reciprocal(inv_total[:], total[:])
         grouped0 = turn_values(0, picked0, "bank0")
         turned3 = turn_probs(prob3, "bank7")
         turn_weights(2, weights2, "bank4")
+        inverse = keep.tile([P, NQ], F32, name="inverse")
+        nc.scalar.copy(inverse[:, half_queries[0]], turn_inverse(0, "bank5"))
         w_half0 = quantize(w_grouped[0][:], HALF_Q, "w0", "prob2")
         values0 = quantize(grouped0[:], P, "v0")
         sums00 = products(values0, [w_half0], "sums00", "bank1")
         gather_values_on_scalar(v1_window, picked1, 1)
-        invert_totals(1)
         multiply_on_vector(3, turned3)
         w_half1 = quantize(w_grouped[1][:], HALF_Q, "w1")
-        spread_inverse(1, "bank5")
+        nc.scalar.copy(inverse[:, half_queries[1]], turn_inverse(1, "bank5"))
         grouped1 = turn_values(1, picked1, "bank1")
         sums01 = products(values0, [w_half1], "v_picked1", "bank2")
         put_back(0, half_lists[0], sums00, inverse[:, half_queries[0]])

@@ -28,7 +28,8 @@ Q_CHUNKS = NQ // P
 V_CHUNKS = DV // P
 HALVES = 2
 HALF_Q = NQ // HALVES
-V_PIECES = 4
+FIRST_TOKENS = T - N // 2
+V_CUTS = (0, T // 4, T // 2, 3 * T // 4, FIRST_TOKENS, T)
 
 FLOPS = 2 * NQ * N * D + 2 * NQ * N * DV
 BYTES = 4 * (2 * D * T + DV * T + T + DV * T) + 2 * P * (N + NQ) // PER_LIST_COLUMN
@@ -71,11 +72,16 @@ def tile_attend_mod_sorted_kernel(tc, xq, kT, vT, vs, offs, qoffs, out):
         nc.sync.dma_start(q_list[:], qoffs)
         q_tiles = [load(q_rows[:, t, :], "q_tile%d" % t) for t in range(PACK)]
         v1_pieces = []
-        for c in range(V_PIECES):
-            piece = keep.tile([P, T // V_PIECES], F32, align_bytes=64, name="v1_piece%d" % c)
-            nc.sync.dma_start(piece[:], vT[P:DV, c * T // V_PIECES : (c + 1) * T // V_PIECES])
+
+        def load_piece(c):
+            piece = keep.tile([P, V_CUTS[c + 1] - V_CUTS[c]], F32, align_bytes=64, name="v1_piece%d" % c)
+            nc.sync.dma_start(piece[:], vT[P:DV, V_CUTS[c] : V_CUTS[c + 1]])
             v1_pieces.append(piece)
+
+        for c in range(len(V_CUTS) - 2):
+            load_piece(c)
         v0_tile = load(vT[0:P, :], "v0_tile")
+        load_piece(len(V_CUTS) - 2)
 
         def quantize(grouped, width, name, codes_name=None):
             codes = keep.tile([P, width], U32, align_bytes=64, name=codes_name or name + "_codes")
@@ -195,18 +201,17 @@ def tile_attend_mod_sorted_kernel(tc, xq, kT, vT, vs, offs, qoffs, out):
             nc.vector.tensor_copy(by_slot, v0_tile[:].indirect(k_list[:]))
             return picked
 
-        def cast_values():
-            window = keep.tile([P, T], BF16, name="v1_window")
-            for c, piece in enumerate(v1_pieces):
-                nc.scalar.activation(window[:, c * T // V_PIECES : (c + 1) * T // V_PIECES], piece[:], COPY)
-            return window
+        v1_window = keep.tile([P, T], BF16, name="v1_window")
+
+        def cast_values(c):
+            nc.scalar.activation(v1_window[:, V_CUTS[c] : V_CUTS[c + 1]], v1_pieces[c][:], COPY)
 
         def gather_values_on_scalar(window, picked, h):
             by_slot = picked[:].rearrange("p (u s e) -> p s u e", u=2, e=2)
             columns = N // PER_LIST_COLUMN // HALVES
             nc.scalar.activation(
                 by_slot[:, h * P // HALVES : (h + 1) * P // HALVES],
-                window[:].indirect(k_list[:, h * columns : (h + 1) * columns]),
+                window.indirect(k_list[:, h * columns : (h + 1) * columns]),
                 COPY,
             )
 
@@ -243,10 +248,11 @@ def tile_attend_mod_sorted_kernel(tc, xq, kT, vT, vs, offs, qoffs, out):
         def put_back(e, listed, sums, inverse):
             nc.vector.tensor_tensor(out_windows[e][:].indirect(listed), sums[:], inverse, MULT)
 
-        v1_window = cast_values()
+        for c in range(len(V_CUTS) - 2):
+            cast_values(c)
         total = keep.tile([P, Q_CHUNKS], F32, align_bytes=64, name="v1_piece3")
         picked1 = keep.tile([P, N], BF16, align_bytes=64, name="v_picked1")
-        gather_values_on_scalar(v1_window, picked1, 0)
+        gather_values_on_scalar(v1_window[:, 0:FIRST_TOKENS], picked1, 0)
         gather_last_queries(0)
         q_half0 = quantize_queries(0)
         gather_last_queries(1)
@@ -267,6 +273,7 @@ def tile_attend_mod_sorted_kernel(tc, xq, kT, vT, vs, offs, qoffs, out):
         multiply_on_vector(1, turned1)
         nc.vector.reciprocal(inv_total[:], total[:])
         grouped0 = turn_values(0, picked0, "bank0")
+        cast_values(len(V_CUTS) - 2)
         turned3 = turn_probs(prob3, "bank7")
         turn_weights(2, weights2, "bank4")
         inverse = keep.tile([P, NQ], F32, name="inverse")
@@ -274,7 +281,7 @@ def tile_attend_mod_sorted_kernel(tc, xq, kT, vT, vs, offs, qoffs, out):
         w_half0 = quantize(w_grouped[0][:], HALF_Q, "w0", "prob2")
         values0 = quantize(grouped0[:], P, "v0")
         sums00 = products(values0, [w_half0], "sums00", "bank1")
-        gather_values_on_scalar(v1_window, picked1, 1)
+        gather_values_on_scalar(v1_window[:], picked1, 1)
         multiply_on_vector(3, turned3)
         w_half1 = quantize(w_grouped[1][:], HALF_Q, "w1")
         nc.scalar.copy(inverse[:, half_queries[1]], turn_inverse(1, "bank5"))

@@ -133,11 +133,10 @@ def tile_attend_mod_sorted_kernel(tc, xq, kT, vT, vs, offs, qoffs, out):
             last = PACK - 1
             nc.vector.tensor_copy(q_grouped[:, half_queries[h], last], q_tiles[last][:].indirect(half_lists[h]))
 
-        def quantize_queries(h):
-            return quantize(q_grouped[:, half_queries[h], :], HALF_Q, "q%d" % h)
+        def quantize_queries(first, count, name):
+            return quantize(q_grouped[:, first : first + count, :], count, name)
 
-        def scores(b, codes, scales):
-            start = b * P % HALF_Q
+        def scores(b, start, codes, scales):
             bank = psum.tile([P, N], F32, name="bank%d" % b)
             nc.tensor.matmul_mx(
                 out=bank[:],
@@ -254,16 +253,15 @@ def tile_attend_mod_sorted_kernel(tc, xq, kT, vT, vs, offs, qoffs, out):
         picked1 = keep.tile([P, N], BF16, align_bytes=64, name="v_picked1")
         gather_values_on_scalar(v1_window[:, 0:FIRST_TOKENS], picked1, 0)
         gather_last_queries(0)
-        q_half0 = quantize_queries(0)
+        score0 = scores(0, 0, *quantize_queries(0, P, "q0a"))
         gather_last_queries(1)
-        score0 = scores(0, *q_half0)
-        score1 = scores(1, *q_half0)
+        score1 = scores(1, 0, *quantize_queries(P, P, "q0b"))
         prob0 = softmax(0, score0)
         weights0 = multiply_on_gpsimd(0, prob0)
-        q_half1 = quantize_queries(1)
+        q_half1 = quantize_queries(HALF_Q, HALF_Q, "q1")
         prob1 = softmax(1, score1, paired=False)
-        score2 = scores(2, *q_half1)
-        score3 = scores(3, *q_half1)
+        score2 = scores(2, 0, *q_half1)
+        score3 = scores(3, P, *q_half1)
         turned1 = turn_probs(prob1, "bank6")
         prob2 = softmax(2, score2)
         weights2 = multiply_on_gpsimd(2, prob2)

@@ -57,9 +57,6 @@ def tile_attend_mod_sorted_kernel(tc, xq, kT, vT, vs, offs, qoffs, out):
 
         vs_window = keep.tile([P, T], F32, name="vs_window")
         nc.vector.memset(vs_window[:], 0.0)
-        table_column = keep.tile([P, 1], F32, name="table_column")
-        nc.vector.memset(table_column[:], 0.0)
-        nc.scalar.activation(table_column[:], table_column[:], EXP)
 
         ident = keep.tile([P, P], F32, name="ident")
         make_identity(nc, ident[:])

@@ -9,7 +9,6 @@ U32 = mybir.dt.uint32
 U16 = mybir.dt.uint16
 U8 = mybir.dt.uint8
 FP8X4 = mybir.dt.float8_e4m3fn_x4
-COPY_OUT = "p t x -> p x t"
 COPY = mybir.ActivationFunctionType.Copy
 EXP = mybir.ActivationFunctionType.Exp
 MULT = mybir.AluOpType.mult
@@ -18,6 +17,7 @@ AXIS_X = mybir.AxisListType.X
 
 P = 128
 PACK = 4
+PAIR = 2
 T = 2048
 D = 512
 DV = 256
@@ -28,8 +28,12 @@ Q_CHUNKS = NQ // P
 V_CHUNKS = DV // P
 HALVES = 2
 HALF_Q = NQ // HALVES
-FIRST_TOKENS = T - N // 2
+HALF_N = N // HALVES
+FIRST_TOKENS = T - HALF_N
 V_CUTS = (0, T // 4, T // 2, 3 * T // 4, FIRST_TOKENS, T)
+LAST_PIECE = len(V_CUTS) - 2
+ALIGN = 64
+SIDE_BY_SIDE = "p t x -> p x t"
 
 FLOPS = 2 * NQ * N * D + 2 * NQ * N * DV
 BYTES = 4 * (2 * D * T + DV * T + T + DV * T) + 2 * P * (N + NQ) // PER_LIST_COLUMN
@@ -41,48 +45,53 @@ def tile_attend_mod_sorted_kernel(tc, xq, kT, vT, vs, offs, qoffs, out):
         keep = ctx.enter_context(tc.tile_pool(name="keep", bufs=1))
         psum = ctx.enter_context(tc.psum_pool(name="psum", bufs=1))
 
-        k_list = keep.tile([P, N // PER_LIST_COLUMN], U16, name="k_list")
-        q_list = keep.tile([P, NQ // PER_LIST_COLUMN], U16, name="q_list")
+        def sbuf(shape, dtype, name):
+            return keep.tile(shape, dtype, align_bytes=ALIGN, name=name)
 
         def load(rows, name):
-            tile = keep.tile([P, T], F32, name=name)
+            tile = sbuf(list(rows.shape), F32, name)
             nc.sync.dma_start(tile[:], rows)
             return tile
 
+        k_list = sbuf([P, N // PER_LIST_COLUMN], U16, "k_list")
+        q_list = sbuf([P, NQ // PER_LIST_COLUMN], U16, "q_list")
         k_rows = kT.rearrange("(p t) c -> p t c", t=PACK)
         q_rows = xq.rearrange("(p t) c -> p t c", t=PACK)
-        k_tiles = [load(k_rows[:, 0, :], "k_tile0")]
+        k_planes = [load(k_rows[:, 0, :], "k_plane0")]
         nc.sync.dma_start(k_list[:], offs)
-        k_tiles.append(load(k_rows[:, 1, :], "k_tile1"))
+        k_planes.append(load(k_rows[:, 1, :], "k_plane1"))
 
-        vs_window = keep.tile([P, T], F32, name="vs_window")
+        vs_window = sbuf([P, T], F32, "vs_window")
         nc.vector.memset(vs_window[:], 0.0)
-
-        ident = keep.tile([P, P], F32, name="ident")
+        ident = sbuf([P, P], F32, "ident")
         make_identity(nc, ident[:])
-        out_windows = [keep.tile([P, T], F32, name="out_window%d" % e) for e in range(V_CHUNKS)]
+        out_windows = [sbuf([P, T], F32, "out_window%d" % e) for e in range(V_CHUNKS)]
         for window in out_windows:
             nc.gpsimd.memset(window[:], 0.0)
 
         nc.sync.dma_start(vs_window[0:1, :], vs[0:1, :])
-        k_tiles.extend([load(k_rows[:, t, :], "k_tile%d" % t) for t in range(2, PACK)])
+        k_planes.extend([load(k_rows[:, t, :], "k_plane%d" % t) for t in range(2, PACK)])
         nc.sync.dma_start(q_list[:], qoffs)
-        q_tiles = [load(q_rows[:, t, :], "q_tile%d" % t) for t in range(PACK)]
-        v1_pieces = []
+        q_planes = [load(q_rows[:, t, :], "q_plane%d" % t) for t in range(PACK)]
 
         def load_piece(c):
-            piece = keep.tile([P, V_CUTS[c + 1] - V_CUTS[c]], F32, align_bytes=64, name="v1_piece%d" % c)
-            nc.sync.dma_start(piece[:], vT[P:DV, V_CUTS[c] : V_CUTS[c + 1]])
-            v1_pieces.append(piece)
+            return load(vT[P:DV, V_CUTS[c] : V_CUTS[c + 1]], "v1_piece%d" % c)
 
-        for c in range(len(V_CUTS) - 2):
-            load_piece(c)
-        v0_tile = load(vT[0:P, :], "v0_tile")
-        load_piece(len(V_CUTS) - 2)
+        v1_pieces = [load_piece(c) for c in range(LAST_PIECE)]
+        v0_window = load(vT[0:P, :], "v0_window")
+        v1_pieces.append(load_piece(LAST_PIECE))
 
-        def quantize(grouped, width, name, codes_name=None):
-            codes = keep.tile([P, width], U32, align_bytes=64, name=codes_name or name + "_codes")
-            scales = keep.tile([P, width], U8, align_bytes=64, name=name + "_scales")
+        def half_of(listed, h):
+            columns = HALF_N // PER_LIST_COLUMN
+            return listed[:, h * columns : (h + 1) * columns]
+
+        def by_slot(paired):
+            return paired.rearrange("p (u s e) -> p s u e", u=PAIR, e=PAIR)
+
+        def quantize(grouped, name, codes_name=None):
+            width = grouped.shape[1]
+            codes = sbuf([P, width], U32, codes_name or name + "_codes")
+            scales = sbuf([P, width], U8, name + "_scales")
             nc.vector.quantize_mx(
                 out=codes[:].bitcast(FP8X4),
                 scales=scales[:],
@@ -90,68 +99,65 @@ def tile_attend_mod_sorted_kernel(tc, xq, kT, vT, vs, offs, qoffs, out):
             )
             return codes, scales
 
-        k_grouped = keep.tile([P, N, PACK], BF16, align_bytes=64, name="k_grouped")
-        k_by_slot = k_grouped[:].rearrange("p (u s e) t -> p s u e t", u=2, e=2)
-        nc.vector.tensor_copy(k_by_slot[:, :, :, :, 0], k_tiles[0][:].indirect(k_list[:]))
+        def product(result, stationary, moving):
+            nc.tensor.matmul_mx(
+                out=result,
+                lhsT=stationary[0].bitcast(FP8X4),
+                lhsT_scale=stationary[1],
+                rhs=moving[0][:].bitcast(FP8X4),
+                rhs_scale=moving[1][:],
+                start=True,
+                stop=True,
+            )
 
-        vs_picked = keep.tile([P, N], F32, name="vs_picked")
+        k_grouped = sbuf([P, N, PACK], BF16, "k_grouped")
+        nc.vector.tensor_copy(by_slot(k_grouped[:, :, 0]), k_planes[0][:].indirect(k_list[:]))
+
+        vs_picked = sbuf([P, N], F32, "vs_picked")
         nc.vector.tensor_copy(vs_picked[:], vs_window[:].indirect(k_list[:]))
         column_bank = psum.tile([P, PACK, P], F32, name="bank4")
         for t in range(PACK):
             nc.tensor.transpose(column_bank[:, t, :], vs_picked[:, t::PACK], ident[:])
-        vs_column = keep.tile([P, PACK], F32, name="vs_column")
+        vs_column = sbuf([P, PACK], F32, "vs_column")
         nc.scalar.copy(vs_column[:], column_bank[:, :, 0])
         row_bank = psum.tile([P, PACK, P], F32, name="bank5")
         for t in range(PACK):
             nc.tensor.transpose(row_bank[:, t, :], vs_column[:, t : t + 1].to_broadcast([P, P]), ident[:])
-        vs_row = keep.tile([P, N], F32, name="vs_row")
+        vs_row = sbuf([P, N], F32, "vs_row")
         nc.scalar.copy(
-            vs_row[:].rearrange("p (u s e) -> p u s e", u=2, e=2),
-            row_bank[:].rearrange("p (u e) s -> p u s e", e=2),
+            vs_row[:].rearrange("p (u s e) -> p u s e", u=PAIR, e=PAIR),
+            row_bank[:].rearrange("p (u e) s -> p u s e", e=PAIR),
         )
 
         for t in range(1, PACK):
-            nc.vector.tensor_copy(k_by_slot[:, :, :, :, t], k_tiles[t][:].indirect(k_list[:]))
-        k_codes, k_scales = quantize(k_grouped[:], N, "k")
+            nc.vector.tensor_copy(by_slot(k_grouped[:, :, t]), k_planes[t][:].indirect(k_list[:]))
+        keys = quantize(k_grouped[:], "k")
 
-        q_grouped = keep.tile([P, NQ, PACK], BF16, align_bytes=64, name="q_grouped")
+        q_grouped = sbuf([P, NQ, PACK], BF16, "q_grouped")
         for t in range(PACK - 1):
-            nc.vector.tensor_copy(q_grouped[:, :, t], q_tiles[t][:].indirect(q_list[:]))
+            nc.vector.tensor_copy(q_grouped[:, :, t], q_planes[t][:].indirect(q_list[:]))
 
         half_queries = [slice(h * HALF_Q, (h + 1) * HALF_Q) for h in range(HALVES)]
-        half_lists = [
-            q_list[:, h * HALF_Q // PER_LIST_COLUMN : (h + 1) * HALF_Q // PER_LIST_COLUMN] for h in range(HALVES)
-        ]
-        neg_max = keep.tile([P, Q_CHUNKS], F32, name="neg_max")
-        inv_total = keep.tile([P, Q_CHUNKS], F32, name="inv_total")
-        w_grouped = [keep.tile([P, HALF_Q, PACK], BF16, align_bytes=64, name="w_grouped%d" % h) for h in range(HALVES)]
+        neg_max = sbuf([P, Q_CHUNKS], F32, "neg_max")
+        inv_total = sbuf([P, Q_CHUNKS], F32, "inv_total")
+        w_grouped = [sbuf([P, HALF_Q, PACK], BF16, "w_grouped%d" % h) for h in range(HALVES)]
+        v1_window = sbuf([P, T], BF16, "v1_window")
 
-        def gather_last_queries(h):
+        def gather_last_plane(h):
             last = PACK - 1
-            nc.vector.tensor_copy(q_grouped[:, half_queries[h], last], q_tiles[last][:].indirect(half_lists[h]))
+            nc.vector.tensor_copy(q_grouped[:, half_queries[h], last], q_planes[last][:].indirect(half_of(q_list, h)))
 
-        def quantize_queries(first, count, name):
-            return quantize(q_grouped[:, first : first + count, :], count, name)
-
-        def scores(b, start, codes, scales):
+        def scores(b, queries, first):
             bank = psum.tile([P, N], F32, name="bank%d" % b)
-            nc.tensor.matmul_mx(
-                out=bank[:],
-                lhsT=codes[:, start : start + P].bitcast(FP8X4),
-                lhsT_scale=scales[:, start : start + P],
-                rhs=k_codes[:].bitcast(FP8X4),
-                rhs_scale=k_scales[:],
-                start=True,
-                stop=True,
-            )
+            product(bank[:], [part[:, first : first + P] for part in queries], keys)
             return bank
 
-        def softmax(b, bank, paired=True, name=None):
+        def softmax(b, bank, order):
             nc.vector.tensor_reduce(neg_max[:, b : b + 1], bank[:], AXIS_X, MAX, negate=True)
-            prob = keep.tile([P, N], F32, align_bytes=64, name=name or "prob%d" % b)
+            prob = sbuf([P, N], F32, "prob%d" % b)
             nc.scalar.activation(
-                prob[:] if paired else prob[:].rearrange("p (u e s) -> p u e s", u=2, e=2),
-                bank[:] if paired else bank[:].rearrange("p (u s e) -> p u e s", u=2, e=2),
+                prob[:].rearrange("p (%s) -> p %s" % (order, order), u=PAIR, e=PAIR),
+                bank[:].rearrange("p (u s e) -> p %s" % order, u=PAIR, e=PAIR),
                 EXP,
                 bias=neg_max[:, b : b + 1],
                 accum_out=total[:, b : b + 1],
@@ -162,20 +168,18 @@ def tile_attend_mod_sorted_kernel(tc, xq, kT, vT, vs, offs, qoffs, out):
             h, i = divmod(b, Q_CHUNKS // HALVES)
             return w_grouped[h][:, i * P : (i + 1) * P, :]
 
+        def turn_pairs(paired, grouped, bank_name):
+            words = paired[:].bitcast(F32)
+            bank = psum.tile([P, PAIR, P], F32, name=bank_name)
+            for u in range(PAIR):
+                nc.tensor.transpose(bank[:, u, :], words[:, u * P : (u + 1) * P], ident[:])
+            grouped_words = grouped.rearrange("p x t -> p (x t)").bitcast(F32).rearrange("p (x u) -> p x u", u=PAIR)
+            nc.scalar.copy(grouped_words, bank[:].rearrange(SIDE_BY_SIDE))
+
         def multiply_on_gpsimd(b, prob):
-            weights = keep.tile([P, N], BF16, align_bytes=64, name="weights%d" % b)
+            weights = sbuf([P, N], BF16, "weights%d" % b)
             nc.gpsimd.tensor_tensor(weights[:], prob[:], vs_row[:], MULT)
             return weights
-
-        def turn_weights(b, weights, bank_name):
-            turn_pairs(weights[:].bitcast(F32).rearrange("p (u s) -> p u s", u=2), w_columns(b), bank_name)
-
-        def turn_pairs(words, grouped, bank_name):
-            bank = psum.tile([P, 2, P], F32, name=bank_name)
-            for u in range(2):
-                nc.tensor.transpose(bank[:, u, :], words[:, u, :], ident[:])
-            grouped_words = grouped.rearrange("p x t -> p (x t)").bitcast(F32).rearrange("p (x u) -> p x u", u=2)
-            nc.scalar.copy(grouped_words, bank[:].rearrange(COPY_OUT))
 
         def turn_probs(prob, bank_name):
             bank = psum.tile([P, PACK, P], F32, name=bank_name)
@@ -186,106 +190,88 @@ def tile_attend_mod_sorted_kernel(tc, xq, kT, vT, vs, offs, qoffs, out):
         def multiply_on_vector(b, bank):
             nc.vector.tensor_tensor(
                 w_columns(b),
-                bank[:].rearrange(COPY_OUT),
+                bank[:].rearrange(SIDE_BY_SIDE),
                 vs_column[:].unsqueeze(1).to_broadcast([P, P, PACK]),
                 MULT,
             )
 
-        def gather_values_on_vector(name):
-            picked = keep.tile([P, N], BF16, align_bytes=64, name=name)
-            by_slot = picked[:].rearrange("p (u s e) -> p s u e", u=2, e=2)
-            nc.vector.tensor_copy(by_slot, v0_tile[:].indirect(k_list[:]))
-            return picked
-
-        v1_window = keep.tile([P, T], BF16, name="v1_window")
-
-        def cast_values(c):
+        def cast_piece(c):
             nc.scalar.activation(v1_window[:, V_CUTS[c] : V_CUTS[c + 1]], v1_pieces[c][:], COPY)
 
-        def gather_values_on_scalar(window, picked, h):
-            by_slot = picked[:].rearrange("p (u s e) -> p s u e", u=2, e=2)
-            columns = N // PER_LIST_COLUMN // HALVES
-            nc.scalar.activation(
-                by_slot[:, h * P // HALVES : (h + 1) * P // HALVES],
-                window.indirect(k_list[:, h * columns : (h + 1) * columns]),
-                COPY,
-            )
+        def gather_v1_half(h, window):
+            partitions_to_be = slice(h * P // HALVES, (h + 1) * P // HALVES)
+            nc.scalar.activation(by_slot(v1_picked[:])[:, partitions_to_be], window.indirect(half_of(k_list, h)), COPY)
 
         def turn_values(e, picked, bank_name):
-            grouped = keep.tile([P, P, PACK], BF16, align_bytes=64, name="v_grouped%d" % e)
-            turn_pairs(picked[:].bitcast(F32).rearrange("p (u s) -> p u s", u=2), grouped[:], bank_name)
+            grouped = sbuf([P, P, PACK], BF16, "v_grouped%d" % e)
+            turn_pairs(picked, grouped[:], bank_name)
             return grouped
 
-        def products(values, halves, name, bank_name):
-            v_codes, v_scales = values
+        def weighted_sums(values, halves, name, bank_name):
             bank = psum.tile([P, len(halves), HALF_Q], F32, name=bank_name)
-            for i, (w_codes, w_scales) in enumerate(halves):
-                nc.tensor.matmul_mx(
-                    out=bank[:, i, :],
-                    lhsT=v_codes[:].bitcast(FP8X4),
-                    lhsT_scale=v_scales[:],
-                    rhs=w_codes[:].bitcast(FP8X4),
-                    rhs_scale=w_scales[:],
-                    start=True,
-                    stop=True,
-                )
-            sums = keep.tile([P, len(halves) * HALF_Q], F32, align_bytes=64, name=name)
+            for i, weights in enumerate(halves):
+                product(bank[:, i, :], [part[:] for part in values], weights)
+            sums = sbuf([P, len(halves) * HALF_Q], F32, name)
             nc.scalar.copy(sums[:], bank[:].rearrange("p h q -> p (h q)"))
             return sums
 
-
-        def turn_inverse(h, bank_name):
-            bank = psum.tile([P, Q_CHUNKS // HALVES, P], F32, name=bank_name)
+        def spread_inverse(h):
+            bank = psum.tile([P, Q_CHUNKS // HALVES, P], F32, name="bank5")
             for i in range(Q_CHUNKS // HALVES):
                 b = h * Q_CHUNKS // HALVES + i
                 nc.tensor.transpose(bank[:, i, :], inv_total[:, b : b + 1].to_broadcast([P, P]), ident[:])
-            return bank[:].rearrange("p b q -> p (b q)")
+            nc.scalar.copy(inverse[:, half_queries[h]], bank[:].rearrange("p b q -> p (b q)"))
 
-        def put_back(e, listed, sums, inverse):
-            nc.vector.tensor_tensor(out_windows[e][:].indirect(listed), sums[:], inverse, MULT)
+        def put_back(e, listed, sums, inverse_part):
+            nc.vector.tensor_tensor(out_windows[e][:].indirect(listed), sums[:], inverse_part, MULT)
 
-        for c in range(len(V_CUTS) - 2):
-            cast_values(c)
-        total = keep.tile([P, Q_CHUNKS], F32, align_bytes=64, name="v1_piece3")
-        picked1 = keep.tile([P, N], BF16, align_bytes=64, name="v_picked1")
-        gather_values_on_scalar(v1_window[:, 0:FIRST_TOKENS], picked1, 0)
-        gather_last_queries(0)
-        score0 = scores(0, 0, *quantize_queries(0, P, "q0a"))
-        gather_last_queries(1)
-        score1 = scores(1, 0, *quantize_queries(P, P, "q0b"))
-        prob0 = softmax(0, score0)
+        for c in range(LAST_PIECE):
+            cast_piece(c)
+        total = sbuf([P, Q_CHUNKS], F32, "v1_piece%d" % (LAST_PIECE - 1))
+        v1_picked = sbuf([P, N], BF16, "v1_picked")
+        gather_v1_half(0, v1_window[:, 0:FIRST_TOKENS])
+
+        gather_last_plane(0)
+        score0 = scores(0, quantize(q_grouped[:, 0:P, :], "q0"), 0)
+        gather_last_plane(1)
+        score1 = scores(1, quantize(q_grouped[:, P:HALF_Q, :], "q1"), 0)
+        prob0 = softmax(0, score0, "u s e")
         weights0 = multiply_on_gpsimd(0, prob0)
-        q_half1 = quantize_queries(HALF_Q, HALF_Q, "q1")
-        prob1 = softmax(1, score1, paired=False)
-        score2 = scores(2, 0, *q_half1)
-        score3 = scores(3, P, *q_half1)
+        q23 = quantize(q_grouped[:, half_queries[1], :], "q23")
+        prob1 = softmax(1, score1, "u e s")
+        score2 = scores(2, q23, 0)
+        score3 = scores(3, q23, P)
         turned1 = turn_probs(prob1, "bank6")
-        prob2 = softmax(2, score2)
+        prob2 = softmax(2, score2, "u s e")
         weights2 = multiply_on_gpsimd(2, prob2)
-        prob3 = softmax(3, score3, paired=False)
-        turn_weights(0, weights0, "bank4")
-        picked0 = gather_values_on_vector("q1_codes")
+        prob3 = softmax(3, score3, "u e s")
+        turn_pairs(weights0, w_columns(0), "bank4")
+
+        v0_picked = sbuf([P, N], BF16, "q23_codes")
+        nc.vector.tensor_copy(by_slot(v0_picked[:]), v0_window[:].indirect(k_list[:]))
         multiply_on_vector(1, turned1)
         nc.vector.reciprocal(inv_total[:], total[:])
-        grouped0 = turn_values(0, picked0, "bank0")
-        cast_values(len(V_CUTS) - 2)
+        v0_grouped = turn_values(0, v0_picked, "bank0")
+        cast_piece(LAST_PIECE)
         turned3 = turn_probs(prob3, "bank7")
-        turn_weights(2, weights2, "bank4")
-        inverse = keep.tile([P, NQ], F32, name="inverse")
-        nc.scalar.copy(inverse[:, half_queries[0]], turn_inverse(0, "bank5"))
-        w_half0 = quantize(w_grouped[0][:], HALF_Q, "w0", "prob2")
-        values0 = quantize(grouped0[:], P, "v0")
-        sums00 = products(values0, [w_half0], "sums00", "bank1")
-        gather_values_on_scalar(v1_window[:], picked1, 1)
+        turn_pairs(weights2, w_columns(2), "bank4")
+        inverse = sbuf([P, NQ], F32, "inverse")
+        spread_inverse(0)
+
+        w_half0 = quantize(w_grouped[0][:], "w0", "prob2")
+        values0 = quantize(v0_grouped[:], "v0")
+        sums00 = weighted_sums(values0, [w_half0], "sums00", "bank1")
+        gather_v1_half(1, v1_window[:])
         multiply_on_vector(3, turned3)
-        w_half1 = quantize(w_grouped[1][:], HALF_Q, "w1")
-        nc.scalar.copy(inverse[:, half_queries[1]], turn_inverse(1, "bank5"))
-        grouped1 = turn_values(1, picked1, "bank1")
-        sums01 = products(values0, [w_half1], "v_picked1", "bank2")
-        put_back(0, half_lists[0], sums00, inverse[:, half_queries[0]])
-        values1 = quantize(grouped1[:], P, "v1")
-        sums1 = products(values1, [w_half0, w_half1], "sums1", "bank3")
-        put_back(0, half_lists[1], sums01, inverse[:, half_queries[1]])
+        w_half1 = quantize(w_grouped[1][:], "w1")
+        spread_inverse(1)
+
+        v1_grouped = turn_values(1, v1_picked, "bank1")
+        sums01 = weighted_sums(values0, [w_half1], "v1_picked", "bank2")
+        put_back(0, half_of(q_list, 0), sums00, inverse[:, half_queries[0]])
+        values1 = quantize(v1_grouped[:], "v1")
+        sums1 = weighted_sums(values1, [w_half0, w_half1], "sums1", "bank3")
+        put_back(0, half_of(q_list, 1), sums01, inverse[:, half_queries[1]])
         nc.sync.dma_start(out[0:P, :], out_windows[0][:])
         put_back(1, q_list[:], sums1, inverse[:])
         nc.sync.dma_start(out[P:DV, :], out_windows[1][:])

@@ -32,7 +32,7 @@ HALF_N = N // HALVES
 FIRST_TOKENS = T - HALF_N
 V_CUTS = (0, T // 4, T // 2, 3 * T // 4, FIRST_TOKENS, T)
 LAST_PIECE = len(V_CUTS) - 2
-ALIGN = 64
+ALIGN = 256
 SIDE_BY_SIDE = "p t x -> p x t"
 
 FLOPS = 2 * NQ * N * D + 2 * NQ * N * DV

@@ -88,15 +88,17 @@ def tile_attend_mod_sorted_kernel(tc, xq, kT, vT, vs, offs, qoffs, out):
         def by_slot(paired):
             return paired.rearrange("p (u s e) -> p s u e", u=PAIR, e=PAIR)
 
-        def quantize(grouped, name, codes_name=None):
+        def quantize(grouped, name, codes_name=None, calls=1):
             width = grouped.shape[1]
             codes = sbuf([P, width], U32, codes_name or name + "_codes")
             scales = sbuf([P, width], U8, name + "_scales")
-            nc.vector.quantize_mx(
-                out=codes[:].bitcast(FP8X4),
-                scales=scales[:],
-                in_=grouped.rearrange("p c t -> p (c t)"),
-            )
+            for i in range(calls):
+                columns = slice(i * width // calls, (i + 1) * width // calls)
+                nc.vector.quantize_mx(
+                    out=codes[:, columns].bitcast(FP8X4),
+                    scales=scales[:, columns],
+                    in_=grouped[:, columns, :].rearrange("p c t -> p (c t)"),
+                )
             return codes, scales
 
         def product(result, stationary, moving):
@@ -215,6 +217,10 @@ def tile_attend_mod_sorted_kernel(tc, xq, kT, vT, vs, offs, qoffs, out):
             nc.scalar.copy(sums[:], bank[:].rearrange("p h q -> p (h q)"))
             return sums
 
+        def invert_totals(h):
+            chunks = slice(h * Q_CHUNKS // HALVES, (h + 1) * Q_CHUNKS // HALVES)
+            nc.vector.reciprocal(inv_total[:, chunks], total[:, chunks])
+
         def spread_inverse(h):
             bank = psum.tile([P, Q_CHUNKS // HALVES, P], F32, name="bank5")
             for i in range(Q_CHUNKS // HALVES):
@@ -245,25 +251,26 @@ def tile_attend_mod_sorted_kernel(tc, xq, kT, vT, vs, offs, qoffs, out):
         prob2 = softmax(2, score2, "u s e")
         weights2 = multiply_on_gpsimd(2, prob2)
         prob3 = softmax(3, score3, "u e s")
+        invert_totals(0)
         turn_pairs(weights0, w_columns(0), "bank4")
+        inverse = sbuf([P, NQ], F32, "inverse")
+        spread_inverse(0)
 
         v0_picked = sbuf([P, N], BF16, "q23_codes")
         nc.vector.tensor_copy(by_slot(v0_picked[:]), v0_window[:].indirect(k_list[:]))
         multiply_on_vector(1, turned1)
-        nc.vector.reciprocal(inv_total[:], total[:])
         v0_grouped = turn_values(0, v0_picked, "bank0")
         cast_piece(LAST_PIECE)
-        turned3 = turn_probs(prob3, "bank7")
+        turned3 = turn_probs(prob3, "bank6")
         turn_pairs(weights2, w_columns(2), "bank4")
-        inverse = sbuf([P, NQ], F32, "inverse")
-        spread_inverse(0)
 
-        w_half0 = quantize(w_grouped[0][:], "w0", "prob2")
+        w_half0 = quantize(w_grouped[0][:], "w0", "prob2", calls=2)
         values0 = quantize(v0_grouped[:], "v0")
         sums00 = weighted_sums(values0, [w_half0], "sums00", "bank1")
         gather_v1_half(1, v1_window[:])
         multiply_on_vector(3, turned3)
-        w_half1 = quantize(w_grouped[1][:], "w1")
+        invert_totals(1)
+        w_half1 = quantize(w_grouped[1][:], "w1", calls=2)
         spread_inverse(1)
 
         v1_grouped = turn_values(1, v1_picked, "bank1")

@@ -261,7 +261,7 @@ def tile_attend_mod_sorted_kernel(tc, xq, kT, vT, vs, offs, qoffs, out):
         multiply_on_vector(1, turned1)
         v0_grouped = turn_values(0, v0_picked, "bank0")
         cast_piece(LAST_PIECE)
-        turned3 = turn_probs(prob3, "bank6")
+        turned3 = turn_probs(prob3, "bank7")
         turn_pairs(weights2, w_columns(2), "bank4")
 
         w_half0 = quantize(w_grouped[0][:], "w0", "prob2", calls=2)

@@ -106,8 +106,8 @@ def tile_attend_mod_sorted_kernel(tc, xq, kT, vT, vs, offs, qoffs, out):
                 out=result,
                 lhsT=stationary[0].bitcast(FP8X4),
                 lhsT_scale=stationary[1],
-                rhs=moving[0][:].bitcast(FP8X4),
-                rhs_scale=moving[1][:],
+                rhs=moving[0].bitcast(FP8X4),
+                rhs_scale=moving[1],
                 start=True,
                 stop=True,
             )
@@ -151,7 +151,7 @@ def tile_attend_mod_sorted_kernel(tc, xq, kT, vT, vs, offs, qoffs, out):
 
         def scores(b, queries, first):
             bank = psum.tile([P, N], F32, name="bank%d" % b)
-            product(bank[:], [part[:, first : first + P] for part in queries], keys)
+            product(bank[:], [part[:, first : first + P] for part in queries], [part[:] for part in keys])
             return bank
 
         def softmax(b, bank, order):
@@ -212,7 +212,7 @@ def tile_attend_mod_sorted_kernel(tc, xq, kT, vT, vs, offs, qoffs, out):
         def weighted_sums(values, halves, name, bank_name):
             bank = psum.tile([P, len(halves), HALF_Q], F32, name=bank_name)
             for i, weights in enumerate(halves):
-                product(bank[:, i, :], [part[:] for part in values], weights)
+                product(bank[:, i, :], [part[:] for part in values], [part[:] for part in weights])
             sums = sbuf([P, len(halves) * HALF_Q], F32, name)
             nc.scalar.copy(sums[:], bank[:].rearrange("p h q -> p (h q)"))
             return sums
@@ -266,7 +266,12 @@ def tile_attend_mod_sorted_kernel(tc, xq, kT, vT, vs, offs, qoffs, out):
 
         w_half0 = quantize(w_grouped[0][:], "w0", "prob2", calls=2)
         values0 = quantize(v0_grouped[:], "v0")
-        sums00 = weighted_sums(values0, [w_half0], "sums00", "bank1")
+        sums00 = sbuf([P, HALF_Q], F32, "sums00")
+        for i, bank_name in enumerate(("bank1", "bank0")):
+            columns = slice(i * P, (i + 1) * P)
+            bank = psum.tile([P, P], F32, name=bank_name)
+            product(bank[:], [part[:] for part in values0], [part[:, columns] for part in w_half0])
+            nc.scalar.copy(sums00[:, columns], bank[:])
         gather_v1_half(1, v1_window[:])
         multiply_on_vector(3, turned3)
         invert_totals(1)

@@ -282,7 +282,11 @@ def tile_attend_mod_sorted_kernel(tc, xq, kT, vT, vs, offs, qoffs, out):
         sums01 = weighted_sums(values0, [w_half1], "v1_picked", "bank2")
         put_back(0, half_of(q_list, 0), sums00, inverse[:, half_queries[0]])
         values1 = quantize(v1_grouped[:], "v1")
-        sums1 = weighted_sums(values1, [w_half0, w_half1], "sums1", "bank3")
+        sums1 = sbuf([P, NQ], F32, "sums1")
+        for weights, columns, bank_name in zip((w_half0, w_half1), half_queries, ("bank3", "bank6")):
+            bank = psum.tile([P, HALF_Q], F32, name=bank_name)
+            product(bank[:], [part[:] for part in values1], [part[:] for part in weights])
+            nc.scalar.copy(sums1[:, columns], bank[:])
         put_back(0, half_of(q_list, 1), sums01, inverse[:, half_queries[1]])
         nc.sync.dma_start(out[0:P, :], out_windows[0][:])
         put_back(1, q_list[:], sums1, inverse[:])

@@ -247,6 +247,9 @@ def tile_attend_mod_sorted_kernel(tc, xq, kT, vT, vs, offs, qoffs, out):
         prob1 = softmax(1, score1, "u e s")
         score2 = scores(2, q23, 0)
         score3 = scores(3, q23, P)
+        for columns, bank_name in ((N, "bank7"), (HALF_N, "bank5")):
+            bank = psum.tile([P, columns], F32, name=bank_name)
+            product(bank[:], [part[:, P:HALF_Q] for part in q23], [part[:, 0:columns] for part in keys])
         turned1 = turn_probs(prob1, "bank6")
         prob2 = softmax(2, score2, "u s e")
         weights2 = multiply_on_gpsimd(2, prob2)

@@ -27,6 +27,7 @@ PER_LIST_COLUMN = 16
 Q_CHUNKS = NQ // P
 V_CHUNKS = DV // P
 HALVES = 2
+CHUNKS_PER_HALF = Q_CHUNKS // HALVES
 HALF_Q = NQ // HALVES
 HALF_N = N // HALVES
 FIRST_TOKENS = T - HALF_N
@@ -151,7 +152,7 @@ def tile_attend_mod_sorted_kernel(tc, xq, kT, vT, vs, offs, qoffs, out):
 
         def scores(b, queries, first):
             bank = psum.tile([P, N], F32, name="bank%d" % b)
-            product(bank[:], [part[:, first : first + P] for part in queries], [part[:] for part in keys])
+            product(bank[:], columns_of(queries, first, P), columns_of(keys, 0, N))
             return bank
 
         def softmax(b, bank, order):
@@ -167,7 +168,7 @@ def tile_attend_mod_sorted_kernel(tc, xq, kT, vT, vs, offs, qoffs, out):
             return prob
 
         def w_columns(b):
-            h, i = divmod(b, Q_CHUNKS // HALVES)
+            h, i = divmod(b, CHUNKS_PER_HALF)
             return w_grouped[h][:, i * P : (i + 1) * P, :]
 
         def turn_pairs(paired, grouped, bank_name):
@@ -209,22 +210,26 @@ def tile_attend_mod_sorted_kernel(tc, xq, kT, vT, vs, offs, qoffs, out):
             turn_pairs(picked, grouped[:], bank_name)
             return grouped
 
-        def weighted_sums(values, halves, name, bank_name):
-            bank = psum.tile([P, len(halves), HALF_Q], F32, name=bank_name)
-            for i, weights in enumerate(halves):
-                product(bank[:, i, :], [part[:] for part in values], [part[:] for part in weights])
-            sums = sbuf([P, len(halves) * HALF_Q], F32, name)
-            nc.scalar.copy(sums[:], bank[:].rearrange("p h q -> p (h q)"))
+        def weighted_sums(values, runs, name, bank_names):
+            width = runs[0][0].shape[1]
+            sums = sbuf([P, len(runs) * width], F32, name)
+            for i, (weights, bank_name) in enumerate(zip(runs, bank_names)):
+                bank = psum.tile([P, width], F32, name=bank_name)
+                product(bank[:], [part[:] for part in values], weights)
+                nc.scalar.copy(sums[:, i * width : (i + 1) * width], bank[:])
             return sums
 
+        def columns_of(quantised, first, count):
+            return [part[:, first : first + count] for part in quantised]
+
         def invert_totals(h):
-            chunks = slice(h * Q_CHUNKS // HALVES, (h + 1) * Q_CHUNKS // HALVES)
+            chunks = slice(h * CHUNKS_PER_HALF, (h + 1) * CHUNKS_PER_HALF)
             nc.vector.reciprocal(inv_total[:, chunks], total[:, chunks])
 
         def spread_inverse(h):
-            bank = psum.tile([P, Q_CHUNKS // HALVES, P], F32, name="bank5")
-            for i in range(Q_CHUNKS // HALVES):
-                b = h * Q_CHUNKS // HALVES + i
+            bank = psum.tile([P, CHUNKS_PER_HALF, P], F32, name="bank5")
+            for i in range(CHUNKS_PER_HALF):
+                b = h * CHUNKS_PER_HALF + i
                 nc.tensor.transpose(bank[:, i, :], inv_total[:, b : b + 1].to_broadcast([P, P]), ident[:])
             nc.scalar.copy(inverse[:, half_queries[h]], bank[:].rearrange("p b q -> p (b q)"))
 
@@ -247,9 +252,9 @@ def tile_attend_mod_sorted_kernel(tc, xq, kT, vT, vs, offs, qoffs, out):
         prob1 = softmax(1, score1, "u e s")
         score2 = scores(2, q23, 0)
         score3 = scores(3, q23, P)
-        for columns, bank_name in ((N, "bank7"), (HALF_N, "bank5")):
-            bank = psum.tile([P, columns], F32, name=bank_name)
-            product(bank[:], [part[:, P:HALF_Q] for part in q23], [part[:, 0:columns] for part in keys])
+        for count, bank_name in ((N, "bank7"),):
+            unread = psum.tile([P, count], F32, name=bank_name)
+            product(unread[:], columns_of(q23, P, P), columns_of(keys, 0, count))
         turned1 = turn_probs(prob1, "bank6")
         prob2 = softmax(2, score2, "u s e")
         weights2 = multiply_on_gpsimd(2, prob2)
@@ -267,29 +272,22 @@ def tile_attend_mod_sorted_kernel(tc, xq, kT, vT, vs, offs, qoffs, out):
         turned3 = turn_probs(prob3, "bank7")
         turn_pairs(weights2, w_columns(2), "bank4")
 
-        w_half0 = quantize(w_grouped[0][:], "w0", "prob2", calls=2)
+        w_half0 = quantize(w_grouped[0][:], "w0", "prob2", calls=CHUNKS_PER_HALF)
         values0 = quantize(v0_grouped[:], "v0")
-        sums00 = sbuf([P, HALF_Q], F32, "sums00")
-        for i, bank_name in enumerate(("bank1", "bank0")):
-            columns = slice(i * P, (i + 1) * P)
-            bank = psum.tile([P, P], F32, name=bank_name)
-            product(bank[:], [part[:] for part in values0], [part[:, columns] for part in w_half0])
-            nc.scalar.copy(sums00[:, columns], bank[:])
+        first_chunks = [columns_of(w_half0, i * P, P) for i in range(CHUNKS_PER_HALF)]
+        sums00 = weighted_sums(values0, first_chunks, "sums00", ("bank1", "bank0"))
         gather_v1_half(1, v1_window[:])
         multiply_on_vector(3, turned3)
         invert_totals(1)
-        w_half1 = quantize(w_grouped[1][:], "w1", calls=2)
+        w_half1 = quantize(w_grouped[1][:], "w1", calls=CHUNKS_PER_HALF)
         spread_inverse(1)
 
         v1_grouped = turn_values(1, v1_picked, "bank1")
-        sums01 = weighted_sums(values0, [w_half1], "v1_picked", "bank2")
+        w_halves = [columns_of(half, 0, HALF_Q) for half in (w_half0, w_half1)]
+        sums01 = weighted_sums(values0, w_halves[1:], "v1_picked", ("bank2",))
         put_back(0, half_of(q_list, 0), sums00, inverse[:, half_queries[0]])
         values1 = quantize(v1_grouped[:], "v1")
-        sums1 = sbuf([P, NQ], F32, "sums1")
-        for weights, columns, bank_name in zip((w_half0, w_half1), half_queries, ("bank3", "bank6")):
-            bank = psum.tile([P, HALF_Q], F32, name=bank_name)
-            product(bank[:], [part[:] for part in values1], [part[:] for part in weights])
-            nc.scalar.copy(sums1[:, columns], bank[:])
+        sums1 = weighted_sums(values1, w_halves, "sums1", ("bank3", "bank6"))
         put_back(0, half_of(q_list, 1), sums01, inverse[:, half_queries[1]])
         nc.sync.dma_start(out[0:P, :], out_windows[0][:])
         put_back(1, q_list[:], sums1, inverse[:])

@@ -243,12 +243,12 @@ def tile_attend_mod_sorted_kernel(tc, xq, kT, vT, vs, offs, qoffs, out):
         gather_v1_half(0, v1_window[:, 0:FIRST_TOKENS])
 
         gather_last_plane(0)
-        score0 = scores(0, quantize(q_grouped[:, 0:P, :], "q0"), 0)
         gather_last_plane(1)
+        score0 = scores(0, quantize(q_grouped[:, 0:P, :], "q0"), 0)
         score1 = scores(1, quantize(q_grouped[:, P:HALF_Q, :], "q1"), 0)
+        q23 = quantize(q_grouped[:, half_queries[1], :], "q23")
         prob0 = softmax(0, score0, "u s e")
         weights0 = multiply_on_gpsimd(0, prob0)
-        q23 = quantize(q_grouped[:, half_queries[1], :], "q23")
         prob1 = softmax(1, score1, "u e s")
         score2 = scores(2, q23, 0)
         score3 = scores(3, q23, P)

@@ -12,6 +12,7 @@ FP8X4 = mybir.dt.float8_e4m3fn_x4
 COPY = mybir.ActivationFunctionType.Copy
 EXP = mybir.ActivationFunctionType.Exp
 MULT = mybir.AluOpType.mult
+ADD = mybir.AluOpType.add
 MAX = mybir.AluOpType.max
 AXIS_X = mybir.AxisListType.X
 
@@ -44,6 +45,7 @@ def tile_attend_mod_sorted_kernel(tc, xq, kT, vT, vs, offs, qoffs, out):
     nc = tc.nc
     with ExitStack() as ctx:
         keep = ctx.enter_context(tc.tile_pool(name="keep", bufs=1))
+        shared = ctx.enter_context(tc.tile_pool(name="shared", bufs=1))
         psum = ctx.enter_context(tc.psum_pool(name="psum", bufs=1))
 
         def sbuf(shape, dtype, name):
@@ -89,10 +91,13 @@ def tile_attend_mod_sorted_kernel(tc, xq, kT, vT, vs, offs, qoffs, out):
         def by_slot(paired):
             return paired.rearrange("p (u s e) -> p s u e", u=PAIR, e=PAIR)
 
-        def quantize(grouped, name, codes_name=None, calls=1):
+        def quantize(grouped, name, codes_name=None, calls=1, scales_at=None):
             width = grouped.shape[1]
             codes = sbuf([P, width], U32, codes_name or name + "_codes")
-            scales = sbuf([P, width], U8, name + "_scales")
+            if scales_at is None:
+                scales = sbuf([P, width], U8, name + "_scales")
+            else:
+                scales = shared.tile([P, width], U8, align_bytes=64, offset=scales_at, name=name + "_scales")
             for i in range(calls):
                 columns = slice(i * width // calls, (i + 1) * width // calls)
                 nc.vector.quantize_mx(
@@ -145,10 +150,6 @@ def tile_attend_mod_sorted_kernel(tc, xq, kT, vT, vs, offs, qoffs, out):
         inv_total = sbuf([P, Q_CHUNKS], F32, "inv_total")
         w_grouped = [sbuf([P, HALF_Q, PACK], BF16, "w_grouped%d" % h) for h in range(HALVES)]
         v1_window = sbuf([P, T], BF16, "v1_window")
-
-        def gather_last_plane(h):
-            last = PACK - 1
-            nc.vector.tensor_copy(q_grouped[:, half_queries[h], last], q_planes[last][:].indirect(half_of(q_list, h)))
 
         def scores(b, queries, first):
             bank = psum.tile([P, N], F32, name="bank%d" % b)
@@ -242,11 +243,14 @@ def tile_attend_mod_sorted_kernel(tc, xq, kT, vT, vs, offs, qoffs, out):
         v1_picked = sbuf([P, N], BF16, "v1_picked")
         gather_v1_half(0, v1_window[:, 0:FIRST_TOKENS])
 
-        gather_last_plane(0)
-        gather_last_plane(1)
+        first_chunk = shared.tile([P, P], BF16, align_bytes=64, offset=0, name="first_chunk")
+        first_columns = P // PER_LIST_COLUMN
+        nc.vector.tensor_copy(first_chunk[:], q_planes[PACK - 1][:].indirect(q_list[:, 0:first_columns]))
+        nc.gpsimd.tensor_scalar(q_grouped[:, 0:P, PACK - 1], first_chunk[:], 1.0, 0.0, MULT, ADD)
+        nc.vector.tensor_copy(q_grouped[:, P:NQ, PACK - 1], q_planes[PACK - 1][:].indirect(q_list[:, first_columns:]))
         score0 = scores(0, quantize(q_grouped[:, 0:P, :], "q0"), 0)
-        score1 = scores(1, quantize(q_grouped[:, P:HALF_Q, :], "q1"), 0)
-        q23 = quantize(q_grouped[:, half_queries[1], :], "q23")
+        score1 = scores(1, quantize(q_grouped[:, P:HALF_Q, :], "q1", scales_at=0), 0)
+        q23 = quantize(q_grouped[:, half_queries[1], :], "q23", scales_at=P)
         prob0 = softmax(0, score0, "u s e")
         weights0 = multiply_on_gpsimd(0, prob0)
         prob1 = softmax(1, score1, "u e s")

@@ -243,22 +243,31 @@ def tile_attend_mod_sorted_kernel(tc, xq, kT, vT, vs, offs, qoffs, out):
         v1_picked = sbuf([P, N], BF16, "v1_picked")
         gather_v1_half(0, v1_window[:, 0:FIRST_TOKENS])
 
-        first_chunk = shared.tile([P, P], BF16, align_bytes=64, offset=0, name="first_chunk")
-        first_columns = P // PER_LIST_COLUMN
-        nc.vector.tensor_copy(first_chunk[:], q_planes[PACK - 1][:].indirect(q_list[:, 0:first_columns]))
-        nc.gpsimd.tensor_scalar(q_grouped[:, 0:P, PACK - 1], first_chunk[:], 1.0, 0.0, MULT, ADD)
-        nc.vector.tensor_copy(q_grouped[:, P:NQ, PACK - 1], q_planes[PACK - 1][:].indirect(q_list[:, first_columns:]))
+        def last_plane(first, count):
+            columns = slice(first // PER_LIST_COLUMN, (first + count) // PER_LIST_COLUMN)
+            return q_planes[PACK - 1][:].indirect(q_list[:, columns])
+
+        def place_on_gpsimd(b, picked):
+            nc.vector.tensor_copy(picked, last_plane(b * P, P))
+            nc.gpsimd.tensor_scalar(q_grouped[:, b * P : (b + 1) * P, PACK - 1], picked, 1.0, 0.0, MULT, ADD)
+
+        first_chunk = shared.tile([P, 2 * P], BF16, align_bytes=64, offset=0, name="first_chunk")
+        place_on_gpsimd(0, first_chunk[:, 0:P])
+        nc.vector.tensor_copy(q_grouped[:, P : 3 * P, PACK - 1], last_plane(P, 2 * P))
         score0 = scores(0, quantize(q_grouped[:, 0:P, :], "q0"), 0)
-        score1 = scores(1, quantize(q_grouped[:, P:HALF_Q, :], "q1", scales_at=0), 0)
-        q23 = quantize(q_grouped[:, half_queries[1], :], "q23", scales_at=P)
+        last_chunk = shared.tile([P, P], BF16, align_bytes=64, offset=0, name="last_chunk")
+        place_on_gpsimd(3, last_chunk[:])
+        q12 = quantize(q_grouped[:, P : 3 * P, :], "q12", scales_at=2 * P)
+        score1 = scores(1, q12, 0)
+        score2 = scores(2, q12, P)
         prob0 = softmax(0, score0, "u s e")
         weights0 = multiply_on_gpsimd(0, prob0)
+        q3 = quantize(q_grouped[:, 3 * P : NQ, :], "q3", "q0_codes")
         prob1 = softmax(1, score1, "u e s")
-        score2 = scores(2, q23, 0)
-        score3 = scores(3, q23, P)
+        score3 = scores(3, q3, 0)
         for count, bank_name in ((N, "bank7"),):
             unread = psum.tile([P, count], F32, name=bank_name)
-            product(unread[:], columns_of(q23, P, P), columns_of(keys, 0, count))
+            product(unread[:], columns_of(q3, 0, P), columns_of(keys, 0, count))
         turned1 = turn_probs(prob1, "bank6")
         prob2 = softmax(2, score2, "u s e")
         weights2 = multiply_on_gpsimd(2, prob2)
@@ -268,7 +277,7 @@ def tile_attend_mod_sorted_kernel(tc, xq, kT, vT, vs, offs, qoffs, out):
         inverse = sbuf([P, NQ], F32, "inverse")
         spread_inverse(0)
 
-        v0_picked = sbuf([P, N], BF16, "q23_codes")
+        v0_picked = sbuf([P, N], BF16, "q0_codes")
         nc.vector.tensor_copy(by_slot(v0_picked[:]), v0_window[:].indirect(k_list[:]))
         multiply_on_vector(1, turned1)
         v0_grouped = turn_values(0, v0_picked, "bank0")

@@ -256,13 +256,14 @@ def tile_attend_mod_sorted_kernel(tc, xq, kT, vT, vs, offs, qoffs, out):
         nc.vector.tensor_copy(q_grouped[:, P : 3 * P, PACK - 1], last_plane(P, 2 * P))
         score0 = scores(0, quantize(q_grouped[:, 0:P, :], "q0"), 0)
         last_chunk = shared.tile([P, P], BF16, align_bytes=64, offset=0, name="last_chunk")
-        place_on_gpsimd(3, last_chunk[:])
+        nc.vector.tensor_copy(last_chunk[:], last_plane(3 * P, P))
         q12 = quantize(q_grouped[:, P : 3 * P, :], "q12", scales_at=2 * P)
+        nc.vector.tensor_copy(q_grouped[:, 3 * P : NQ, PACK - 1], last_chunk[:])
+        q3 = quantize(q_grouped[:, 3 * P : NQ, :], "q3")
         score1 = scores(1, q12, 0)
         score2 = scores(2, q12, P)
         prob0 = softmax(0, score0, "u s e")
         weights0 = multiply_on_gpsimd(0, prob0)
-        q3 = quantize(q_grouped[:, 3 * P : NQ, :], "q3", "q0_codes")
         prob1 = softmax(1, score1, "u e s")
         score3 = scores(3, q3, 0)
         for count, bank_name in ((N, "bank7"),):
@@ -277,7 +278,7 @@ def tile_attend_mod_sorted_kernel(tc, xq, kT, vT, vs, offs, qoffs, out):
         inverse = sbuf([P, NQ], F32, "inverse")
         spread_inverse(0)
 
-        v0_picked = sbuf([P, N], BF16, "q0_codes")
+        v0_picked = sbuf([P, N], BF16, "q3_codes")
         nc.vector.tensor_copy(by_slot(v0_picked[:]), v0_window[:].indirect(k_list[:]))
         multiply_on_vector(1, turned1)
         v0_grouped = turn_values(0, v0_picked, "bank0")

@@ -227,8 +227,8 @@ def tile_attend_mod_sorted_kernel(tc, xq, kT, vT, vs, offs, qoffs, out):
             chunks = slice(h * CHUNKS_PER_HALF, (h + 1) * CHUNKS_PER_HALF)
             nc.vector.reciprocal(inv_total[:, chunks], total[:, chunks])
 
-        def spread_inverse(h):
-            bank = psum.tile([P, CHUNKS_PER_HALF, P], F32, name="bank5")
+        def spread_inverse(h, bank_name):
+            bank = psum.tile([P, CHUNKS_PER_HALF, P], F32, name=bank_name)
             for i in range(CHUNKS_PER_HALF):
                 b = h * CHUNKS_PER_HALF + i
                 nc.tensor.transpose(bank[:, i, :], inv_total[:, b : b + 1].to_broadcast([P, P]), ident[:])
@@ -274,9 +274,9 @@ def tile_attend_mod_sorted_kernel(tc, xq, kT, vT, vs, offs, qoffs, out):
         weights2 = multiply_on_gpsimd(2, prob2)
         prob3 = softmax(3, score3, "u e s")
         invert_totals(0)
-        turn_pairs(weights0, w_columns(0), "bank4")
         inverse = sbuf([P, NQ], F32, "inverse")
-        spread_inverse(0)
+        spread_inverse(0, "bank5")
+        turn_pairs(weights0, w_columns(0), "bank4")
 
         v0_picked = sbuf([P, N], BF16, "q3_codes")
         nc.vector.tensor_copy(by_slot(v0_picked[:]), v0_window[:].indirect(k_list[:]))
@@ -294,7 +294,7 @@ def tile_attend_mod_sorted_kernel(tc, xq, kT, vT, vs, offs, qoffs, out):
         multiply_on_vector(3, turned3)
         invert_totals(1)
         w_half1 = quantize(w_grouped[1][:], "w1", calls=CHUNKS_PER_HALF)
-        spread_inverse(1)
+        spread_inverse(1, "bank0")
 
         v1_grouped = turn_values(1, v1_picked, "bank1")
         w_halves = [columns_of(half, 0, HALF_Q) for half in (w_half0, w_half1)]

@@ -147,7 +147,6 @@ def tile_attend_mod_sorted_kernel(tc, xq, kT, vT, vs, offs, qoffs, out):
 
         half_queries = [slice(h * HALF_Q, (h + 1) * HALF_Q) for h in range(HALVES)]
         neg_max = sbuf([P, Q_CHUNKS], F32, "neg_max")
-        inv_total = sbuf([P, Q_CHUNKS], F32, "inv_total")
         w_grouped = [sbuf([P, HALF_Q, PACK], BF16, "w_grouped%d" % h) for h in range(HALVES)]
         v1_window = sbuf([P, T], BF16, "v1_window")
 
@@ -223,10 +222,6 @@ def tile_attend_mod_sorted_kernel(tc, xq, kT, vT, vs, offs, qoffs, out):
         def columns_of(quantised, first, count):
             return [part[:, first : first + count] for part in quantised]
 
-        def invert_totals(h):
-            chunks = slice(h * CHUNKS_PER_HALF, (h + 1) * CHUNKS_PER_HALF)
-            nc.vector.reciprocal(inv_total[:, chunks], total[:, chunks])
-
         def spread_inverse(h, bank_name):
             bank = psum.tile([P, CHUNKS_PER_HALF, P], F32, name=bank_name)
             for i in range(CHUNKS_PER_HALF):
@@ -273,26 +268,26 @@ def tile_attend_mod_sorted_kernel(tc, xq, kT, vT, vs, offs, qoffs, out):
         prob2 = softmax(2, score2, "u s e")
         weights2 = multiply_on_gpsimd(2, prob2)
         prob3 = softmax(3, score3, "u e s")
-        invert_totals(0)
-        inverse = sbuf([P, NQ], F32, "inverse")
-        spread_inverse(0, "bank5")
         turn_pairs(weights0, w_columns(0), "bank4")
 
         v0_picked = sbuf([P, N], BF16, "q3_codes")
         nc.vector.tensor_copy(by_slot(v0_picked[:]), v0_window[:].indirect(k_list[:]))
+        inv_total = sbuf([P, Q_CHUNKS], F32, "v0_window")
+        nc.vector.reciprocal(inv_total[:], total[:])
         multiply_on_vector(1, turned1)
         v0_grouped = turn_values(0, v0_picked, "bank0")
         cast_piece(LAST_PIECE)
         turned3 = turn_probs(prob3, "bank7")
+        inverse = sbuf([P, NQ], F32, "inverse")
+        spread_inverse(0, "bank5")
         turn_pairs(weights2, w_columns(2), "bank4")
 
-        w_half0 = quantize(w_grouped[0][:], "w0", "prob2", calls=CHUNKS_PER_HALF)
+        w_half0 = quantize(w_grouped[0][:], "w0", calls=CHUNKS_PER_HALF)
         values0 = quantize(v0_grouped[:], "v0")
         first_chunks = [columns_of(w_half0, i * P, P) for i in range(CHUNKS_PER_HALF)]
         sums00 = weighted_sums(values0, first_chunks, "sums00", ("bank1", "bank0"))
         gather_v1_half(1, v1_window[:])
         multiply_on_vector(3, turned3)
-        invert_totals(1)
         w_half1 = quantize(w_grouped[1][:], "w1", calls=CHUNKS_PER_HALF)
         spread_inverse(1, "bank0")
 

@@ -32,7 +32,7 @@ CHUNKS_PER_HALF = Q_CHUNKS // HALVES
 HALF_Q = NQ // HALVES
 HALF_N = N // HALVES
 FIRST_TOKENS = T - HALF_N
-V_CUTS = (0, T // 4, T // 2, 3 * T // 4, FIRST_TOKENS, T)
+V_CUTS = (0, 384, 896, 1408, FIRST_TOKENS, T)
 LAST_PIECE = len(V_CUTS) - 2
 ALIGN = 256
 SIDE_BY_SIDE = "p t x -> p x t"
@@ -232,11 +232,6 @@ def tile_attend_mod_sorted_kernel(tc, xq, kT, vT, vs, offs, qoffs, out):
         def put_back(e, listed, sums, inverse_part):
             nc.vector.tensor_tensor(out_windows[e][:].indirect(listed), sums[:], inverse_part, MULT)
 
-        for c in range(LAST_PIECE):
-            cast_piece(c)
-        total = sbuf([P, Q_CHUNKS], F32, "v1_piece%d" % (LAST_PIECE - 1))
-        v1_picked = sbuf([P, N], BF16, "v1_picked")
-        gather_v1_half(0, v1_window[:, 0:FIRST_TOKENS])
 
         def last_plane(first, count):
             columns = slice(first // PER_LIST_COLUMN, (first + count) // PER_LIST_COLUMN)
@@ -244,7 +239,7 @@ def tile_attend_mod_sorted_kernel(tc, xq, kT, vT, vs, offs, qoffs, out):
 
         def place_on_gpsimd(b, picked):
             nc.vector.tensor_copy(picked, last_plane(b * P, P))
-            nc.gpsimd.tensor_scalar(q_grouped[:, b * P : (b + 1) * P, PACK - 1], picked, 1.0, 0.0, MULT, ADD)
+            nc.scalar.copy(q_grouped[:, b * P : (b + 1) * P, PACK - 1], picked)
 
         first_chunk = shared.tile([P, 2 * P], BF16, align_bytes=64, offset=0, name="first_chunk")
         place_on_gpsimd(0, first_chunk[:, 0:P])
@@ -254,7 +249,13 @@ def tile_attend_mod_sorted_kernel(tc, xq, kT, vT, vs, offs, qoffs, out):
         nc.vector.tensor_copy(last_chunk[:], last_plane(3 * P, P))
         q12 = quantize(q_grouped[:, P : 3 * P, :], "q12", scales_at=2 * P)
         nc.vector.tensor_copy(q_grouped[:, 3 * P : NQ, PACK - 1], last_chunk[:])
+        nc.vector.tensor_copy(v1_window[:, 0 : V_CUTS[1]], v1_pieces[0][:])
         q3 = quantize(q_grouped[:, 3 * P : NQ, :], "q3")
+        for c in range(1, LAST_PIECE):
+            cast_piece(c)
+        total = sbuf([P, Q_CHUNKS], F32, "v1_piece%d" % (LAST_PIECE - 1))
+        v1_picked = sbuf([P, N], BF16, "v1_picked")
+        gather_v1_half(0, v1_window[:, 0:FIRST_TOKENS])
         score1 = scores(1, q12, 0)
         score2 = scores(2, q12, P)
         prob0 = softmax(0, score0, "u s e")

@@ -250,7 +250,6 @@ def tile_attend_mod_sorted_kernel(tc, xq, kT, vT, vs, offs, qoffs, out):
         q12 = quantize(q_grouped[:, P : 3 * P, :], "q12", scales_at=2 * P)
         nc.vector.tensor_copy(q_grouped[:, 3 * P : NQ, PACK - 1], last_chunk[:])
         nc.vector.tensor_copy(v1_window[:, 0 : V_CUTS[1]], v1_pieces[0][:])
-        q3 = quantize(q_grouped[:, 3 * P : NQ, :], "q3")
         for c in range(1, LAST_PIECE):
             cast_piece(c)
         total = sbuf([P, Q_CHUNKS], F32, "v1_piece%d" % (LAST_PIECE - 1))
@@ -260,9 +259,10 @@ def tile_attend_mod_sorted_kernel(tc, xq, kT, vT, vs, offs, qoffs, out):
         score2 = scores(2, q12, P)
         prob0 = softmax(0, score0, "u s e")
         weights0 = multiply_on_gpsimd(0, prob0)
+        q3 = quantize(q_grouped[:, 3 * P : NQ, :], "q3", "q0_codes")
         prob1 = softmax(1, score1, "u e s")
         score3 = scores(3, q3, 0)
-        for count, bank_name in ((N, "bank7"),):
+        for count, bank_name in ((N, "bank7"), (N // 2, "bank5")):
             unread = psum.tile([P, count], F32, name=bank_name)
             product(unread[:], columns_of(q3, 0, P), columns_of(keys, 0, count))
         turned1 = turn_probs(prob1, "bank6")
@@ -271,7 +271,7 @@ def tile_attend_mod_sorted_kernel(tc, xq, kT, vT, vs, offs, qoffs, out):
         prob3 = softmax(3, score3, "u e s")
         turn_pairs(weights0, w_columns(0), "bank4")
 
-        v0_picked = sbuf([P, N], BF16, "q3_codes")
+        v0_picked = sbuf([P, N], BF16, "q12_codes")
         nc.vector.tensor_copy(by_slot(v0_picked[:]), v0_window[:].indirect(k_list[:]))
         inv_total = sbuf([P, Q_CHUNKS], F32, "v0_window")
         nc.vector.reciprocal(inv_total[:], total[:])

@@ -32,7 +32,7 @@ CHUNKS_PER_HALF = Q_CHUNKS // HALVES
 HALF_Q = NQ // HALVES
 HALF_N = N // HALVES
 FIRST_TOKENS = T - HALF_N
-V_CUTS = (0, 384, 896, 1408, FIRST_TOKENS, T)
+V_CUTS = (0, T // 4, T // 2, 3 * T // 4, FIRST_TOKENS, T)
 LAST_PIECE = len(V_CUTS) - 2
 ALIGN = 256
 SIDE_BY_SIDE = "p t x -> p x t"
@@ -248,9 +248,8 @@ def tile_attend_mod_sorted_kernel(tc, xq, kT, vT, vs, offs, qoffs, out):
         last_chunk = shared.tile([P, P], BF16, align_bytes=64, offset=0, name="last_chunk")
         nc.vector.tensor_copy(last_chunk[:], last_plane(3 * P, P))
         q12 = quantize(q_grouped[:, P : 3 * P, :], "q12", scales_at=2 * P)
-        nc.vector.tensor_copy(q_grouped[:, 3 * P : NQ, PACK - 1], last_chunk[:])
-        nc.vector.tensor_copy(v1_window[:, 0 : V_CUTS[1]], v1_pieces[0][:])
-        for c in range(1, LAST_PIECE):
+        nc.gpsimd.tensor_scalar(q_grouped[:, 3 * P : NQ, PACK - 1], last_chunk[:], 1.0, 0.0, MULT, ADD)
+        for c in range(LAST_PIECE):
             cast_piece(c)
         total = sbuf([P, Q_CHUNKS], F32, "v1_piece%d" % (LAST_PIECE - 1))
         v1_picked = sbuf([P, N], BF16, "v1_picked")

@@ -12,7 +12,6 @@ FP8X4 = mybir.dt.float8_e4m3fn_x4
 COPY = mybir.ActivationFunctionType.Copy
 EXP = mybir.ActivationFunctionType.Exp
 MULT = mybir.AluOpType.mult
-ADD = mybir.AluOpType.add
 MAX = mybir.AluOpType.max
 AXIS_X = mybir.AxisListType.X
 
@@ -248,7 +247,7 @@ def tile_attend_mod_sorted_kernel(tc, xq, kT, vT, vs, offs, qoffs, out):
         last_chunk = shared.tile([P, P], BF16, align_bytes=64, offset=0, name="last_chunk")
         nc.vector.tensor_copy(last_chunk[:], last_plane(3 * P, P))
         q12 = quantize(q_grouped[:, P : 3 * P, :], "q12", scales_at=2 * P)
-        nc.gpsimd.tensor_scalar(q_grouped[:, 3 * P : NQ, PACK - 1], last_chunk[:], 1.0, 0.0, MULT, ADD)
+        nc.gpsimd.tensor_copy(q_grouped[:, 3 * P : NQ, PACK - 1], last_chunk[:])
         for c in range(LAST_PIECE):
             cast_piece(c)
         total = sbuf([P, Q_CHUNKS], F32, "v1_piece%d" % (LAST_PIECE - 1))

@@ -59,7 +59,9 @@ def tile_attend_mod_sorted_kernel(tc, xq, kT, vT, vs, offs, qoffs, out):
         q_list = sbuf([P, NQ // PER_LIST_COLUMN], U16, "q_list")
         k_rows = kT.rearrange("(p t) c -> p t c", t=PACK)
         q_rows = xq.rearrange("(p t) c -> p t c", t=PACK)
-        k_planes = [load(k_rows[:, 0, :], "k_plane0")]
+        k_planes = [sbuf([P, T], F32, "k_plane0")]
+        nc.sync.dma_start(k_planes[0][:, 0 : T // 2], k_rows[:, 0, 0 : T // 2])
+        nc.scalar.dma_start(k_planes[0][:, T // 2 : T], k_rows[:, 0, T // 2 : T])
         nc.sync.dma_start(k_list[:], offs)
         k_planes.append(load(k_rows[:, 1, :], "k_plane1"))
 

@@ -78,12 +78,7 @@ def tile_attend_mod_sorted_kernel(tc, xq, kT, vT, vs, offs, qoffs, out):
         nc.sync.dma_start(q_list[:], qoffs)
         q_planes = [load(q_rows[:, t, :], "q_plane%d" % t) for t in range(PACK)]
 
-        def load_piece(c):
-            return load(vT[P:DV, V_CUTS[c] : V_CUTS[c + 1]], "v1_piece%d" % c)
-
-        v1_pieces = [load_piece(c) for c in range(LAST_PIECE)]
-        v0_window = load(vT[0:P, :], "v0_window")
-        v1_pieces.append(load_piece(LAST_PIECE))
+        v_windows = [load(vT[0:P, :], "v_window0")]
 
         def half_of(listed, h):
             columns = HALF_N // PER_LIST_COLUMN
@@ -146,10 +141,12 @@ def tile_attend_mod_sorted_kernel(tc, xq, kT, vT, vs, offs, qoffs, out):
         for t in range(PACK - 1):
             nc.vector.tensor_copy(q_grouped[:, :, t], q_planes[t][:].indirect(q_list[:]))
 
+        v_windows.append(sbuf([P, T], F32, "q_plane%d" % (PACK - 2)))
+        nc.scalar.dma_start(v_windows[1][:], vT[P:DV, :])
+
         half_queries = [slice(h * HALF_Q, (h + 1) * HALF_Q) for h in range(HALVES)]
         neg_max = sbuf([P, Q_CHUNKS], F32, "neg_max")
         w_grouped = [sbuf([P, HALF_Q, PACK], BF16, "w_grouped%d" % h) for h in range(HALVES)]
-        v1_window = sbuf([P, T], BF16, "v1_window")
 
         def scores(b, queries, first):
             bank = psum.tile([P, N], F32, name="bank%d" % b)
@@ -199,12 +196,10 @@ def tile_attend_mod_sorted_kernel(tc, xq, kT, vT, vs, offs, qoffs, out):
                 MULT,
             )
 
-        def cast_piece(c):
-            nc.scalar.activation(v1_window[:, V_CUTS[c] : V_CUTS[c + 1]], v1_pieces[c][:], COPY)
-
-        def gather_v1_half(h, window):
-            partitions_to_be = slice(h * P // HALVES, (h + 1) * P // HALVES)
-            nc.scalar.activation(by_slot(v1_picked[:])[:, partitions_to_be], window.indirect(half_of(k_list, h)), COPY)
+        def gather_values(e, name):
+            picked = sbuf([P, N], BF16, name)
+            nc.vector.tensor_copy(by_slot(picked[:]), v_windows[e][:].indirect(k_list[:]))
+            return picked
 
         def turn_values(e, picked, bank_name):
             grouped = sbuf([P, P, PACK], BF16, "v_grouped%d" % e)
@@ -249,17 +244,13 @@ def tile_attend_mod_sorted_kernel(tc, xq, kT, vT, vs, offs, qoffs, out):
         last_chunk = shared.tile([P, P], BF16, align_bytes=64, offset=0, name="last_chunk")
         nc.vector.tensor_copy(last_chunk[:], last_plane(3 * P, P))
         q12 = quantize(q_grouped[:, P : 3 * P, :], "q12", scales_at=2 * P)
-        nc.gpsimd.tensor_copy(q_grouped[:, 3 * P : NQ, PACK - 1], last_chunk[:])
-        for c in range(LAST_PIECE):
-            cast_piece(c)
-        total = sbuf([P, Q_CHUNKS], F32, "v1_piece%d" % (LAST_PIECE - 1))
-        v1_picked = sbuf([P, N], BF16, "v1_picked")
-        gather_v1_half(0, v1_window[:, 0:FIRST_TOKENS])
+        nc.scalar.copy(q_grouped[:, 3 * P : NQ, PACK - 1], last_chunk[:])
+        total = sbuf([P, Q_CHUNKS], F32, "total")
         score1 = scores(1, q12, 0)
         score2 = scores(2, q12, P)
         prob0 = softmax(0, score0, "u s e")
         weights0 = multiply_on_gpsimd(0, prob0)
-        q3 = quantize(q_grouped[:, 3 * P : NQ, :], "q3", "q0_codes")
+        q3 = quantize(q_grouped[:, 3 * P : NQ, :], "q3")
         prob1 = softmax(1, score1, "u e s")
         score3 = scores(3, q3, 0)
         for count, bank_name in ((N, "bank7"), (N // 2, "bank5")):
@@ -271,13 +262,12 @@ def tile_attend_mod_sorted_kernel(tc, xq, kT, vT, vs, offs, qoffs, out):
         prob3 = softmax(3, score3, "u e s")
         turn_pairs(weights0, w_columns(0), "bank4")
 
-        v0_picked = sbuf([P, N], BF16, "q12_codes")
-        nc.vector.tensor_copy(by_slot(v0_picked[:]), v0_window[:].indirect(k_list[:]))
-        inv_total = sbuf([P, Q_CHUNKS], F32, "v0_window")
-        nc.vector.reciprocal(inv_total[:], total[:])
+        v0_picked = gather_values(0, "v0_picked")
+        v1_picked = gather_values(1, "v1_picked")
         multiply_on_vector(1, turned1)
         v0_grouped = turn_values(0, v0_picked, "bank0")
-        cast_piece(LAST_PIECE)
+        inv_total = sbuf([P, Q_CHUNKS], F32, "inv_total")
+        nc.vector.reciprocal(inv_total[:], total[:])
         turned3 = turn_probs(prob3, "bank7")
         inverse = sbuf([P, NQ], F32, "inverse")
         spread_inverse(0, "bank5")
@@ -287,7 +277,6 @@ def tile_attend_mod_sorted_kernel(tc, xq, kT, vT, vs, offs, qoffs, out):
         values0 = quantize(v0_grouped[:], "v0")
         first_chunks = [columns_of(w_half0, i * P, P) for i in range(CHUNKS_PER_HALF)]
         sums00 = weighted_sums(values0, first_chunks, "sums00", ("bank1", "bank0"))
-        gather_v1_half(1, v1_window[:])
         multiply_on_vector(3, turned3)
         w_half1 = quantize(w_grouped[1][:], "w1", calls=CHUNKS_PER_HALF)
         spread_inverse(1, "bank0")

@@ -9,7 +9,6 @@ U32 = mybir.dt.uint32
 U16 = mybir.dt.uint16
 U8 = mybir.dt.uint8
 FP8X4 = mybir.dt.float8_e4m3fn_x4
-COPY = mybir.ActivationFunctionType.Copy
 EXP = mybir.ActivationFunctionType.Exp
 MULT = mybir.AluOpType.mult
 MAX = mybir.AluOpType.max
@@ -24,17 +23,9 @@ DV = 256
 N = 512
 NQ = 512
 PER_LIST_COLUMN = 16
-Q_CHUNKS = NQ // P
-V_CHUNKS = DV // P
-HALVES = 2
-CHUNKS_PER_HALF = Q_CHUNKS // HALVES
-HALF_Q = NQ // HALVES
-HALF_N = N // HALVES
-FIRST_TOKENS = T - HALF_N
-V_CUTS = (0, T // 4, T // 2, 3 * T // 4, FIRST_TOKENS, T)
-LAST_PIECE = len(V_CUTS) - 2
+CHUNKS = NQ // P
+HALF = NQ // 2
 ALIGN = 256
-SIDE_BY_SIDE = "p t x -> p x t"
 
 FLOPS = 2 * NQ * N * D + 2 * NQ * N * DV
 BYTES = 4 * (2 * D * T + DV * T + T + DV * T) + 2 * P * (N + NQ) // PER_LIST_COLUMN
@@ -55,6 +46,47 @@ def tile_attend_mod_sorted_kernel(tc, xq, kT, vT, vs, offs, qoffs, out):
             nc.sync.dma_start(tile[:], rows)
             return tile
 
+        def by_slot(paired):
+            return paired.rearrange("p (u s e) -> p s u e", u=PAIR, e=PAIR)
+
+        def listed(tile, first, count):
+            return tile[:, first // PER_LIST_COLUMN : (first + count) // PER_LIST_COLUMN]
+
+        def quantize(grouped, codes, scales):
+            nc.vector.quantize_mx(out=codes.bitcast(FP8X4), scales=scales, in_=grouped.rearrange("p c t -> p (c t)"))
+            return codes, scales
+
+        def operand(width, name, codes_name=None):
+            return sbuf([P, width], U32, codes_name or name + "_codes"), sbuf([P, width], U8, name + "_scales")
+
+        def part(pair, first, count):
+            return [tile[:, first : first + count] for tile in pair]
+
+        def product(bank_name, stationary, moving):
+            bank = psum.tile([P, moving[0].shape[1]], F32, name=bank_name)
+            nc.tensor.matmul_mx(
+                out=bank[:],
+                lhsT=stationary[0].bitcast(FP8X4),
+                lhsT_scale=stationary[1],
+                rhs=moving[0].bitcast(FP8X4),
+                rhs_scale=moving[1],
+                start=True,
+                stop=True,
+            )
+            return bank
+
+        def turn(paired, name, bank_name):
+            grouped = sbuf([P, P, PACK], BF16, name)
+            words = paired[:].bitcast(F32)
+            bank = psum.tile([P, PAIR, P], F32, name=bank_name)
+            for u in range(PAIR):
+                nc.tensor.transpose(bank[:, u, :], words[:, u * P : (u + 1) * P], ident[:])
+            nc.scalar.copy(
+                grouped[:].rearrange("p x t -> p (x t)").bitcast(F32).rearrange("p (x u) -> p x u", u=PAIR),
+                bank[:].rearrange("p u x -> p x u"),
+            )
+            return grouped
+
         k_list = sbuf([P, N // PER_LIST_COLUMN], U16, "k_list")
         q_list = sbuf([P, NQ // PER_LIST_COLUMN], U16, "q_list")
         k_rows = kT.rearrange("(p t) c -> p t c", t=PACK)
@@ -64,59 +96,21 @@ def tile_attend_mod_sorted_kernel(tc, xq, kT, vT, vs, offs, qoffs, out):
         nc.scalar.dma_start(k_planes[0][:, T // 2 : T], k_rows[:, 0, T // 2 : T])
         nc.sync.dma_start(k_list[:], offs)
         k_planes.append(load(k_rows[:, 1, :], "k_plane1"))
-
         vs_window = sbuf([P, T], F32, "vs_window")
         nc.vector.memset(vs_window[:], 0.0)
         ident = sbuf([P, P], F32, "ident")
         make_identity(nc, ident[:])
-        out_windows = [sbuf([P, T], F32, "out_window%d" % e) for e in range(V_CHUNKS)]
+        out_windows = [sbuf([P, T], F32, "out_window%d" % e) for e in range(DV // P)]
         for window in out_windows:
             nc.gpsimd.memset(window[:], 0.0)
-
         nc.sync.dma_start(vs_window[0:1, :], vs[0:1, :])
         k_planes.extend([load(k_rows[:, t, :], "k_plane%d" % t) for t in range(2, PACK)])
         nc.sync.dma_start(q_list[:], qoffs)
         q_planes = [load(q_rows[:, t, :], "q_plane%d" % t) for t in range(PACK)]
-
-        v_windows = [load(vT[0:P, :], "v_window0")]
-
-        def half_of(listed, h):
-            columns = HALF_N // PER_LIST_COLUMN
-            return listed[:, h * columns : (h + 1) * columns]
-
-        def by_slot(paired):
-            return paired.rearrange("p (u s e) -> p s u e", u=PAIR, e=PAIR)
-
-        def quantize(grouped, name, codes_name=None, calls=1, scales_at=None):
-            width = grouped.shape[1]
-            codes = sbuf([P, width], U32, codes_name or name + "_codes")
-            if scales_at is None:
-                scales = sbuf([P, width], U8, name + "_scales")
-            else:
-                scales = shared.tile([P, width], U8, align_bytes=64, offset=scales_at, name=name + "_scales")
-            for i in range(calls):
-                columns = slice(i * width // calls, (i + 1) * width // calls)
-                nc.vector.quantize_mx(
-                    out=codes[:, columns].bitcast(FP8X4),
-                    scales=scales[:, columns],
-                    in_=grouped[:, columns, :].rearrange("p c t -> p (c t)"),
-                )
-            return codes, scales
-
-        def product(result, stationary, moving):
-            nc.tensor.matmul_mx(
-                out=result,
-                lhsT=stationary[0].bitcast(FP8X4),
-                lhsT_scale=stationary[1],
-                rhs=moving[0].bitcast(FP8X4),
-                rhs_scale=moving[1],
-                start=True,
-                stop=True,
-            )
+        v_windows = [load(vT[e * P : (e + 1) * P, :], "v_window%d" % e) for e in range(DV // P)]
 
         k_grouped = sbuf([P, N, PACK], BF16, "k_grouped")
         nc.vector.tensor_copy(by_slot(k_grouped[:, :, 0]), k_planes[0][:].indirect(k_list[:]))
-
         vs_picked = sbuf([P, N], F32, "vs_picked")
         nc.vector.tensor_copy(vs_picked[:], vs_window[:].indirect(k_list[:]))
         column_bank = psum.tile([P, PACK, P], F32, name="bank4")
@@ -127,72 +121,57 @@ def tile_attend_mod_sorted_kernel(tc, xq, kT, vT, vs, offs, qoffs, out):
         row_bank = psum.tile([P, PACK, P], F32, name="bank5")
         for t in range(PACK):
             nc.tensor.transpose(row_bank[:, t, :], vs_column[:, t : t + 1].to_broadcast([P, P]), ident[:])
+        row_view = row_bank[:].rearrange("p (u e) s -> p u s e", e=PAIR)
         vs_row = sbuf([P, N], F32, "vs_row")
-        nc.scalar.copy(
-            vs_row[:].rearrange("p (u s e) -> p u s e", u=PAIR, e=PAIR),
-            row_bank[:].rearrange("p (u e) s -> p u s e", e=PAIR),
-        )
-
+        nc.scalar.copy(vs_row[:].rearrange("p (u s e) -> p u s e", u=PAIR, e=PAIR), row_view)
         for t in range(1, PACK):
             nc.vector.tensor_copy(by_slot(k_grouped[:, :, t]), k_planes[t][:].indirect(k_list[:]))
-        keys = quantize(k_grouped[:], "k")
+        keys = part(operand(N, "k"), 0, N)
+        quantize(k_grouped[:], *keys)
 
         q_grouped = sbuf([P, NQ, PACK], BF16, "q_grouped")
         for t in range(PACK - 1):
             nc.vector.tensor_copy(q_grouped[:, :, t], q_planes[t][:].indirect(q_list[:]))
+        last = q_planes[PACK - 1]
+        first_chunk = shared.tile([P, 2 * P], BF16, align_bytes=64, offset=0, name="first_chunk")
+        nc.vector.tensor_copy(first_chunk[:, 0:P], last[:].indirect(listed(q_list, 0, P)))
+        nc.scalar.copy(q_grouped[:, 0:P, PACK - 1], first_chunk[:, 0:P])
+        nc.vector.tensor_copy(q_grouped[:, P : 3 * P, PACK - 1], last[:].indirect(listed(q_list, P, 2 * P)))
+        scores = [product("bank0", quantize(q_grouped[:, 0:P, :], *part(operand(P, "q0"), 0, P)), keys)]
+        last_chunk = shared.tile([P, P], BF16, align_bytes=64, offset=0, name="last_chunk")
+        nc.vector.tensor_copy(last_chunk[:], last[:].indirect(listed(q_list, 3 * P, P)))
+        q12 = (
+            sbuf([P, 2 * P], U32, "q12_codes"),
+            shared.tile([P, 2 * P], U8, align_bytes=64, offset=2 * P, name="q12_scales"),
+        )
+        quantize(q_grouped[:, P : 3 * P, :], *part(q12, 0, 2 * P))
+        nc.gpsimd.tensor_copy(q_grouped[:, 3 * P : NQ, PACK - 1], last_chunk[:])
+        scores += [product("bank%d" % b, part(q12, (b - 1) * P, P), keys) for b in (1, 2)]
+        q3 = quantize(q_grouped[:, 3 * P : NQ, :], *part(operand(P, "q3", "q0_codes"), 0, P))
+        scores.append(product("bank3", q3, keys))
+        product("bank7", q3, keys)
+        product("bank6", q3, [half[:, 0:HALF] for half in keys])
 
-        v_windows.append(sbuf([P, T], F32, "q_plane%d" % (PACK - 2)))
-        nc.scalar.dma_start(v_windows[1][:], vT[P:DV, :])
-
-        half_queries = [slice(h * HALF_Q, (h + 1) * HALF_Q) for h in range(HALVES)]
-        neg_max = sbuf([P, Q_CHUNKS], F32, "neg_max")
-        w_grouped = [sbuf([P, HALF_Q, PACK], BF16, "w_grouped%d" % h) for h in range(HALVES)]
-
-        def scores(b, queries, first):
-            bank = psum.tile([P, N], F32, name="bank%d" % b)
-            product(bank[:], columns_of(queries, first, P), columns_of(keys, 0, N))
-            return bank
-
-        def softmax(b, bank, order):
-            nc.vector.tensor_reduce(neg_max[:, b : b + 1], bank[:], AXIS_X, MAX, negate=True)
-            prob = sbuf([P, N], F32, "prob%d" % b)
+        neg_max = sbuf([P, CHUNKS], F32, "neg_max")
+        total = sbuf([P, CHUNKS], F32, "total")
+        probs = []
+        weights = [None] * CHUNKS
+        for b in range(CHUNKS):
+            nc.vector.tensor_reduce(neg_max[:, b : b + 1], scores[b][:], AXIS_X, MAX, negate=True)
+            probs.append(sbuf([P, N], F32, "prob%d" % b))
             nc.scalar.activation(
-                prob[:].rearrange("p (%s) -> p %s" % (order, order), u=PAIR, e=PAIR),
-                bank[:].rearrange("p (u s e) -> p %s" % order, u=PAIR, e=PAIR),
-                EXP,
-                bias=neg_max[:, b : b + 1],
-                accum_out=total[:, b : b + 1],
+                probs[b][:], scores[b][:], EXP, bias=neg_max[:, b : b + 1], accum_out=total[:, b : b + 1]
             )
-            return prob
+            if b % 2 == 0:
+                weights[b] = sbuf([P, N], BF16, "weights%d" % b)
+                nc.gpsimd.tensor_tensor(weights[b][:], probs[b][:], vs_row[:], MULT)
 
-        def w_columns(b):
-            h, i = divmod(b, CHUNKS_PER_HALF)
-            return w_grouped[h][:, i * P : (i + 1) * P, :]
-
-        def turn_pairs(paired, grouped, bank_name):
-            words = paired[:].bitcast(F32)
-            bank = psum.tile([P, PAIR, P], F32, name=bank_name)
-            for u in range(PAIR):
-                nc.tensor.transpose(bank[:, u, :], words[:, u * P : (u + 1) * P], ident[:])
-            grouped_words = grouped.rearrange("p x t -> p (x t)").bitcast(F32).rearrange("p (x u) -> p x u", u=PAIR)
-            nc.scalar.copy(grouped_words, bank[:].rearrange(SIDE_BY_SIDE))
-
-        def multiply_on_gpsimd(b, prob):
-            weights = sbuf([P, N], BF16, "weights%d" % b)
-            nc.gpsimd.tensor_tensor(weights[:], prob[:], vs_row[:], MULT)
-            return weights
-
-        def turn_probs(prob, bank_name):
-            bank = psum.tile([P, PACK, P], F32, name=bank_name)
-            for t in range(PACK):
-                nc.tensor.transpose(bank[:, t, :], prob[:, t * P : (t + 1) * P], ident[:])
-            return bank
-
-        def multiply_on_vector(b, bank):
+        def multiply_on_vector(b):
+            weights[b] = sbuf([P, N], BF16, "weights%d" % b)
             nc.vector.tensor_tensor(
-                w_columns(b),
-                bank[:].rearrange(SIDE_BY_SIDE),
-                vs_column[:].unsqueeze(1).to_broadcast([P, P, PACK]),
+                weights[b][:].rearrange("p (u s e) -> p u s e", u=PAIR, e=PAIR),
+                row_view,
+                probs[b][:].rearrange("p (u s e) -> p u s e", u=PAIR, e=PAIR),
                 MULT,
             )
 
@@ -201,93 +180,52 @@ def tile_attend_mod_sorted_kernel(tc, xq, kT, vT, vs, offs, qoffs, out):
             nc.vector.tensor_copy(by_slot(picked[:]), v_windows[e][:].indirect(k_list[:]))
             return picked
 
-        def turn_values(e, picked, bank_name):
-            grouped = sbuf([P, P, PACK], BF16, "v_grouped%d" % e)
-            turn_pairs(picked, grouped[:], bank_name)
-            return grouped
+        def spread(h, bank_name):
+            bank = psum.tile([P, 2, P], F32, name=bank_name)
+            for i in range(2):
+                nc.tensor.transpose(bank[:, i, :], inv_total[:, 2 * h + i : 2 * h + i + 1].to_broadcast([P, P]), ident[:])
+            nc.scalar.copy(inverse[:, h * HALF : (h + 1) * HALF], bank[:].rearrange("p b q -> p (b q)"))
 
-        def weighted_sums(values, runs, name, bank_names):
+        def sums_of(values, runs, name, bank_names):
             width = runs[0][0].shape[1]
             sums = sbuf([P, len(runs) * width], F32, name)
-            for i, (weights, bank_name) in enumerate(zip(runs, bank_names)):
-                bank = psum.tile([P, width], F32, name=bank_name)
-                product(bank[:], [part[:] for part in values], weights)
-                nc.scalar.copy(sums[:, i * width : (i + 1) * width], bank[:])
+            for i, bank_name in enumerate(bank_names):
+                nc.scalar.copy(sums[:, i * width : (i + 1) * width], product(bank_name, values, runs[i])[:])
             return sums
 
-        def columns_of(quantised, first, count):
-            return [part[:, first : first + count] for part in quantised]
+        def put_back(e, first, count, sums):
+            nc.vector.tensor_tensor(
+                out_windows[e][:].indirect(listed(q_list, first, count)), sums[:], inverse[:, first : first + count], MULT
+            )
 
-        def spread_inverse(h, bank_name):
-            bank = psum.tile([P, CHUNKS_PER_HALF, P], F32, name=bank_name)
-            for i in range(CHUNKS_PER_HALF):
-                b = h * CHUNKS_PER_HALF + i
-                nc.tensor.transpose(bank[:, i, :], inv_total[:, b : b + 1].to_broadcast([P, P]), ident[:])
-            nc.scalar.copy(inverse[:, half_queries[h]], bank[:].rearrange("p b q -> p (b q)"))
-
-        def put_back(e, listed, sums, inverse_part):
-            nc.vector.tensor_tensor(out_windows[e][:].indirect(listed), sums[:], inverse_part, MULT)
-
-
-        def last_plane(first, count):
-            columns = slice(first // PER_LIST_COLUMN, (first + count) // PER_LIST_COLUMN)
-            return q_planes[PACK - 1][:].indirect(q_list[:, columns])
-
-        def place_on_gpsimd(b, picked):
-            nc.vector.tensor_copy(picked, last_plane(b * P, P))
-            nc.scalar.copy(q_grouped[:, b * P : (b + 1) * P, PACK - 1], picked)
-
-        first_chunk = shared.tile([P, 2 * P], BF16, align_bytes=64, offset=0, name="first_chunk")
-        place_on_gpsimd(0, first_chunk[:, 0:P])
-        nc.vector.tensor_copy(q_grouped[:, P : 3 * P, PACK - 1], last_plane(P, 2 * P))
-        score0 = scores(0, quantize(q_grouped[:, 0:P, :], "q0"), 0)
-        last_chunk = shared.tile([P, P], BF16, align_bytes=64, offset=0, name="last_chunk")
-        nc.vector.tensor_copy(last_chunk[:], last_plane(3 * P, P))
-        q12 = quantize(q_grouped[:, P : 3 * P, :], "q12", scales_at=2 * P)
-        nc.scalar.copy(q_grouped[:, 3 * P : NQ, PACK - 1], last_chunk[:])
-        total = sbuf([P, Q_CHUNKS], F32, "total")
-        score1 = scores(1, q12, 0)
-        score2 = scores(2, q12, P)
-        prob0 = softmax(0, score0, "u s e")
-        weights0 = multiply_on_gpsimd(0, prob0)
-        q3 = quantize(q_grouped[:, 3 * P : NQ, :], "q3")
-        prob1 = softmax(1, score1, "u e s")
-        score3 = scores(3, q3, 0)
-        for count, bank_name in ((N, "bank7"), (N // 2, "bank5")):
-            unread = psum.tile([P, count], F32, name=bank_name)
-            product(unread[:], columns_of(q3, 0, P), columns_of(keys, 0, count))
-        turned1 = turn_probs(prob1, "bank6")
-        prob2 = softmax(2, score2, "u s e")
-        weights2 = multiply_on_gpsimd(2, prob2)
-        prob3 = softmax(3, score3, "u e s")
-        turn_pairs(weights0, w_columns(0), "bank4")
-
-        v0_picked = gather_values(0, "v0_picked")
-        v1_picked = gather_values(1, "v1_picked")
-        multiply_on_vector(1, turned1)
-        v0_grouped = turn_values(0, v0_picked, "bank0")
-        inv_total = sbuf([P, Q_CHUNKS], F32, "inv_total")
+        picked0 = gather_values(0, "picked0")
+        multiply_on_vector(1)
+        multiply_on_vector(3)
+        inv_total = sbuf([P, CHUNKS], F32, "inv_total")
         nc.vector.reciprocal(inv_total[:], total[:])
-        turned3 = turn_probs(prob3, "bank7")
+        w0 = turn(weights[0], "w0", "bank4")
+        v0 = turn(picked0, "v0", "bank0")
+        w1 = turn(weights[1], "w1", "bank6")
         inverse = sbuf([P, NQ], F32, "inverse")
-        spread_inverse(0, "bank5")
-        turn_pairs(weights2, w_columns(2), "bank4")
+        spread(0, "bank1")
+        w3 = turn(weights[3], "w3", "bank7")
+        w2 = turn(weights[2], "w2", "bank4")
 
-        w_half0 = quantize(w_grouped[0][:], "w0", calls=CHUNKS_PER_HALF)
-        values0 = quantize(v0_grouped[:], "v0")
-        first_chunks = [columns_of(w_half0, i * P, P) for i in range(CHUNKS_PER_HALF)]
-        sums00 = weighted_sums(values0, first_chunks, "sums00", ("bank1", "bank0"))
-        multiply_on_vector(3, turned3)
-        w_half1 = quantize(w_grouped[1][:], "w1", calls=CHUNKS_PER_HALF)
-        spread_inverse(1, "bank0")
-
-        v1_grouped = turn_values(1, v1_picked, "bank1")
-        w_halves = [columns_of(half, 0, HALF_Q) for half in (w_half0, w_half1)]
-        sums01 = weighted_sums(values0, w_halves[1:], "v1_picked", ("bank2",))
-        put_back(0, half_of(q_list, 0), sums00, inverse[:, half_queries[0]])
-        values1 = quantize(v1_grouped[:], "v1")
-        sums1 = weighted_sums(values1, w_halves, "sums1", ("bank3", "bank6"))
-        put_back(0, half_of(q_list, 1), sums01, inverse[:, half_queries[1]])
+        halves = [operand(HALF, "w_half0", "prob2"), operand(HALF, "w_half1")]
+        quantize(w0[:], *part(halves[0], 0, P))
+        values0 = quantize(v0[:], *part(operand(P, "v0"), 0, P))
+        quantize(w1[:], *part(halves[0], P, P))
+        sums00 = sums_of(values0, [part(halves[0], i * P, P) for i in range(2)], "sums00", ("bank2", "bank3"))
+        picked1 = gather_values(1, "picked1")
+        quantize(w3[:], *part(halves[1], P, P))
+        quantize(w2[:], *part(halves[1], 0, P))
+        spread(1, "bank0")
+        v1 = turn(picked1, "v1", "bank2")
+        sums01 = sums_of(values0, [part(halves[1], 0, HALF)], "picked1", ("bank1",))
+        put_back(0, 0, HALF, sums00)
+        values1 = quantize(v1[:], *part(operand(P, "v1"), 0, P))
+        sums1 = sums_of(values1, [part(half, 0, HALF) for half in halves], "sums1", ("bank3", "bank6"))
+        put_back(0, HALF, HALF, sums01)
         nc.sync.dma_start(out[0:P, :], out_windows[0][:])
-        put_back(1, q_list[:], sums1, inverse[:])
+        put_back(1, 0, NQ, sums1)
         nc.sync.dma_start(out[P:DV, :], out_windows[1][:])

@@ -159,9 +159,18 @@ def tile_attend_mod_sorted_kernel(tc, xq, kT, vT, vs, offs, qoffs, out):
         for b in range(CHUNKS):
             nc.vector.tensor_reduce(neg_max[:, b : b + 1], scores[b][:], AXIS_X, MAX, negate=True)
             probs.append(sbuf([P, N], F32, "prob%d" % b))
+            order = "u e s" if b == 1 else "u s e"
             nc.scalar.activation(
-                probs[b][:], scores[b][:], EXP, bias=neg_max[:, b : b + 1], accum_out=total[:, b : b + 1]
+                probs[b][:].rearrange("p (%s) -> p %s" % (order, order), u=PAIR, e=PAIR),
+                scores[b][:].rearrange("p (u s e) -> p %s" % order, u=PAIR, e=PAIR),
+                EXP,
+                bias=neg_max[:, b : b + 1],
+                accum_out=total[:, b : b + 1],
             )
+            if b == 1:
+                turned1 = psum.tile([P, PACK, P], F32, name="bank6")
+                for t in range(PACK):
+                    nc.tensor.transpose(turned1[:, t, :], probs[b][:, t * P : (t + 1) * P], ident[:])
             if b % 2 == 0:
                 weights[b] = sbuf([P, N], BF16, "weights%d" % b)
                 nc.gpsimd.tensor_tensor(weights[b][:], probs[b][:], vs_row[:], MULT)
@@ -199,29 +208,31 @@ def tile_attend_mod_sorted_kernel(tc, xq, kT, vT, vs, offs, qoffs, out):
             )
 
         picked0 = gather_values(0, "picked0")
-        multiply_on_vector(1)
-        multiply_on_vector(3)
+        w1 = sbuf([P, P, PACK], BF16, "w1")
+        nc.vector.tensor_tensor(
+            w1[:], turned1[:].rearrange("p t x -> p x t"), vs_column[:].unsqueeze(1).to_broadcast([P, P, PACK]), MULT
+        )
         inv_total = sbuf([P, CHUNKS], F32, "inv_total")
         nc.vector.reciprocal(inv_total[:], total[:])
-        w0 = turn(weights[0], "w0", "bank4")
+        multiply_on_vector(3)
+        w0 = turn(weights[0], "w0", "bank1")
         v0 = turn(picked0, "v0", "bank0")
-        w1 = turn(weights[1], "w1", "bank6")
         inverse = sbuf([P, NQ], F32, "inverse")
-        spread(0, "bank1")
+        spread(0, "bank4")
         w3 = turn(weights[3], "w3", "bank7")
-        w2 = turn(weights[2], "w2", "bank4")
+        w2 = turn(weights[2], "w2", "bank1")
 
-        halves = [operand(HALF, "w_half0", "prob2"), operand(HALF, "w_half1")]
+        halves = [operand(HALF, "w_half0", "prob3"), operand(HALF, "w_half1")]
         quantize(w0[:], *part(halves[0], 0, P))
         values0 = quantize(v0[:], *part(operand(P, "v0"), 0, P))
         quantize(w1[:], *part(halves[0], P, P))
         sums00 = sums_of(values0, [part(halves[0], i * P, P) for i in range(2)], "sums00", ("bank2", "bank3"))
-        picked1 = gather_values(1, "picked1")
+        picked1 = gather_values(1, "v0")
         quantize(w3[:], *part(halves[1], P, P))
         quantize(w2[:], *part(halves[1], 0, P))
         spread(1, "bank0")
         v1 = turn(picked1, "v1", "bank2")
-        sums01 = sums_of(values0, [part(halves[1], 0, HALF)], "picked1", ("bank1",))
+        sums01 = sums_of(values0, [part(halves[1], 0, HALF)], "v0", ("bank4",))
         put_back(0, 0, HALF, sums00)
         values1 = quantize(v1[:], *part(operand(P, "v1"), 0, P))
         sums1 = sums_of(values1, [part(half, 0, HALF) for half in halves], "sums1", ("bank3", "bank6"))

@@ -121,9 +121,11 @@ def tile_attend_mod_sorted_kernel(tc, xq, kT, vT, vs, offs, qoffs, out):
         row_bank = psum.tile([P, PACK, P], F32, name="bank5")
         for t in range(PACK):
             nc.tensor.transpose(row_bank[:, t, :], vs_column[:, t : t + 1].to_broadcast([P, P]), ident[:])
-        row_view = row_bank[:].rearrange("p (u e) s -> p u s e", e=PAIR)
         vs_row = sbuf([P, N], F32, "vs_row")
-        nc.scalar.copy(vs_row[:].rearrange("p (u s e) -> p u s e", u=PAIR, e=PAIR), row_view)
+        nc.scalar.copy(
+            vs_row[:].rearrange("p (u s e) -> p u s e", u=PAIR, e=PAIR),
+            row_bank[:].rearrange("p (u e) s -> p u s e", e=PAIR),
+        )
         for t in range(1, PACK):
             nc.vector.tensor_copy(by_slot(k_grouped[:, :, t]), k_planes[t][:].indirect(k_list[:]))
         keys = part(operand(N, "k"), 0, N)
@@ -152,6 +154,12 @@ def tile_attend_mod_sorted_kernel(tc, xq, kT, vT, vs, offs, qoffs, out):
         product("bank7", q3, keys)
         product("bank6", q3, [half[:, 0:HALF] for half in keys])
 
+        def turn_probs(b, bank_name):
+            bank = psum.tile([P, PACK, P], F32, name=bank_name)
+            for t in range(PACK):
+                nc.tensor.transpose(bank[:, t, :], probs[b][:, t * P : (t + 1) * P], ident[:])
+            return bank
+
         neg_max = sbuf([P, CHUNKS], F32, "neg_max")
         total = sbuf([P, CHUNKS], F32, "total")
         probs = []
@@ -159,7 +167,7 @@ def tile_attend_mod_sorted_kernel(tc, xq, kT, vT, vs, offs, qoffs, out):
         for b in range(CHUNKS):
             nc.vector.tensor_reduce(neg_max[:, b : b + 1], scores[b][:], AXIS_X, MAX, negate=True)
             probs.append(sbuf([P, N], F32, "prob%d" % b))
-            order = "u e s" if b == 1 else "u s e"
+            order = "u e s" if b % 2 else "u s e"
             nc.scalar.activation(
                 probs[b][:].rearrange("p (%s) -> p %s" % (order, order), u=PAIR, e=PAIR),
                 scores[b][:].rearrange("p (u s e) -> p %s" % order, u=PAIR, e=PAIR),
@@ -168,21 +176,17 @@ def tile_attend_mod_sorted_kernel(tc, xq, kT, vT, vs, offs, qoffs, out):
                 accum_out=total[:, b : b + 1],
             )
             if b == 1:
-                turned1 = psum.tile([P, PACK, P], F32, name="bank6")
-                for t in range(PACK):
-                    nc.tensor.transpose(turned1[:, t, :], probs[b][:, t * P : (t + 1) * P], ident[:])
+                turned1 = turn_probs(b, "bank6")
             if b % 2 == 0:
                 weights[b] = sbuf([P, N], BF16, "weights%d" % b)
                 nc.gpsimd.tensor_tensor(weights[b][:], probs[b][:], vs_row[:], MULT)
 
-        def multiply_on_vector(b):
-            weights[b] = sbuf([P, N], BF16, "weights%d" % b)
+        def multiply_on_vector(b, bank):
+            grouped = sbuf([P, P, PACK], BF16, "w%d" % b)
             nc.vector.tensor_tensor(
-                weights[b][:].rearrange("p (u s e) -> p u s e", u=PAIR, e=PAIR),
-                row_view,
-                probs[b][:].rearrange("p (u s e) -> p u s e", u=PAIR, e=PAIR),
-                MULT,
+                grouped[:], bank[:].rearrange("p t x -> p x t"), vs_column[:].unsqueeze(1).to_broadcast([P, P, PACK]), MULT
             )
+            return grouped
 
         def gather_values(e, name):
             picked = sbuf([P, N], BF16, name)
@@ -208,31 +212,29 @@ def tile_attend_mod_sorted_kernel(tc, xq, kT, vT, vs, offs, qoffs, out):
             )
 
         picked0 = gather_values(0, "picked0")
-        w1 = sbuf([P, P, PACK], BF16, "w1")
-        nc.vector.tensor_tensor(
-            w1[:], turned1[:].rearrange("p t x -> p x t"), vs_column[:].unsqueeze(1).to_broadcast([P, P, PACK]), MULT
-        )
         inv_total = sbuf([P, CHUNKS], F32, "inv_total")
-        nc.vector.reciprocal(inv_total[:], total[:])
-        multiply_on_vector(3)
+        nc.vector.reciprocal(inv_total[:, 0:2], total[:, 0:2])
+        w1 = multiply_on_vector(1, turned1)
+        picked1 = gather_values(1, "prob1")
         w0 = turn(weights[0], "w0", "bank1")
         v0 = turn(picked0, "v0", "bank0")
         inverse = sbuf([P, NQ], F32, "inverse")
         spread(0, "bank4")
-        w3 = turn(weights[3], "w3", "bank7")
+        turned3 = turn_probs(3, "bank7")
         w2 = turn(weights[2], "w2", "bank1")
 
-        halves = [operand(HALF, "w_half0", "prob3"), operand(HALF, "w_half1")]
+        halves = [operand(HALF, "w_half0"), operand(HALF, "w_half1")]
         quantize(w0[:], *part(halves[0], 0, P))
         values0 = quantize(v0[:], *part(operand(P, "v0"), 0, P))
         quantize(w1[:], *part(halves[0], P, P))
         sums00 = sums_of(values0, [part(halves[0], i * P, P) for i in range(2)], "sums00", ("bank2", "bank3"))
-        picked1 = gather_values(1, "v0")
-        quantize(w3[:], *part(halves[1], P, P))
+        w3 = multiply_on_vector(3, turned3)
         quantize(w2[:], *part(halves[1], 0, P))
+        quantize(w3[:], *part(halves[1], P, P))
+        nc.vector.reciprocal(inv_total[:, 2:4], total[:, 2:4])
         spread(1, "bank0")
         v1 = turn(picked1, "v1", "bank2")
-        sums01 = sums_of(values0, [part(halves[1], 0, HALF)], "v0", ("bank4",))
+        sums01 = sums_of(values0, [part(halves[1], 0, HALF)], "prob1", ("bank4",))
         put_back(0, 0, HALF, sums00)
         values1 = quantize(v1[:], *part(operand(P, "v1"), 0, P))
         sums1 = sums_of(values1, [part(half, 0, HALF) for half in halves], "sums1", ("bank3", "bank6"))

@@ -160,19 +160,19 @@ def tile_attend_mod_sorted_kernel(tc, xq, kT, vT, vs, offs, qoffs, out):
                 nc.tensor.transpose(bank[:, t, :], probs[b][:, t * P : (t + 1) * P], ident[:])
             return bank
 
-        neg_max = sbuf([P, CHUNKS], F32, "neg_max")
+        neg_max = [sbuf([P, 1], F32, "neg_max%d" % b) for b in range(CHUNKS)]
         total = sbuf([P, CHUNKS], F32, "total")
         probs = []
         weights = [None] * CHUNKS
         for b in range(CHUNKS):
-            nc.vector.tensor_reduce(neg_max[:, b : b + 1], scores[b][:], AXIS_X, MAX, negate=True)
+            nc.vector.tensor_reduce(neg_max[b][:], scores[b][:], AXIS_X, MAX, negate=True)
             probs.append(sbuf([P, N], F32, "prob%d" % b))
             order = "u e s" if b % 2 else "u s e"
             nc.scalar.activation(
                 probs[b][:].rearrange("p (%s) -> p %s" % (order, order), u=PAIR, e=PAIR),
                 scores[b][:].rearrange("p (u s e) -> p %s" % order, u=PAIR, e=PAIR),
                 EXP,
-                bias=neg_max[:, b : b + 1],
+                bias=neg_max[b][:],
                 accum_out=total[:, b : b + 1],
             )
             if b == 1:
@@ -211,15 +211,15 @@ def tile_attend_mod_sorted_kernel(tc, xq, kT, vT, vs, offs, qoffs, out):
                 out_windows[e][:].indirect(listed(q_list, first, count)), sums[:], inverse[:, first : first + count], MULT
             )
 
-        picked0 = gather_values(0, "picked0")
         inv_total = sbuf([P, CHUNKS], F32, "inv_total")
         nc.vector.reciprocal(inv_total[:, 0:2], total[:, 0:2])
+        inverse = sbuf([P, NQ], F32, "inverse")
+        spread(0, "bank4")
+        picked0 = gather_values(0, "neg_max1")
         w1 = multiply_on_vector(1, turned1)
         picked1 = gather_values(1, "prob1")
         w0 = turn(weights[0], "w0", "bank1")
         v0 = turn(picked0, "v0", "bank0")
-        inverse = sbuf([P, NQ], F32, "inverse")
-        spread(0, "bank4")
         turned3 = turn_probs(3, "bank7")
         w2 = turn(weights[2], "w2", "bank1")
 
@@ -232,7 +232,7 @@ def tile_attend_mod_sorted_kernel(tc, xq, kT, vT, vs, offs, qoffs, out):
         quantize(w2[:], *part(halves[1], 0, P))
         quantize(w3[:], *part(halves[1], P, P))
         nc.vector.reciprocal(inv_total[:, 2:4], total[:, 2:4])
-        spread(1, "bank0")
+        spread(1, "bank3")
         v1 = turn(picked1, "v1", "bank2")
         sums01 = sums_of(values0, [part(halves[1], 0, HALF)], "prob1", ("bank4",))
         put_back(0, 0, HALF, sums00)

@@ -75,14 +75,15 @@ def tile_attend_mod_sorted_kernel(tc, xq, kT, vT, vs, offs, qoffs, out):
             )
             return bank
 
-        def turn(paired, name, bank_name):
-            grouped = sbuf([P, P, PACK], BF16, name)
-            words = paired[:].bitcast(F32)
+        def runs(paired):
+            return [paired.bitcast(F32)[:, u * P : (u + 1) * P] for u in range(PAIR)]
+
+        def turn(words, grouped, bank_name):
             bank = psum.tile([P, PAIR, P], F32, name=bank_name)
             for u in range(PAIR):
-                nc.tensor.transpose(bank[:, u, :], words[:, u * P : (u + 1) * P], ident[:])
+                nc.tensor.transpose(bank[:, u, :], words[u], ident[:])
             nc.scalar.copy(
-                grouped[:].rearrange("p x t -> p (x t)").bitcast(F32).rearrange("p (x u) -> p x u", u=PAIR),
+                grouped.rearrange("p x t -> p (x t)").bitcast(F32).rearrange("p (x u) -> p x u", u=PAIR),
                 bank[:].rearrange("p u x -> p x u"),
             )
             return grouped
@@ -188,10 +189,8 @@ def tile_attend_mod_sorted_kernel(tc, xq, kT, vT, vs, offs, qoffs, out):
             )
             return grouped
 
-        def gather_values(e, name):
-            picked = sbuf([P, N], BF16, name)
-            nc.vector.tensor_copy(by_slot(picked[:]), v_windows[e][:].indirect(k_list[:]))
-            return picked
+        def gather_second_values(first, count):
+            nc.vector.tensor_copy(picked1[:, first : first + count], v_windows[1][:].indirect(listed(k_list, first, count)))
 
         def spread(h, bank_name):
             bank = psum.tile([P, 2, P], F32, name=bank_name)
@@ -215,28 +214,32 @@ def tile_attend_mod_sorted_kernel(tc, xq, kT, vT, vs, offs, qoffs, out):
         nc.vector.reciprocal(inv_total[:, 0:2], total[:, 0:2])
         inverse = sbuf([P, NQ], F32, "inverse")
         spread(0, "bank4")
-        picked0 = gather_values(0, "neg_max1")
+        picked0 = sbuf([P, N], BF16, "neg_max1")
+        nc.vector.tensor_copy(by_slot(picked0[:]), v_windows[0][:].indirect(k_list[:]))
         w1 = multiply_on_vector(1, turned1)
-        picked1 = gather_values(1, "prob1")
-        w0 = turn(weights[0], "w0", "bank1")
-        v0 = turn(picked0, "v0", "bank0")
+        both = sbuf([P, 2 * N - P], BF16, "prob1")
+        picked1 = both[:, 0:N]
+        gather_second_values(0, N - P)
+        w0 = turn(runs(weights[0][:]), sbuf([P, P, PACK], BF16, "w0")[:], "bank1")
+        v0 = turn(runs(picked0[:]), both[:, N - P :].rearrange("p (x t) -> p x t", t=PACK), "bank0")
         turned3 = turn_probs(3, "bank7")
-        w2 = turn(weights[2], "w2", "bank1")
+        w2 = turn(runs(weights[2][:]), sbuf([P, P, PACK], BF16, "w2")[:], "bank1")
 
         halves = [operand(HALF, "w_half0"), operand(HALF, "w_half1")]
-        quantize(w0[:], *part(halves[0], 0, P))
-        values0 = quantize(v0[:], *part(operand(P, "v0"), 0, P))
+        quantize(w0, *part(halves[0], 0, P))
+        values0 = quantize(v0, *part(operand(P, "v0"), 0, P))
         quantize(w1[:], *part(halves[0], P, P))
         sums00 = sums_of(values0, [part(halves[0], i * P, P) for i in range(2)], "sums00", ("bank2", "bank3"))
         w3 = multiply_on_vector(3, turned3)
-        quantize(w2[:], *part(halves[1], 0, P))
+        gather_second_values(N - P, P)
+        quantize(w2, *part(halves[1], 0, P))
         quantize(w3[:], *part(halves[1], P, P))
         nc.vector.reciprocal(inv_total[:, 2:4], total[:, 2:4])
         spread(1, "bank3")
-        v1 = turn(picked1, "v1", "bank2")
+        v1 = turn([picked1.bitcast(F32)[:, u::PAIR] for u in range(PAIR)], sbuf([P, P, PACK], BF16, "v1")[:], "bank2")
         sums01 = sums_of(values0, [part(halves[1], 0, HALF)], "prob1", ("bank4",))
         put_back(0, 0, HALF, sums00)
-        values1 = quantize(v1[:], *part(operand(P, "v1"), 0, P))
+        values1 = quantize(v1, *part(operand(P, "v1"), 0, P))
         sums1 = sums_of(values1, [part(half, 0, HALF) for half in halves], "sums1", ("bank3", "bank6"))
         put_back(0, HALF, HALF, sums01)
         nc.sync.dma_start(out[0:P, :], out_windows[0][:])

@@ -148,7 +148,7 @@ def tile_attend_mod_sorted_kernel(tc, xq, kT, vT, vs, offs, qoffs, out):
             shared.tile([P, 2 * P], U8, align_bytes=64, offset=2 * P, name="q12_scales"),
         )
         quantize(q_grouped[:, P : 3 * P, :], *part(q12, 0, 2 * P))
-        nc.gpsimd.tensor_copy(q_grouped[:, 3 * P : NQ, PACK - 1], last_chunk[:])
+        nc.scalar.copy(q_grouped[:, 3 * P : NQ, PACK - 1], last_chunk[:])
         scores += [product("bank%d" % b, part(q12, (b - 1) * P, P), keys) for b in (1, 2)]
         q3 = quantize(q_grouped[:, 3 * P : NQ, :], *part(operand(P, "q3", "q0_codes"), 0, P))
         scores.append(product("bank3", q3, keys))

@@ -26,6 +26,7 @@ PER_LIST_COLUMN = 16
 CHUNKS = NQ // P
 HALF = NQ // 2
 ALIGN = 256
+LATE = 192
 
 FLOPS = 2 * NQ * N * D + 2 * NQ * N * DV
 BYTES = 4 * (2 * D * T + DV * T + T + DV * T) + 2 * P * (N + NQ) // PER_LIST_COLUMN
@@ -217,11 +218,11 @@ def tile_attend_mod_sorted_kernel(tc, xq, kT, vT, vs, offs, qoffs, out):
         picked0 = sbuf([P, N], BF16, "neg_max1")
         nc.vector.tensor_copy(by_slot(picked0[:]), v_windows[0][:].indirect(k_list[:]))
         w1 = multiply_on_vector(1, turned1)
-        both = sbuf([P, 2 * N - P], BF16, "prob1")
+        both = sbuf([P, 2 * N - LATE], BF16, "prob1")
         picked1 = both[:, 0:N]
-        gather_second_values(0, N - P)
+        gather_second_values(0, N - LATE)
         w0 = turn(runs(weights[0][:]), sbuf([P, P, PACK], BF16, "w0")[:], "bank1")
-        v0 = turn(runs(picked0[:]), both[:, N - P :].rearrange("p (x t) -> p x t", t=PACK), "bank0")
+        v0 = turn(runs(picked0[:]), both[:, N - LATE :].rearrange("p (x t) -> p x t", t=PACK), "bank0")
         turned3 = turn_probs(3, "bank7")
         w2 = turn(runs(weights[2][:]), sbuf([P, P, PACK], BF16, "w2")[:], "bank1")
 
@@ -231,7 +232,7 @@ def tile_attend_mod_sorted_kernel(tc, xq, kT, vT, vs, offs, qoffs, out):
         quantize(w1[:], *part(halves[0], P, P))
         sums00 = sums_of(values0, [part(halves[0], i * P, P) for i in range(2)], "sums00", ("bank2", "bank3"))
         w3 = multiply_on_vector(3, turned3)
-        gather_second_values(N - P, P)
+        gather_second_values(N - LATE, LATE)
         quantize(w2, *part(halves[1], 0, P))
         quantize(w3[:], *part(halves[1], P, P))
         nc.vector.reciprocal(inv_total[:, 2:4], total[:, 2:4])

@@ -211,19 +211,19 @@ def tile_attend_mod_sorted_kernel(tc, xq, kT, vT, vs, offs, qoffs, out):
                 out_windows[e][:].indirect(listed(q_list, first, count)), sums[:], inverse[:, first : first + count], MULT
             )
 
-        inv_total = sbuf([P, CHUNKS], F32, "inv_total")
-        nc.vector.reciprocal(inv_total[:, 0:2], total[:, 0:2])
-        inverse = sbuf([P, NQ], F32, "inverse")
-        spread(0, "bank4")
         picked0 = sbuf([P, N], BF16, "neg_max1")
         nc.vector.tensor_copy(by_slot(picked0[:]), v_windows[0][:].indirect(k_list[:]))
         w1 = multiply_on_vector(1, turned1)
+        inv_total = sbuf([P, CHUNKS], F32, "inv_total")
+        nc.vector.reciprocal(inv_total[:], total[:])
         both = sbuf([P, 2 * N - LATE], BF16, "prob1")
         picked1 = both[:, 0:N]
         gather_second_values(0, N - LATE)
         w0 = turn(runs(weights[0][:]), sbuf([P, P, PACK], BF16, "w0")[:], "bank1")
         v0 = turn(runs(picked0[:]), both[:, N - LATE :].rearrange("p (x t) -> p x t", t=PACK), "bank0")
         turned3 = turn_probs(3, "bank7")
+        inverse = sbuf([P, NQ], F32, "inverse")
+        spread(0, "bank4")
         w2 = turn(runs(weights[2][:]), sbuf([P, P, PACK], BF16, "w2")[:], "bank1")
 
         halves = [operand(HALF, "w_half0"), operand(HALF, "w_half1")]
@@ -235,7 +235,6 @@ def tile_attend_mod_sorted_kernel(tc, xq, kT, vT, vs, offs, qoffs, out):
         gather_second_values(N - LATE, LATE)
         quantize(w2, *part(halves[1], 0, P))
         quantize(w3[:], *part(halves[1], P, P))
-        nc.vector.reciprocal(inv_total[:, 2:4], total[:, 2:4])
         spread(1, "bank3")
         v1 = turn([picked1.bitcast(F32)[:, u::PAIR] for u in range(PAIR)], sbuf([P, P, PACK], BF16, "v1")[:], "bank2")
         sums01 = sums_of(values0, [part(halves[1], 0, HALF)], "prob1", ("bank4",))

@@ -26,7 +26,6 @@ PER_LIST_COLUMN = 16
 CHUNKS = NQ // P
 HALF = NQ // 2
 ALIGN = 256
-LATE = 192
 
 FLOPS = 2 * NQ * N * D + 2 * NQ * N * DV
 BYTES = 4 * (2 * D * T + DV * T + T + DV * T) + 2 * P * (N + NQ) // PER_LIST_COLUMN
@@ -183,15 +182,14 @@ def tile_attend_mod_sorted_kernel(tc, xq, kT, vT, vs, offs, qoffs, out):
                 weights[b] = sbuf([P, N], BF16, "weights%d" % b)
                 nc.gpsimd.tensor_tensor(weights[b][:], probs[b][:], vs_row[:], MULT)
 
-        def multiply_on_vector(b, bank):
-            grouped = sbuf([P, P, PACK], BF16, "w%d" % b)
+        def multiply_on_vector(grouped, bank):
             nc.vector.tensor_tensor(
-                grouped[:], bank[:].rearrange("p t x -> p x t"), vs_column[:].unsqueeze(1).to_broadcast([P, P, PACK]), MULT
+                grouped, bank[:].rearrange("p t x -> p x t"), vs_column[:].unsqueeze(1).to_broadcast([P, P, PACK]), MULT
             )
-            return grouped
 
-        def gather_second_values(first, count):
-            nc.vector.tensor_copy(picked1[:, first : first + count], v_windows[1][:].indirect(listed(k_list, first, count)))
+        def gather_second_values(h):
+            rows = slice(h * P // 2, (h + 1) * P // 2)
+            nc.vector.tensor_copy(by_slot(picked1)[:, rows], v_windows[1][:].indirect(listed(k_list, h * HALF, HALF)))
 
         def spread(h, bank_name):
             bank = psum.tile([P, 2, P], F32, name=bank_name)
@@ -213,30 +211,29 @@ def tile_attend_mod_sorted_kernel(tc, xq, kT, vT, vs, offs, qoffs, out):
 
         picked0 = sbuf([P, N], BF16, "neg_max1")
         nc.vector.tensor_copy(by_slot(picked0[:]), v_windows[0][:].indirect(k_list[:]))
-        w1 = multiply_on_vector(1, turned1)
+        w_grouped = [sbuf([P, HALF, PACK], BF16, "w_grouped%d" % h) for h in range(2)]
+        multiply_on_vector(w_grouped[0][:, P:HALF, :], turned1)
         inv_total = sbuf([P, CHUNKS], F32, "inv_total")
         nc.vector.reciprocal(inv_total[:], total[:])
-        both = sbuf([P, 2 * N - LATE], BF16, "prob1")
+        both = sbuf([P, 2 * N - P], BF16, "prob1")
         picked1 = both[:, 0:N]
-        gather_second_values(0, N - LATE)
-        w0 = turn(runs(weights[0][:]), sbuf([P, P, PACK], BF16, "w0")[:], "bank1")
-        v0 = turn(runs(picked0[:]), both[:, N - LATE :].rearrange("p (x t) -> p x t", t=PACK), "bank0")
+        gather_second_values(0)
+        turn(runs(weights[0][:]), w_grouped[0][:, 0:P, :], "bank1")
+        v0 = turn(runs(picked0[:]), both[:, N - P :].rearrange("p (x t) -> p x t", t=PACK), "bank0")
         turned3 = turn_probs(3, "bank7")
         inverse = sbuf([P, NQ], F32, "inverse")
         spread(0, "bank4")
-        w2 = turn(runs(weights[2][:]), sbuf([P, P, PACK], BF16, "w2")[:], "bank1")
+        turn(runs(weights[2][:]), w_grouped[1][:, 0:P, :], "bank1")
 
         halves = [operand(HALF, "w_half0"), operand(HALF, "w_half1")]
-        quantize(w0, *part(halves[0], 0, P))
+        quantize(w_grouped[0][:], *part(halves[0], 0, HALF))
         values0 = quantize(v0, *part(operand(P, "v0"), 0, P))
-        quantize(w1[:], *part(halves[0], P, P))
         sums00 = sums_of(values0, [part(halves[0], i * P, P) for i in range(2)], "sums00", ("bank2", "bank3"))
-        w3 = multiply_on_vector(3, turned3)
-        gather_second_values(N - LATE, LATE)
-        quantize(w2, *part(halves[1], 0, P))
-        quantize(w3[:], *part(halves[1], P, P))
+        multiply_on_vector(w_grouped[1][:, P:HALF, :], turned3)
+        gather_second_values(1)
+        quantize(w_grouped[1][:], *part(halves[1], 0, HALF))
+        v1 = turn(runs(picked1), sbuf([P, P, PACK], BF16, "v1")[:], "bank2")
         spread(1, "bank3")
-        v1 = turn([picked1.bitcast(F32)[:, u::PAIR] for u in range(PAIR)], sbuf([P, P, PACK], BF16, "v1")[:], "bank2")
         sums01 = sums_of(values0, [part(halves[1], 0, HALF)], "prob1", ("bank4",))
         put_back(0, 0, HALF, sums00)
         values1 = quantize(v1, *part(operand(P, "v1"), 0, P))

@@ -23,9 +23,15 @@ DV = 256
 N = 512
 NQ = 512
 PER_LIST_COLUMN = 16
-CHUNKS = NQ // P
-HALF = NQ // 2
+Q_CHUNKS = NQ // P
+V_CHUNKS = DV // P
+HALVES = 2
+HALF_Q = NQ // HALVES
+HALF_N = N // HALVES
+CHUNKS_PER_HALF = Q_CHUNKS // HALVES
 ALIGN = 256
+MX_ALIGN = 64
+SIDE_BY_SIDE = "p t x -> p x t"
 
 FLOPS = 2 * NQ * N * D + 2 * NQ * N * DV
 BYTES = 4 * (2 * D * T + DV * T + T + DV * T) + 2 * P * (N + NQ) // PER_LIST_COLUMN
@@ -46,21 +52,24 @@ def tile_attend_mod_sorted_kernel(tc, xq, kT, vT, vs, offs, qoffs, out):
             nc.sync.dma_start(tile[:], rows)
             return tile
 
+        def entries(listed, first, count):
+            return listed[:, first // PER_LIST_COLUMN : (first + count) // PER_LIST_COLUMN]
+
         def by_slot(paired):
             return paired.rearrange("p (u s e) -> p s u e", u=PAIR, e=PAIR)
 
-        def listed(tile, first, count):
-            return tile[:, first // PER_LIST_COLUMN : (first + count) // PER_LIST_COLUMN]
-
-        def quantize(grouped, codes, scales):
-            nc.vector.quantize_mx(out=codes.bitcast(FP8X4), scales=scales, in_=grouped.rearrange("p c t -> p (c t)"))
-            return codes, scales
-
-        def operand(width, name, codes_name=None):
+        def mx_tiles(width, name, codes_name=None):
             return sbuf([P, width], U32, codes_name or name + "_codes"), sbuf([P, width], U8, name + "_scales")
 
-        def part(pair, first, count):
-            return [tile[:, first : first + count] for tile in pair]
+        def columns(quantised, first, count):
+            return [tile[:, first : first + count] for tile in quantised]
+
+        def quantize(grouped, quantised):
+            codes, scales = quantised
+            nc.vector.quantize_mx(
+                out=codes[:].bitcast(FP8X4), scales=scales[:], in_=grouped.rearrange("p c t -> p (c t)")
+            )
+            return quantised
 
         def product(bank_name, stationary, moving):
             bank = psum.tile([P, moving[0].shape[1]], F32, name=bank_name)
@@ -75,18 +84,13 @@ def tile_attend_mod_sorted_kernel(tc, xq, kT, vT, vs, offs, qoffs, out):
             )
             return bank
 
-        def runs(paired):
-            return [paired.bitcast(F32)[:, u * P : (u + 1) * P] for u in range(PAIR)]
-
-        def turn(words, grouped, bank_name):
+        def turn_pairs(paired, grouped, bank_name):
+            words = paired.bitcast(F32)
             bank = psum.tile([P, PAIR, P], F32, name=bank_name)
             for u in range(PAIR):
-                nc.tensor.transpose(bank[:, u, :], words[u], ident[:])
-            nc.scalar.copy(
-                grouped.rearrange("p x t -> p (x t)").bitcast(F32).rearrange("p (x u) -> p x u", u=PAIR),
-                bank[:].rearrange("p u x -> p x u"),
-            )
-            return grouped
+                nc.tensor.transpose(bank[:, u, :], words[:, u * P : (u + 1) * P], ident[:])
+            grouped_words = grouped.rearrange("p x t -> p (x t)").bitcast(F32).rearrange("p (x u) -> p x u", u=PAIR)
+            nc.scalar.copy(grouped_words, bank[:].rearrange(SIDE_BY_SIDE))
 
         k_list = sbuf([P, N // PER_LIST_COLUMN], U16, "k_list")
         q_list = sbuf([P, NQ // PER_LIST_COLUMN], U16, "q_list")
@@ -97,21 +101,24 @@ def tile_attend_mod_sorted_kernel(tc, xq, kT, vT, vs, offs, qoffs, out):
         nc.scalar.dma_start(k_planes[0][:, T // 2 : T], k_rows[:, 0, T // 2 : T])
         nc.sync.dma_start(k_list[:], offs)
         k_planes.append(load(k_rows[:, 1, :], "k_plane1"))
+
         vs_window = sbuf([P, T], F32, "vs_window")
         nc.vector.memset(vs_window[:], 0.0)
         ident = sbuf([P, P], F32, "ident")
         make_identity(nc, ident[:])
-        out_windows = [sbuf([P, T], F32, "out_window%d" % e) for e in range(DV // P)]
+        out_windows = [sbuf([P, T], F32, "out_window%d" % e) for e in range(V_CHUNKS)]
         for window in out_windows:
             nc.gpsimd.memset(window[:], 0.0)
+
         nc.sync.dma_start(vs_window[0:1, :], vs[0:1, :])
         k_planes.extend([load(k_rows[:, t, :], "k_plane%d" % t) for t in range(2, PACK)])
         nc.sync.dma_start(q_list[:], qoffs)
         q_planes = [load(q_rows[:, t, :], "q_plane%d" % t) for t in range(PACK)]
-        v_windows = [load(vT[e * P : (e + 1) * P, :], "v_window%d" % e) for e in range(DV // P)]
+        v_windows = [load(vT[e * P : (e + 1) * P, :], "v_window%d" % e) for e in range(V_CHUNKS)]
 
         k_grouped = sbuf([P, N, PACK], BF16, "k_grouped")
         nc.vector.tensor_copy(by_slot(k_grouped[:, :, 0]), k_planes[0][:].indirect(k_list[:]))
+
         vs_picked = sbuf([P, N], F32, "vs_picked")
         nc.vector.tensor_copy(vs_picked[:], vs_window[:].indirect(k_list[:]))
         column_bank = psum.tile([P, PACK, P], F32, name="bank4")
@@ -127,118 +134,136 @@ def tile_attend_mod_sorted_kernel(tc, xq, kT, vT, vs, offs, qoffs, out):
             vs_row[:].rearrange("p (u s e) -> p u s e", u=PAIR, e=PAIR),
             row_bank[:].rearrange("p (u e) s -> p u s e", e=PAIR),
         )
+
         for t in range(1, PACK):
             nc.vector.tensor_copy(by_slot(k_grouped[:, :, t]), k_planes[t][:].indirect(k_list[:]))
-        keys = part(operand(N, "k"), 0, N)
-        quantize(k_grouped[:], *keys)
+        keys = columns(quantize(k_grouped[:], mx_tiles(N, "k")), 0, N)
 
         q_grouped = sbuf([P, NQ, PACK], BF16, "q_grouped")
         for t in range(PACK - 1):
             nc.vector.tensor_copy(q_grouped[:, :, t], q_planes[t][:].indirect(q_list[:]))
-        last = q_planes[PACK - 1]
-        first_chunk = shared.tile([P, 2 * P], BF16, align_bytes=64, offset=0, name="first_chunk")
-        nc.vector.tensor_copy(first_chunk[:, 0:P], last[:].indirect(listed(q_list, 0, P)))
-        nc.scalar.copy(q_grouped[:, 0:P, PACK - 1], first_chunk[:, 0:P])
-        nc.vector.tensor_copy(q_grouped[:, P : 3 * P, PACK - 1], last[:].indirect(listed(q_list, P, 2 * P)))
-        scores = [product("bank0", quantize(q_grouped[:, 0:P, :], *part(operand(P, "q0"), 0, P)), keys)]
-        last_chunk = shared.tile([P, P], BF16, align_bytes=64, offset=0, name="last_chunk")
-        nc.vector.tensor_copy(last_chunk[:], last[:].indirect(listed(q_list, 3 * P, P)))
-        q12 = (
-            sbuf([P, 2 * P], U32, "q12_codes"),
-            shared.tile([P, 2 * P], U8, align_bytes=64, offset=2 * P, name="q12_scales"),
-        )
-        quantize(q_grouped[:, P : 3 * P, :], *part(q12, 0, 2 * P))
-        nc.scalar.copy(q_grouped[:, 3 * P : NQ, PACK - 1], last_chunk[:])
-        scores += [product("bank%d" % b, part(q12, (b - 1) * P, P), keys) for b in (1, 2)]
-        q3 = quantize(q_grouped[:, 3 * P : NQ, :], *part(operand(P, "q3", "q0_codes"), 0, P))
+
+        def last_plane(first, count):
+            return q_planes[PACK - 1][:].indirect(entries(q_list, first, count))
+
+        def q_chunks(first, count):
+            return q_grouped[:, first * P : (first + count) * P, :]
+
+        run0 = shared.tile([P, 2 * P], BF16, align_bytes=MX_ALIGN, offset=0, name="run0")
+        nc.vector.tensor_copy(run0[:, 0:P], last_plane(0, P))
+        nc.scalar.copy(q_chunks(0, 1)[:, :, PACK - 1], run0[:, 0:P])
+        nc.vector.tensor_copy(q_chunks(1, 2)[:, :, PACK - 1], last_plane(P, 2 * P))
+        q0 = quantize(q_chunks(0, 1), mx_tiles(P, "q0"))
+        scores = [product("bank0", columns(q0, 0, P), keys)]
+        run3 = shared.tile([P, P], BF16, align_bytes=MX_ALIGN, offset=0, name="run3")
+        nc.vector.tensor_copy(run3[:], last_plane(3 * P, P))
+        q12_codes = sbuf([P, 2 * P], U32, "q12_codes")
+        q12_scales = shared.tile([P, 2 * P], U8, align_bytes=MX_ALIGN, offset=2 * P, name="q12_scales")
+        q12 = quantize(q_chunks(1, 2), (q12_codes, q12_scales))
+        nc.scalar.copy(q_chunks(3, 1)[:, :, PACK - 1], run3[:])
+        scores.extend([product("bank%d" % (1 + i), columns(q12, i * P, P), keys) for i in range(2)])
+        q3 = columns(quantize(q_chunks(3, 1), mx_tiles(P, "q3", "q0_codes")), 0, P)
         scores.append(product("bank3", q3, keys))
+
         product("bank7", q3, keys)
-        product("bank6", q3, [half[:, 0:HALF] for half in keys])
+        product("bank5", q3, columns(keys, 0, HALF_N))
 
-        def turn_probs(b, bank_name):
-            bank = psum.tile([P, PACK, P], F32, name=bank_name)
-            for t in range(PACK):
-                nc.tensor.transpose(bank[:, t, :], probs[b][:, t * P : (t + 1) * P], ident[:])
-            return bank
+        neg_max = [sbuf([P, 1], F32, "neg_max%d" % b) for b in range(Q_CHUNKS)]
+        total = sbuf([P, Q_CHUNKS], F32, "total")
 
-        neg_max = [sbuf([P, 1], F32, "neg_max%d" % b) for b in range(CHUNKS)]
-        total = sbuf([P, CHUNKS], F32, "total")
-        probs = []
-        weights = [None] * CHUNKS
-        for b in range(CHUNKS):
+        def softmax(b, order):
             nc.vector.tensor_reduce(neg_max[b][:], scores[b][:], AXIS_X, MAX, negate=True)
-            probs.append(sbuf([P, N], F32, "prob%d" % b))
-            order = "u e s" if b % 2 else "u s e"
+            prob = sbuf([P, N], F32, "prob%d" % b)
             nc.scalar.activation(
-                probs[b][:].rearrange("p (%s) -> p %s" % (order, order), u=PAIR, e=PAIR),
+                prob[:].rearrange("p (%s) -> p %s" % (order, order), u=PAIR, e=PAIR),
                 scores[b][:].rearrange("p (u s e) -> p %s" % order, u=PAIR, e=PAIR),
                 EXP,
                 bias=neg_max[b][:],
                 accum_out=total[:, b : b + 1],
             )
-            if b == 1:
-                turned1 = turn_probs(b, "bank6")
-            if b % 2 == 0:
-                weights[b] = sbuf([P, N], BF16, "weights%d" % b)
-                nc.gpsimd.tensor_tensor(weights[b][:], probs[b][:], vs_row[:], MULT)
+            return prob
 
-        def multiply_on_vector(grouped, bank):
-            nc.vector.tensor_tensor(
-                grouped, bank[:].rearrange("p t x -> p x t"), vs_column[:].unsqueeze(1).to_broadcast([P, P, PACK]), MULT
-            )
+        def multiply_on_gpsimd(prob, name):
+            weights = sbuf([P, N], BF16, name)
+            nc.gpsimd.tensor_tensor(weights[:], prob[:], vs_row[:], MULT)
+            return weights
+
+        def turn_probs(prob, bank_name):
+            bank = psum.tile([P, PACK, P], F32, name=bank_name)
+            for t in range(PACK):
+                nc.tensor.transpose(bank[:, t, :], prob[:, t * P : (t + 1) * P], ident[:])
+            return bank
+
+        def multiply_on_vector(turned, grouped):
+            scales = vs_column[:].unsqueeze(1).to_broadcast([P, P, PACK])
+            nc.vector.tensor_tensor(grouped, turned[:].rearrange(SIDE_BY_SIDE), scales, MULT)
+
+        weights0 = multiply_on_gpsimd(softmax(0, "u s e"), "weights0")
+        turned1 = turn_probs(softmax(1, "u e s"), "bank6")
+        weights2 = multiply_on_gpsimd(softmax(2, "u s e"), "weights2")
+        prob3 = softmax(3, "u e s")
 
         def gather_second_values(h):
-            rows = slice(h * P // 2, (h + 1) * P // 2)
-            nc.vector.tensor_copy(by_slot(picked1)[:, rows], v_windows[1][:].indirect(listed(k_list, h * HALF, HALF)))
+            partitions_to_be = slice(h * P // HALVES, (h + 1) * P // HALVES)
+            picked = v_windows[1][:].indirect(entries(k_list, h * HALF_N, HALF_N))
+            nc.vector.tensor_copy(by_slot(v1_paired)[:, partitions_to_be], picked)
 
-        def spread(h, bank_name):
-            bank = psum.tile([P, 2, P], F32, name=bank_name)
-            for i in range(2):
-                nc.tensor.transpose(bank[:, i, :], inv_total[:, 2 * h + i : 2 * h + i + 1].to_broadcast([P, P]), ident[:])
-            nc.scalar.copy(inverse[:, h * HALF : (h + 1) * HALF], bank[:].rearrange("p b q -> p (b q)"))
+        def spread_inverse(h, bank_name):
+            bank = psum.tile([P, CHUNKS_PER_HALF, P], F32, name=bank_name)
+            for i in range(CHUNKS_PER_HALF):
+                b = h * CHUNKS_PER_HALF + i
+                nc.tensor.transpose(bank[:, i, :], inv_total[:, b : b + 1].to_broadcast([P, P]), ident[:])
+            nc.scalar.copy(inverse[:, h * HALF_Q : (h + 1) * HALF_Q], bank[:].rearrange("p b q -> p (b q)"))
 
-        def sums_of(values, runs, name, bank_names):
+        def weighted_sums(values, runs, name, bank_names):
             width = runs[0][0].shape[1]
             sums = sbuf([P, len(runs) * width], F32, name)
             for i, bank_name in enumerate(bank_names):
-                nc.scalar.copy(sums[:, i * width : (i + 1) * width], product(bank_name, values, runs[i])[:])
+                bank = product(bank_name, columns(values, 0, P), runs[i])
+                nc.scalar.copy(sums[:, i * width : (i + 1) * width], bank[:])
             return sums
 
         def put_back(e, first, count, sums):
-            nc.vector.tensor_tensor(
-                out_windows[e][:].indirect(listed(q_list, first, count)), sums[:], inverse[:, first : first + count], MULT
-            )
+            window = out_windows[e][:].indirect(entries(q_list, first, count))
+            nc.vector.tensor_tensor(window, sums[:], inverse[:, first : first + count], MULT)
 
-        picked0 = sbuf([P, N], BF16, "neg_max1")
-        nc.vector.tensor_copy(by_slot(picked0[:]), v_windows[0][:].indirect(k_list[:]))
-        w_grouped = [sbuf([P, HALF, PACK], BF16, "w_grouped%d" % h) for h in range(2)]
-        multiply_on_vector(w_grouped[0][:, P:HALF, :], turned1)
-        inv_total = sbuf([P, CHUNKS], F32, "inv_total")
+        v0_paired = sbuf([P, N], BF16, "neg_max1")
+        nc.vector.tensor_copy(by_slot(v0_paired[:]), v_windows[0][:].indirect(k_list[:]))
+        w_grouped = [sbuf([P, HALF_Q, PACK], BF16, "w_grouped%d" % h) for h in range(HALVES)]
+        multiply_on_vector(turned1, w_grouped[0][:, P:HALF_Q, :])
+        inv_total = sbuf([P, Q_CHUNKS], F32, "inv_total")
         nc.vector.reciprocal(inv_total[:], total[:])
-        both = sbuf([P, 2 * N - P], BF16, "prob1")
-        picked1 = both[:, 0:N]
-        gather_second_values(0)
-        turn(runs(weights[0][:]), w_grouped[0][:, 0:P, :], "bank1")
-        v0 = turn(runs(picked0[:]), both[:, N - P :].rearrange("p (x t) -> p x t", t=PACK), "bank0")
-        turned3 = turn_probs(3, "bank7")
-        inverse = sbuf([P, NQ], F32, "inverse")
-        spread(0, "bank4")
-        turn(runs(weights[2][:]), w_grouped[1][:, 0:P, :], "bank1")
 
-        halves = [operand(HALF, "w_half0"), operand(HALF, "w_half1")]
-        quantize(w_grouped[0][:], *part(halves[0], 0, HALF))
-        values0 = quantize(v0, *part(operand(P, "v0"), 0, P))
-        sums00 = sums_of(values0, [part(halves[0], i * P, P) for i in range(2)], "sums00", ("bank2", "bank3"))
-        multiply_on_vector(w_grouped[1][:, P:HALF, :], turned3)
+        v_overlap = N // 4
+        v_tile = sbuf([P, 2 * N - v_overlap], BF16, "prob1")
+        v1_paired = v_tile[:, 0:N]
+        v0_grouped = v_tile[:, N - v_overlap :].rearrange("p (x t) -> p x t", t=PACK)
+        gather_second_values(0)
+        turn_pairs(weights0[:], w_grouped[0][:, 0:P, :], "bank1")
+        turn_pairs(v0_paired[:], v0_grouped, "bank0")
+        turned3 = turn_probs(prob3, "bank7")
+        inverse = sbuf([P, NQ], F32, "inverse")
+        spread_inverse(0, "bank4")
+        turn_pairs(weights2[:], w_grouped[1][:, 0:P, :], "bank1")
+
+        w_halves = [mx_tiles(HALF_Q, "w_half%d" % h) for h in range(HALVES)]
+        quantize(w_grouped[0][:], w_halves[0])
+        values0 = quantize(v0_grouped, mx_tiles(P, "v0"))
+        first_chunks = [columns(w_halves[0], i * P, P) for i in range(CHUNKS_PER_HALF)]
+        sums00 = weighted_sums(values0, first_chunks, "sums00", ("bank2", "bank3"))
+        multiply_on_vector(turned3, w_grouped[1][:, P:HALF_Q, :])
         gather_second_values(1)
-        quantize(w_grouped[1][:], *part(halves[1], 0, HALF))
-        v1 = turn(runs(picked1), sbuf([P, P, PACK], BF16, "v1")[:], "bank2")
-        spread(1, "bank3")
-        sums01 = sums_of(values0, [part(halves[1], 0, HALF)], "prob1", ("bank4",))
-        put_back(0, 0, HALF, sums00)
-        values1 = quantize(v1, *part(operand(P, "v1"), 0, P))
-        sums1 = sums_of(values1, [part(half, 0, HALF) for half in halves], "sums1", ("bank3", "bank6"))
-        put_back(0, HALF, HALF, sums01)
+        quantize(w_grouped[1][:], w_halves[1])
+
+        v1_grouped = sbuf([P, P, PACK], BF16, "v1_grouped")
+        turn_pairs(v1_paired, v1_grouped[:], "bank2")
+        spread_inverse(1, "bank3")
+        whole_halves = [columns(half, 0, HALF_Q) for half in w_halves]
+        sums01 = weighted_sums(values0, whole_halves[1:], "prob1", ("bank4",))
+        put_back(0, 0, HALF_Q, sums00)
+        values1 = quantize(v1_grouped[:], mx_tiles(P, "v1"))
+        sums1 = weighted_sums(values1, whole_halves, "sums1", ("bank3", "bank6"))
+        put_back(0, HALF_Q, HALF_Q, sums01)
         nc.sync.dma_start(out[0:P, :], out_windows[0][:])
         put_back(1, 0, NQ, sums1)
         nc.sync.dma_start(out[P:DV, :], out_windows[1][:])

@@ -150,8 +150,10 @@ def tile_attend_mod_sorted_kernel(tc, xq, kT, vT, vs, offs, qoffs, out):
             return q_grouped[:, first * P : (first + count) * P, :]
 
         run0 = shared.tile([P, 2 * P], BF16, align_bytes=MX_ALIGN, offset=0, name="run0")
-        nc.vector.tensor_copy(run0[:, 0:P], last_plane(0, P))
-        nc.scalar.copy(q_chunks(0, 1)[:, :, PACK - 1], run0[:, 0:P])
+        for first in range(0, P, P // 2):
+            half = slice(first, first + P // 2)
+            nc.vector.tensor_copy(run0[:, half], last_plane(first, P // 2))
+            nc.scalar.copy(q_chunks(0, 1)[:, half, PACK - 1], run0[:, half])
         nc.vector.tensor_copy(q_chunks(1, 2)[:, :, PACK - 1], last_plane(P, 2 * P))
         q0 = quantize(q_chunks(0, 1), mx_tiles(P, "q0"))
         scores = [product("bank0", columns(q0, 0, P), keys)]

@@ -12,6 +12,8 @@ FP8X4 = mybir.dt.float8_e4m3fn_x4
 EXP = mybir.ActivationFunctionType.Exp
 MULT = mybir.AluOpType.mult
 MAX = mybir.AluOpType.max
+MIN = mybir.AluOpType.min
+IDENTITY = mybir.ActivationFunctionType.Identity
 AXIS_X = mybir.AxisListType.X
 
 P = 128
@@ -156,31 +158,39 @@ def tile_attend_mod_sorted_kernel(tc, xq, kT, vT, vs, offs, qoffs, out):
             nc.scalar.copy(q_chunks(0, 1)[:, half, PACK - 1], run0[:, half])
         nc.vector.tensor_copy(q_chunks(1, 2)[:, :, PACK - 1], last_plane(P, 2 * P))
         q0 = quantize(q_chunks(0, 1), mx_tiles(P, "q0"))
-        scores = [product("bank0", columns(q0, 0, P), keys)]
+        scores0 = [
+            product(name, columns(q0, 0, P), columns(keys, h * HALF_N, HALF_N)) for h, name in enumerate(("bank0", "bank4"))
+        ]
+        scores = [None]
         run3 = shared.tile([P, P], BF16, align_bytes=MX_ALIGN, offset=0, name="run3")
-        nc.vector.tensor_copy(run3[:], last_plane(3 * P, P))
+        halves = [slice(first, first + P // 2) for first in range(0, P, P // 2)]
+        for half in halves:
+            nc.vector.tensor_copy(run3[:, half], last_plane(3 * P + half.start, P // 2))
         q12_codes = sbuf([P, 2 * P], U32, "q12_codes")
         q12_scales = shared.tile([P, 2 * P], U8, align_bytes=MX_ALIGN, offset=2 * P, name="q12_scales")
         q12 = quantize(q_chunks(1, 2), (q12_codes, q12_scales))
-        nc.scalar.copy(q_chunks(3, 1)[:, :, PACK - 1], run3[:])
+        for half in halves:
+            nc.scalar.copy(q_chunks(3, 1)[:, half, PACK - 1], run3[:, half])
         scores.extend([product("bank%d" % (1 + i), columns(q12, i * P, P), keys) for i in range(2)])
+        half_max = sbuf([P, 1], F32, "half_max")
+        nc.vector.tensor_reduce(half_max[:], scores0[0][:], AXIS_X, MAX, negate=True)
         q3 = columns(quantize(q_chunks(3, 1), mx_tiles(P, "q3", "q0_codes")), 0, P)
         scores.append(product("bank3", q3, keys))
 
         product("bank7", q3, keys)
         product("bank5", q3, columns(keys, 0, HALF_N))
 
-        neg_max = [sbuf([P, 1], F32, "neg_max%d" % b) for b in range(Q_CHUNKS)]
         total = sbuf([P, Q_CHUNKS], F32, "total")
+        neg_max = [sbuf([P, 1], F32, "neg_max%d" % b)[:] if b != 2 else total[:, 0:1] for b in range(Q_CHUNKS)]
 
         def softmax(b, order):
-            nc.vector.tensor_reduce(neg_max[b][:], scores[b][:], AXIS_X, MAX, negate=True)
+            nc.vector.tensor_reduce(neg_max[b], scores[b][:], AXIS_X, MAX, negate=True)
             prob = sbuf([P, N], F32, "prob%d" % b)
             nc.scalar.activation(
                 prob[:].rearrange("p (%s) -> p %s" % (order, order), u=PAIR, e=PAIR),
                 scores[b][:].rearrange("p (u s e) -> p %s" % order, u=PAIR, e=PAIR),
                 EXP,
-                bias=neg_max[b][:],
+                bias=neg_max[b],
                 accum_out=total[:, b : b + 1],
             )
             return prob
@@ -200,10 +210,19 @@ def tile_attend_mod_sorted_kernel(tc, xq, kT, vT, vs, offs, qoffs, out):
             scales = vs_column[:].unsqueeze(1).to_broadcast([P, P, PACK])
             nc.vector.tensor_tensor(grouped, turned[:].rearrange(SIDE_BY_SIDE), scales, MULT)
 
-        weights0 = multiply_on_gpsimd(softmax(0, "u s e"), "weights0")
+        negated = sbuf([P, HALF_N], F32, "negated")
+        nc.vector.tensor_scalar(negated[:], scores0[1][:], -1.0, half_max[:], MULT, MIN, accum_out=neg_max[0])
+        prob0 = sbuf([P, N], F32, "prob0")
+        half_total = sbuf([P, HALVES], F32, "half_total")
+        nc.scalar.activation(prob0[:, 0:HALF_N], scores0[0][:], EXP, bias=neg_max[0], accum_out=half_total[:, 0:1])
+        nc.scalar.activation(
+            prob0[:, HALF_N:N], negated[:], EXP, bias=neg_max[0], scale=-1.0, accum_out=half_total[:, 1:2]
+        )
+        weights0 = multiply_on_gpsimd(prob0, "weights0")
         turned1 = turn_probs(softmax(1, "u e s"), "bank6")
         weights2 = multiply_on_gpsimd(softmax(2, "u s e"), "weights2")
         prob3 = softmax(3, "u e s")
+        nc.scalar.activation(total[:, 0:1], half_total[:, 0:1], IDENTITY, bias=half_total[:, 1:2])
 
         def gather_second_values(h):
             partitions_to_be = slice(h * P // HALVES, (h + 1) * P // HALVES)

@@ -31,6 +31,7 @@ HALVES = 2
 HALF_Q = NQ // HALVES
 HALF_N = N // HALVES
 CHUNKS_PER_HALF = Q_CHUNKS // HALVES
+V_EARLY = 320
 ALIGN = 256
 MX_ALIGN = 64
 SIDE_BY_SIDE = "p t x -> p x t"
@@ -86,11 +87,12 @@ def tile_attend_mod_sorted_kernel(tc, xq, kT, vT, vs, offs, qoffs, out):
             )
             return bank
 
-        def turn_pairs(paired, grouped, bank_name):
+        def turn_pairs(paired, grouped, bank_name, in_slot_order=False):
             words = paired.bitcast(F32)
             bank = psum.tile([P, PAIR, P], F32, name=bank_name)
             for u in range(PAIR):
-                nc.tensor.transpose(bank[:, u, :], words[:, u * P : (u + 1) * P], ident[:])
+                run = words[:, u::PAIR] if in_slot_order else words[:, u * P : (u + 1) * P]
+                nc.tensor.transpose(bank[:, u, :], run, ident[:])
             grouped_words = grouped.rearrange("p x t -> p (x t)").bitcast(F32).rearrange("p (x u) -> p x u", u=PAIR)
             nc.scalar.copy(grouped_words, bank[:].rearrange(SIDE_BY_SIDE))
 
@@ -224,10 +226,9 @@ def tile_attend_mod_sorted_kernel(tc, xq, kT, vT, vs, offs, qoffs, out):
         prob3 = softmax(3, "u e s")
         nc.scalar.activation(total[:, 0:1], half_total[:, 0:1], IDENTITY, bias=half_total[:, 1:2])
 
-        def gather_second_values(h):
-            partitions_to_be = slice(h * P // HALVES, (h + 1) * P // HALVES)
-            picked = v_windows[1][:].indirect(entries(k_list, h * HALF_N, HALF_N))
-            nc.vector.tensor_copy(by_slot(v1_paired)[:, partitions_to_be], picked)
+        def gather_second_values(first, count):
+            picked = v_windows[1][:].indirect(entries(k_list, first, count))
+            nc.vector.tensor_copy(v1_paired[:, first : first + count], picked)
 
         def spread_inverse(h, bank_name):
             bank = psum.tile([P, CHUNKS_PER_HALF, P], F32, name=bank_name)
@@ -259,7 +260,7 @@ def tile_attend_mod_sorted_kernel(tc, xq, kT, vT, vs, offs, qoffs, out):
         v_tile = sbuf([P, 2 * N - v_overlap], BF16, "prob1")
         v1_paired = v_tile[:, 0:N]
         v0_grouped = v_tile[:, N - v_overlap :].rearrange("p (x t) -> p x t", t=PACK)
-        gather_second_values(0)
+        gather_second_values(0, V_EARLY)
         turn_pairs(weights0[:], w_grouped[0][:, 0:P, :], "bank1")
         turn_pairs(v0_paired[:], v0_grouped, "bank0")
         turned3 = turn_probs(prob3, "bank7")
@@ -273,11 +274,11 @@ def tile_attend_mod_sorted_kernel(tc, xq, kT, vT, vs, offs, qoffs, out):
         first_chunks = [columns(w_halves[0], i * P, P) for i in range(CHUNKS_PER_HALF)]
         sums00 = weighted_sums(values0, first_chunks, "sums00", ("bank2", "bank3"))
         multiply_on_vector(turned3, w_grouped[1][:, P:HALF_Q, :])
-        gather_second_values(1)
+        gather_second_values(V_EARLY, N - V_EARLY)
         quantize(w_grouped[1][:], w_halves[1])
 
         v1_grouped = sbuf([P, P, PACK], BF16, "v1_grouped")
-        turn_pairs(v1_paired, v1_grouped[:], "bank2")
+        turn_pairs(v1_paired, v1_grouped[:], "bank2", True)
         spread_inverse(1, "bank3")
         whole_halves = [columns(half, 0, HALF_Q) for half in w_halves]
         sums01 = weighted_sums(values0, whole_halves[1:], "prob1", ("bank4",))

@@ -12,8 +12,7 @@ FP8X4 = mybir.dt.float8_e4m3fn_x4
 EXP = mybir.ActivationFunctionType.Exp
 MULT = mybir.AluOpType.mult
 MAX = mybir.AluOpType.max
-MIN = mybir.AluOpType.min
-IDENTITY = mybir.ActivationFunctionType.Identity
+COPY = mybir.ActivationFunctionType.Copy
 AXIS_X = mybir.AxisListType.X
 
 P = 128
@@ -31,9 +30,7 @@ HALVES = 2
 HALF_Q = NQ // HALVES
 HALF_N = N // HALVES
 CHUNKS_PER_HALF = Q_CHUNKS // HALVES
-V_EARLY = 320
 ALIGN = 256
-MX_ALIGN = 64
 SIDE_BY_SIDE = "p t x -> p x t"
 
 FLOPS = 2 * NQ * N * D + 2 * NQ * N * DV
@@ -44,7 +41,6 @@ def tile_attend_mod_sorted_kernel(tc, xq, kT, vT, vs, offs, qoffs, out):
     nc = tc.nc
     with ExitStack() as ctx:
         keep = ctx.enter_context(tc.tile_pool(name="keep", bufs=1))
-        shared = ctx.enter_context(tc.tile_pool(name="shared", bufs=1))
         psum = ctx.enter_context(tc.psum_pool(name="psum", bufs=1))
 
         def sbuf(shape, dtype, name):
@@ -87,14 +83,14 @@ def tile_attend_mod_sorted_kernel(tc, xq, kT, vT, vs, offs, qoffs, out):
             )
             return bank
 
-        def turn_pairs(paired, grouped, bank_name, in_slot_order=False):
+        def turn_pairs(paired, grouped, bank_name, in_slot_order, copy):
             words = paired.bitcast(F32)
             bank = psum.tile([P, PAIR, P], F32, name=bank_name)
             for u in range(PAIR):
                 run = words[:, u::PAIR] if in_slot_order else words[:, u * P : (u + 1) * P]
                 nc.tensor.transpose(bank[:, u, :], run, ident[:])
             grouped_words = grouped.rearrange("p x t -> p (x t)").bitcast(F32).rearrange("p (x u) -> p x u", u=PAIR)
-            nc.scalar.copy(grouped_words, bank[:].rearrange(SIDE_BY_SIDE))
+            copy(grouped_words, bank[:].rearrange(SIDE_BY_SIDE))
 
         k_list = sbuf([P, N // PER_LIST_COLUMN], U16, "k_list")
         q_list = sbuf([P, NQ // PER_LIST_COLUMN], U16, "q_list")
@@ -130,14 +126,6 @@ def tile_attend_mod_sorted_kernel(tc, xq, kT, vT, vs, offs, qoffs, out):
             nc.tensor.transpose(column_bank[:, t, :], vs_picked[:, t::PACK], ident[:])
         vs_column = sbuf([P, PACK], F32, "vs_column")
         nc.scalar.copy(vs_column[:], column_bank[:, :, 0])
-        row_bank = psum.tile([P, PACK, P], F32, name="bank5")
-        for t in range(PACK):
-            nc.tensor.transpose(row_bank[:, t, :], vs_column[:, t : t + 1].to_broadcast([P, P]), ident[:])
-        vs_row = sbuf([P, N], F32, "vs_row")
-        nc.scalar.copy(
-            vs_row[:].rearrange("p (u s e) -> p u s e", u=PAIR, e=PAIR),
-            row_bank[:].rearrange("p (u e) s -> p u s e", e=PAIR),
-        )
 
         for t in range(1, PACK):
             nc.vector.tensor_copy(by_slot(k_grouped[:, :, t]), k_planes[t][:].indirect(k_list[:]))
@@ -153,54 +141,38 @@ def tile_attend_mod_sorted_kernel(tc, xq, kT, vT, vs, offs, qoffs, out):
         def q_chunks(first, count):
             return q_grouped[:, first * P : (first + count) * P, :]
 
-        run0 = shared.tile([P, 2 * P], BF16, align_bytes=MX_ALIGN, offset=0, name="run0")
-        for first in range(0, P, P // 2):
-            half = slice(first, first + P // 2)
-            nc.vector.tensor_copy(run0[:, half], last_plane(first, P // 2))
-            nc.scalar.copy(q_chunks(0, 1)[:, half, PACK - 1], run0[:, half])
-        nc.vector.tensor_copy(q_chunks(1, 2)[:, :, PACK - 1], last_plane(P, 2 * P))
-        q0 = quantize(q_chunks(0, 1), mx_tiles(P, "q0"))
-        scores0 = [
-            product(name, columns(q0, 0, P), columns(keys, h * HALF_N, HALF_N)) for h, name in enumerate(("bank0", "bank4"))
-        ]
-        scores = [None]
-        run3 = shared.tile([P, P], BF16, align_bytes=MX_ALIGN, offset=0, name="run3")
+        run0 = sbuf([P, P], BF16, "q_plane2")
         halves = [slice(first, first + P // 2) for first in range(0, P, P // 2)]
         for half in halves:
-            nc.vector.tensor_copy(run3[:, half], last_plane(3 * P + half.start, P // 2))
-        q12_codes = sbuf([P, 2 * P], U32, "q12_codes")
-        q12_scales = shared.tile([P, 2 * P], U8, align_bytes=MX_ALIGN, offset=2 * P, name="q12_scales")
-        q12 = quantize(q_chunks(1, 2), (q12_codes, q12_scales))
+            nc.scalar.activation(run0[:, half], last_plane(half.start, P // 2), COPY)
         for half in halves:
-            nc.scalar.copy(q_chunks(3, 1)[:, half, PACK - 1], run3[:, half])
+            nc.scalar.copy(q_chunks(0, 1)[:, half, PACK - 1], run0[:, half])
+        nc.vector.tensor_copy(q_chunks(1, 2)[:, :, PACK - 1], last_plane(P, 2 * P))
+        run3 = sbuf([P, P], BF16, "run3")
+        nc.vector.tensor_copy(run3[:], last_plane(3 * P, P))
+        nc.scalar.copy(q_chunks(3, 1)[:, :, PACK - 1], run3[:])
+        q0 = quantize(q_chunks(0, 1), mx_tiles(P, "q0"))
+        scores = [product("bank0", columns(q0, 0, P), keys)]
+        q12 = quantize(q_chunks(1, 2), mx_tiles(2 * P, "q12"))
         scores.extend([product("bank%d" % (1 + i), columns(q12, i * P, P), keys) for i in range(2)])
-        half_max = sbuf([P, 1], F32, "half_max")
-        nc.vector.tensor_reduce(half_max[:], scores0[0][:], AXIS_X, MAX, negate=True)
-        q3 = columns(quantize(q_chunks(3, 1), mx_tiles(P, "q3", "q0_codes")), 0, P)
-        scores.append(product("bank3", q3, keys))
+        q3 = quantize(q_chunks(3, 1), mx_tiles(P, "q3"))
+        scores.append(product("bank3", columns(q3, 0, P), keys))
 
-        product("bank7", q3, keys)
-        product("bank5", q3, columns(keys, 0, HALF_N))
+        neg_max = [sbuf([P, 1], F32, "neg_max%d" % b)[:] for b in range(Q_CHUNKS)]
 
-        total = sbuf([P, Q_CHUNKS], F32, "total")
-        neg_max = [sbuf([P, 1], F32, "neg_max%d" % b)[:] if b != 2 else total[:, 0:1] for b in range(Q_CHUNKS)]
-
-        def softmax(b, order):
+        def maximum(b):
             nc.vector.tensor_reduce(neg_max[b], scores[b][:], AXIS_X, MAX, negate=True)
+
+        def probabilities(b):
             prob = sbuf([P, N], F32, "prob%d" % b)
             nc.scalar.activation(
-                prob[:].rearrange("p (%s) -> p %s" % (order, order), u=PAIR, e=PAIR),
-                scores[b][:].rearrange("p (u s e) -> p %s" % order, u=PAIR, e=PAIR),
+                prob[:].rearrange("p (u e s) -> p u e s", u=PAIR, e=PAIR),
+                scores[b][:].rearrange("p (u s e) -> p u e s", u=PAIR, e=PAIR),
                 EXP,
                 bias=neg_max[b],
                 accum_out=total[:, b : b + 1],
             )
             return prob
-
-        def multiply_on_gpsimd(prob, name):
-            weights = sbuf([P, N], BF16, name)
-            nc.gpsimd.tensor_tensor(weights[:], prob[:], vs_row[:], MULT)
-            return weights
 
         def turn_probs(prob, bank_name):
             bank = psum.tile([P, PACK, P], F32, name=bank_name)
@@ -212,80 +184,71 @@ def tile_attend_mod_sorted_kernel(tc, xq, kT, vT, vs, offs, qoffs, out):
             scales = vs_column[:].unsqueeze(1).to_broadcast([P, P, PACK])
             nc.vector.tensor_tensor(grouped, turned[:].rearrange(SIDE_BY_SIDE), scales, MULT)
 
-        negated = sbuf([P, HALF_N], F32, "negated")
-        nc.vector.tensor_scalar(negated[:], scores0[1][:], -1.0, half_max[:], MULT, MIN, accum_out=neg_max[0])
-        prob0 = sbuf([P, N], F32, "prob0")
-        half_total = sbuf([P, HALVES], F32, "half_total")
-        nc.scalar.activation(prob0[:, 0:HALF_N], scores0[0][:], EXP, bias=neg_max[0], accum_out=half_total[:, 0:1])
-        nc.scalar.activation(
-            prob0[:, HALF_N:N], negated[:], EXP, bias=neg_max[0], scale=-1.0, accum_out=half_total[:, 1:2]
-        )
-        weights0 = multiply_on_gpsimd(prob0, "weights0")
-        turned1 = turn_probs(softmax(1, "u e s"), "bank6")
-        weights2 = multiply_on_gpsimd(softmax(2, "u s e"), "weights2")
-        prob3 = softmax(3, "u e s")
-        nc.scalar.activation(total[:, 0:1], half_total[:, 0:1], IDENTITY, bias=half_total[:, 1:2])
+        def values_at(e, first, count):
+            return v_windows[e][:].indirect(entries(k_list, first, count))
 
-        def gather_second_values(first, count):
-            picked = v_windows[1][:].indirect(entries(k_list, first, count))
-            nc.vector.tensor_copy(v1_paired[:, first : first + count], picked)
+        inverse = [sbuf([P, HALF_Q], F32, "inverse%d" % h) for h in range(HALVES)]
 
-        def spread_inverse(h, bank_name):
+        def invert(h):
+            inv_total = sbuf([P, CHUNKS_PER_HALF], F32, "inv_total%d" % h)
+            nc.vector.reciprocal(inv_total[:], total[:, h * CHUNKS_PER_HALF : (h + 1) * CHUNKS_PER_HALF])
+            return inv_total
+
+        def spread(inv_total, h, bank_name):
             bank = psum.tile([P, CHUNKS_PER_HALF, P], F32, name=bank_name)
             for i in range(CHUNKS_PER_HALF):
-                b = h * CHUNKS_PER_HALF + i
-                nc.tensor.transpose(bank[:, i, :], inv_total[:, b : b + 1].to_broadcast([P, P]), ident[:])
-            nc.scalar.copy(inverse[:, h * HALF_Q : (h + 1) * HALF_Q], bank[:].rearrange("p b q -> p (b q)"))
+                nc.tensor.transpose(bank[:, i, :], inv_total[:, i : i + 1].to_broadcast([P, P]), ident[:])
+            nc.scalar.copy(inverse[h][:], bank[:].rearrange("p b q -> p (b q)"))
 
-        def weighted_sums(values, runs, name, bank_names):
-            width = runs[0][0].shape[1]
-            sums = sbuf([P, len(runs) * width], F32, name)
-            for i, bank_name in enumerate(bank_names):
-                bank = product(bank_name, columns(values, 0, P), runs[i])
-                nc.scalar.copy(sums[:, i * width : (i + 1) * width], bank[:])
-            return sums
+        v0_run = sbuf([P, N], BF16, "v0_run")
+        nc.scalar.activation(v0_run[:], values_at(0, 0, N), COPY)
+        total = sbuf([P, Q_CHUNKS], F32, "v_window0")
+        for b in range(Q_CHUNKS):
+            maximum(b)
+        turned0 = turn_probs(probabilities(0), "bank4")
+        turned1 = turn_probs(probabilities(1), "bank6")
+        v_grouped = [sbuf([P, P, PACK], BF16, "v_grouped%d" % e) for e in range(V_CHUNKS)]
+        turn_pairs(v0_run[:], v_grouped[0][:], "bank7", True, nc.scalar.copy)
+        turned2 = turn_probs(probabilities(2), "bank5")
+        spread(invert(0), 0, "bank0")
+        turned3 = turn_probs(probabilities(3), "bank1")
 
-        def put_back(e, first, count, sums):
-            window = out_windows[e][:].indirect(entries(q_list, first, count))
-            nc.vector.tensor_tensor(window, sums[:], inverse[:, first : first + count], MULT)
-
-        v0_paired = sbuf([P, N], BF16, "neg_max1")
-        nc.vector.tensor_copy(by_slot(v0_paired[:]), v_windows[0][:].indirect(k_list[:]))
         w_grouped = [sbuf([P, HALF_Q, PACK], BF16, "w_grouped%d" % h) for h in range(HALVES)]
+        multiply_on_vector(turned0, w_grouped[0][:, 0:P, :])
         multiply_on_vector(turned1, w_grouped[0][:, P:HALF_Q, :])
-        inv_total = sbuf([P, Q_CHUNKS], F32, "inv_total")
-        nc.vector.reciprocal(inv_total[:], total[:])
+        values0 = columns(quantize(v_grouped[0][:], mx_tiles(P, "v0", "neg_max2")), 0, P)
 
-        v_overlap = N // 4
-        v_tile = sbuf([P, 2 * N - v_overlap], BF16, "prob1")
-        v1_paired = v_tile[:, 0:N]
-        v0_grouped = v_tile[:, N - v_overlap :].rearrange("p (x t) -> p x t", t=PACK)
-        gather_second_values(0, V_EARLY)
-        turn_pairs(weights0[:], w_grouped[0][:, 0:P, :], "bank1")
-        turn_pairs(v0_paired[:], v0_grouped, "bank0")
-        turned3 = turn_probs(prob3, "bank7")
-        inverse = sbuf([P, NQ], F32, "inverse")
-        spread_inverse(0, "bank4")
-        turn_pairs(weights2[:], w_grouped[1][:, 0:P, :], "bank1")
+        def window(e, h):
+            return out_windows[e][:].indirect(entries(q_list, h * HALF_Q, HALF_Q))
+
+        def divided(bank, h, name):
+            result = sbuf([P, HALF_Q], F32, name)
+            nc.vector.tensor_tensor(result[:], bank[:], inverse[h][:], MULT)
+            return result
 
         w_halves = [mx_tiles(HALF_Q, "w_half%d" % h) for h in range(HALVES)]
-        quantize(w_grouped[0][:], w_halves[0])
-        values0 = quantize(v0_grouped, mx_tiles(P, "v0"))
-        first_chunks = [columns(w_halves[0], i * P, P) for i in range(CHUNKS_PER_HALF)]
-        sums00 = weighted_sums(values0, first_chunks, "sums00", ("bank2", "bank3"))
-        multiply_on_vector(turned3, w_grouped[1][:, P:HALF_Q, :])
-        gather_second_values(V_EARLY, N - V_EARLY)
-        quantize(w_grouped[1][:], w_halves[1])
-
-        v1_grouped = sbuf([P, P, PACK], BF16, "v1_grouped")
-        turn_pairs(v1_paired, v1_grouped[:], "bank2", True)
-        spread_inverse(1, "bank3")
         whole_halves = [columns(half, 0, HALF_Q) for half in w_halves]
-        sums01 = weighted_sums(values0, whole_halves[1:], "prob1", ("bank4",))
-        put_back(0, 0, HALF_Q, sums00)
-        values1 = quantize(v1_grouped[:], mx_tiles(P, "v1"))
-        sums1 = weighted_sums(values1, whole_halves, "sums1", ("bank3", "bank6"))
-        put_back(0, HALF_Q, HALF_Q, sums01)
+        quantize(w_grouped[0][:], w_halves[0])
+        sums00 = product("bank2", values0, whole_halves[0])
+        multiply_on_vector(turned2, w_grouped[1][:, 0:P, :])
+        spread(invert(1), 1, "bank3")
+        v1_run = sbuf([P, N], BF16, "neg_max3")
+        nc.scalar.activation(v1_run[:], values_at(1, 0, N), COPY)
+        result00 = divided(sums00, 0, "result00")
+        nc.scalar.activation(window(0, 0), result00[:], COPY)
+        multiply_on_vector(turned3, w_grouped[1][:, P:HALF_Q, :])
+        quantize(w_grouped[1][:], w_halves[1])
+        sums01 = product("bank6", values0, whole_halves[1])
+        turn_pairs(v1_run[:], v_grouped[1][:], "bank1", True, nc.vector.tensor_copy)
+        result01 = divided(sums01, 1, "result01")
+        nc.scalar.activation(window(0, 1), result01[:], COPY)
         nc.sync.dma_start(out[0:P, :], out_windows[0][:])
-        put_back(1, 0, NQ, sums1)
+        values1 = columns(quantize(v_grouped[1][:], mx_tiles(P, "v1")), 0, P)
+        sums10 = product("bank0", values1, whole_halves[0])
+        sums11 = product("bank7", values1, whole_halves[1])
+        result10 = divided(sums10, 0, "result10")
+        nc.vector.tensor_copy(window(1, 0), result10[:])
+        undivided = sbuf([P, HALF_Q], F32, "undivided")
+        nc.scalar.copy(undivided[:], sums11[:])
+        nc.vector.tensor_tensor(window(1, 1), undivided[:], inverse[1][:], MULT)
         nc.sync.dma_start(out[P:DV, :], out_windows[1][:])

@@ -41,10 +41,14 @@ def tile_attend_mod_sorted_kernel(tc, xq, kT, vT, vs, offs, qoffs, out):
     nc = tc.nc
     with ExitStack() as ctx:
         keep = ctx.enter_context(tc.tile_pool(name="keep", bufs=1))
+        shared = ctx.enter_context(tc.tile_pool(name="shared", bufs=1))
         psum = ctx.enter_context(tc.psum_pool(name="psum", bufs=1))
 
         def sbuf(shape, dtype, name):
             return keep.tile(shape, dtype, align_bytes=ALIGN, name=name)
+
+        def on_plane2(shape, dtype, offset, name):
+            return shared.tile(shape, dtype, align_bytes=ALIGN, offset=offset, name=name)
 
         def load(rows, name):
             tile = sbuf(list(rows.shape), F32, name)
@@ -83,14 +87,19 @@ def tile_attend_mod_sorted_kernel(tc, xq, kT, vT, vs, offs, qoffs, out):
             )
             return bank
 
-        def turn_pairs(paired, grouped, bank_name, in_slot_order, copy):
+        def pair_bank(bank_name):
+            return psum.tile([P, PAIR, P], F32, name=bank_name)[:]
+
+        def turn_pairs(paired, bank, in_slot_order=False):
             words = paired.bitcast(F32)
-            bank = psum.tile([P, PAIR, P], F32, name=bank_name)
             for u in range(PAIR):
                 run = words[:, u::PAIR] if in_slot_order else words[:, u * P : (u + 1) * P]
                 nc.tensor.transpose(bank[:, u, :], run, ident[:])
+            return bank
+
+        def copy_pairs(copy, turned, grouped):
             grouped_words = grouped.rearrange("p x t -> p (x t)").bitcast(F32).rearrange("p (x u) -> p x u", u=PAIR)
-            copy(grouped_words, bank[:].rearrange(SIDE_BY_SIDE))
+            copy(grouped_words, turned.rearrange(SIDE_BY_SIDE))
 
         k_list = sbuf([P, N // PER_LIST_COLUMN], U16, "k_list")
         q_list = sbuf([P, NQ // PER_LIST_COLUMN], U16, "q_list")
@@ -113,7 +122,10 @@ def tile_attend_mod_sorted_kernel(tc, xq, kT, vT, vs, offs, qoffs, out):
         nc.sync.dma_start(vs_window[0:1, :], vs[0:1, :])
         k_planes.extend([load(k_rows[:, t, :], "k_plane%d" % t) for t in range(2, PACK)])
         nc.sync.dma_start(q_list[:], qoffs)
-        q_planes = [load(q_rows[:, t, :], "q_plane%d" % t) for t in range(PACK)]
+        q_planes = [load(q_rows[:, t, :], "q_plane%d" % t) for t in range(2)]
+        q_planes.append(on_plane2([P, T], F32, 0, "q_plane2"))
+        nc.sync.dma_start(q_planes[2][:], q_rows[:, 2, :])
+        q_planes.append(load(q_rows[:, 3, :], "q_plane3"))
         v_windows = [load(vT[e * P : (e + 1) * P, :], "v_window%d" % e) for e in range(V_CHUNKS)]
 
         k_grouped = sbuf([P, N, PACK], BF16, "k_grouped")
@@ -126,6 +138,14 @@ def tile_attend_mod_sorted_kernel(tc, xq, kT, vT, vs, offs, qoffs, out):
             nc.tensor.transpose(column_bank[:, t, :], vs_picked[:, t::PACK], ident[:])
         vs_column = sbuf([P, PACK], F32, "vs_column")
         nc.scalar.copy(vs_column[:], column_bank[:, :, 0])
+        row_bank = psum.tile([P, PACK, P], F32, name="bank5")
+        for t in range(PACK):
+            nc.tensor.transpose(row_bank[:, t, :], vs_column[:, t : t + 1].to_broadcast([P, P]), ident[:])
+        vs_row = sbuf([P, N], F32, "vs_row")
+        nc.scalar.copy(
+            vs_row[:].rearrange("p (u s e) -> p u s e", u=PAIR, e=PAIR),
+            row_bank[:].rearrange("p (u e) s -> p u s e", e=PAIR),
+        )
 
         for t in range(1, PACK):
             nc.vector.tensor_copy(by_slot(k_grouped[:, :, t]), k_planes[t][:].indirect(k_list[:]))
@@ -141,19 +161,18 @@ def tile_attend_mod_sorted_kernel(tc, xq, kT, vT, vs, offs, qoffs, out):
         def q_chunks(first, count):
             return q_grouped[:, first * P : (first + count) * P, :]
 
-        run0 = sbuf([P, P], BF16, "q_plane2")
-        halves = [slice(first, first + P // 2) for first in range(0, P, P // 2)]
-        for half in halves:
-            nc.scalar.activation(run0[:, half], last_plane(half.start, P // 2), COPY)
-        for half in halves:
-            nc.scalar.copy(q_chunks(0, 1)[:, half, PACK - 1], run0[:, half])
+        run0 = [on_plane2([P, P // 2], BF16, i * ALIGN, "run0_%d" % i) for i in range(2)]
+        for i in range(2):
+            nc.scalar.activation(run0[i][:], last_plane(i * P // 2, P // 2), COPY)
+        for i in range(2):
+            nc.scalar.copy(q_grouped[:, i * P // 2 : (i + 1) * P // 2, PACK - 1], run0[i][:])
         nc.vector.tensor_copy(q_chunks(1, 2)[:, :, PACK - 1], last_plane(P, 2 * P))
-        run3 = sbuf([P, P], BF16, "run3")
-        nc.vector.tensor_copy(run3[:], last_plane(3 * P, P))
-        nc.scalar.copy(q_chunks(3, 1)[:, :, PACK - 1], run3[:])
         q0 = quantize(q_chunks(0, 1), mx_tiles(P, "q0"))
         scores = [product("bank0", columns(q0, 0, P), keys)]
-        q12 = quantize(q_chunks(1, 2), mx_tiles(2 * P, "q12"))
+        run3 = on_plane2([P, P], BF16, 0, "run3")
+        nc.scalar.activation(run3[:], last_plane(3 * P, P), COPY)
+        nc.scalar.copy(q_chunks(3, 1)[:, :, PACK - 1], run3[:])
+        q12 = quantize(q_chunks(1, 2), (sbuf([P, 2 * P], U32, "q12_codes"), on_plane2([P, 2 * P], U8, ALIGN, "q12_scales")))
         scores.extend([product("bank%d" % (1 + i), columns(q12, i * P, P), keys) for i in range(2)])
         q3 = quantize(q_chunks(3, 1), mx_tiles(P, "q3"))
         scores.append(product("bank3", columns(q3, 0, P), keys))
@@ -163,11 +182,11 @@ def tile_attend_mod_sorted_kernel(tc, xq, kT, vT, vs, offs, qoffs, out):
         def maximum(b):
             nc.vector.tensor_reduce(neg_max[b], scores[b][:], AXIS_X, MAX, negate=True)
 
-        def probabilities(b):
+        def probabilities(b, order):
             prob = sbuf([P, N], F32, "prob%d" % b)
             nc.scalar.activation(
-                prob[:].rearrange("p (u e s) -> p u e s", u=PAIR, e=PAIR),
-                scores[b][:].rearrange("p (u s e) -> p u e s", u=PAIR, e=PAIR),
+                prob[:].rearrange("p (%s) -> p %s" % (order, order), u=PAIR, e=PAIR),
+                scores[b][:].rearrange("p (u s e) -> p %s" % order, u=PAIR, e=PAIR),
                 EXP,
                 bias=neg_max[b],
                 accum_out=total[:, b : b + 1],
@@ -189,34 +208,22 @@ def tile_attend_mod_sorted_kernel(tc, xq, kT, vT, vs, offs, qoffs, out):
 
         inverse = [sbuf([P, HALF_Q], F32, "inverse%d" % h) for h in range(HALVES)]
 
-        def invert(h):
-            inv_total = sbuf([P, CHUNKS_PER_HALF], F32, "inv_total%d" % h)
-            nc.vector.reciprocal(inv_total[:], total[:, h * CHUNKS_PER_HALF : (h + 1) * CHUNKS_PER_HALF])
-            return inv_total
-
-        def spread(inv_total, h, bank_name):
-            bank = psum.tile([P, CHUNKS_PER_HALF, P], F32, name=bank_name)
+        def spread(h, bank):
             for i in range(CHUNKS_PER_HALF):
-                nc.tensor.transpose(bank[:, i, :], inv_total[:, i : i + 1].to_broadcast([P, P]), ident[:])
-            nc.scalar.copy(inverse[h][:], bank[:].rearrange("p b q -> p (b q)"))
+                b = h * CHUNKS_PER_HALF + i
+                nc.tensor.transpose(bank[:, i, :], inv_total[:, b : b + 1].to_broadcast([P, P]), ident[:])
+            return bank.rearrange("p b q -> p (b q)")
 
         v0_run = sbuf([P, N], BF16, "v0_run")
         nc.scalar.activation(v0_run[:], values_at(0, 0, N), COPY)
         total = sbuf([P, Q_CHUNKS], F32, "v_window0")
         for b in range(Q_CHUNKS):
             maximum(b)
-        turned0 = turn_probs(probabilities(0), "bank4")
-        turned1 = turn_probs(probabilities(1), "bank6")
-        v_grouped = [sbuf([P, P, PACK], BF16, "v_grouped%d" % e) for e in range(V_CHUNKS)]
-        turn_pairs(v0_run[:], v_grouped[0][:], "bank7", True, nc.scalar.copy)
-        turned2 = turn_probs(probabilities(2), "bank5")
-        spread(invert(0), 0, "bank0")
-        turned3 = turn_probs(probabilities(3), "bank1")
 
-        w_grouped = [sbuf([P, HALF_Q, PACK], BF16, "w_grouped%d" % h) for h in range(HALVES)]
-        multiply_on_vector(turned0, w_grouped[0][:, 0:P, :])
-        multiply_on_vector(turned1, w_grouped[0][:, P:HALF_Q, :])
-        values0 = columns(quantize(v_grouped[0][:], mx_tiles(P, "v0", "neg_max2")), 0, P)
+        def multiply_on_gpsimd(prob, name):
+            weights = sbuf([P, N], BF16, name)
+            nc.gpsimd.tensor_tensor(weights[:], prob[:], vs_row[:], MULT)
+            return weights
 
         def window(e, h):
             return out_windows[e][:].indirect(entries(q_list, h * HALF_Q, HALF_Q))
@@ -226,29 +233,48 @@ def tile_attend_mod_sorted_kernel(tc, xq, kT, vT, vs, offs, qoffs, out):
             nc.vector.tensor_tensor(result[:], bank[:], inverse[h][:], MULT)
             return result
 
+        weights0 = multiply_on_gpsimd(probabilities(0, "u s e"), "weights0")
+        turned1 = turn_probs(probabilities(1, "u e s"), "bank6")
+        weights2 = multiply_on_gpsimd(probabilities(2, "u s e"), "weights2")
+        prob3 = probabilities(3, "u e s")
+
+        v_grouped = [sbuf([P, P, PACK], BF16, "v_grouped%d" % e) for e in range(V_CHUNKS)]
+        w_grouped = [sbuf([P, HALF_Q, PACK], BF16, "w_grouped%d" % h) for h in range(HALVES)]
         w_halves = [mx_tiles(HALF_Q, "w_half%d" % h) for h in range(HALVES)]
         whole_halves = [columns(half, 0, HALF_Q) for half in w_halves]
+        v1_paired = sbuf([P, N], BF16, "v1_paired")
+        nc.vector.tensor_copy(by_slot(v1_paired[:]), values_at(1, 0, N))
+        v0_turned = turn_pairs(v0_run[:], pair_bank("bank7"), True)
+        copy_pairs(nc.scalar.copy, turn_pairs(weights0[:], pair_bank("bank1")), w_grouped[0][:, 0:P, :])
+        copy_pairs(nc.scalar.copy, v0_turned, v_grouped[0][:])
+        multiply_on_vector(turned1, w_grouped[0][:, P:HALF_Q, :])
+        inv_total = sbuf([P, Q_CHUNKS], F32, "v_window1")
+        nc.vector.reciprocal(inv_total[:], total[:])
+        turned3 = turn_probs(prob3, "bank5")
+        nc.scalar.copy(inverse[0][:], spread(0, pair_bank("bank0")))
+        copy_pairs(nc.scalar.copy, turn_pairs(weights2[:], pair_bank("bank1")), w_grouped[1][:, 0:P, :])
         quantize(w_grouped[0][:], w_halves[0])
+        values0 = columns(quantize(v_grouped[0][:], mx_tiles(P, "v0", "neg_max3")), 0, P)
         sums00 = product("bank2", values0, whole_halves[0])
-        multiply_on_vector(turned2, w_grouped[1][:, 0:P, :])
-        spread(invert(1), 1, "bank3")
-        v1_run = sbuf([P, N], BF16, "neg_max3")
-        nc.scalar.activation(v1_run[:], values_at(1, 0, N), COPY)
+        multiply_on_vector(turned3, w_grouped[1][:, P:HALF_Q, :])
         result00 = divided(sums00, 0, "result00")
         nc.scalar.activation(window(0, 0), result00[:], COPY)
-        multiply_on_vector(turned3, w_grouped[1][:, P:HALF_Q, :])
+        late_bank = psum.tile([P, 2 * PAIR, P], F32, name="bank5")
+        v1_turned = turn_pairs(v1_paired[:], late_bank[:, 0:PAIR, :])
+        spread1 = spread(1, late_bank[:, PAIR : 2 * PAIR, :])
         quantize(w_grouped[1][:], w_halves[1])
         sums01 = product("bank6", values0, whole_halves[1])
-        turn_pairs(v1_run[:], v_grouped[1][:], "bank1", True, nc.vector.tensor_copy)
+        copy_pairs(nc.vector.tensor_copy, v1_turned, v_grouped[1][:])
+        nc.vector.tensor_copy(inverse[1][:], spread1)
+        values1 = columns(quantize(v_grouped[1][:], mx_tiles(P, "v1")), 0, P)
+        sums10 = product("bank7", values1, whole_halves[0])
+        sums11 = product("bank4", values1, whole_halves[1])
         result01 = divided(sums01, 1, "result01")
+        result10 = divided(sums10, 0, "result10")
         nc.scalar.activation(window(0, 1), result01[:], COPY)
         nc.sync.dma_start(out[0:P, :], out_windows[0][:])
-        values1 = columns(quantize(v_grouped[1][:], mx_tiles(P, "v1")), 0, P)
-        sums10 = product("bank0", values1, whole_halves[0])
-        sums11 = product("bank7", values1, whole_halves[1])
-        result10 = divided(sums10, 0, "result10")
-        nc.vector.tensor_copy(window(1, 0), result10[:])
-        undivided = sbuf([P, HALF_Q], F32, "undivided")
+        undivided = sbuf([P, HALF_Q], F32, "result01")
         nc.scalar.copy(undivided[:], sums11[:])
+        nc.vector.tensor_copy(window(1, 0), result10[:])
         nc.vector.tensor_tensor(window(1, 1), undivided[:], inverse[1][:], MULT)
         nc.sync.dma_start(out[P:DV, :], out_windows[1][:])

@@ -31,6 +31,8 @@ HALF_Q = NQ // HALVES
 HALF_N = N // HALVES
 CHUNKS_PER_HALF = Q_CHUNKS // HALVES
 ALIGN = 256
+V_WINDOW1 = 4 * T
+V_RUN1 = V_WINDOW1 + 4 * T
 SIDE_BY_SIDE = "p t x -> p x t"
 
 FLOPS = 2 * NQ * N * D + 2 * NQ * N * DV
@@ -48,6 +50,9 @@ def tile_attend_mod_sorted_kernel(tc, xq, kT, vT, vs, offs, qoffs, out):
             return keep.tile(shape, dtype, align_bytes=ALIGN, name=name)
 
         def on_plane2(shape, dtype, offset, name):
+            return shared.tile(shape, dtype, align_bytes=ALIGN, offset=offset, name=name)
+
+        def placed(shape, dtype, offset, name):
             return shared.tile(shape, dtype, align_bytes=ALIGN, offset=offset, name=name)
 
         def load(rows, name):
@@ -126,7 +131,8 @@ def tile_attend_mod_sorted_kernel(tc, xq, kT, vT, vs, offs, qoffs, out):
         q_planes.append(on_plane2([P, T], F32, 0, "q_plane2"))
         nc.sync.dma_start(q_planes[2][:], q_rows[:, 2, :])
         q_planes.append(load(q_rows[:, 3, :], "q_plane3"))
-        v_windows = [load(vT[e * P : (e + 1) * P, :], "v_window%d" % e) for e in range(V_CHUNKS)]
+        v_windows = [load(vT[0:P, :], "v_window0"), placed([P, T], F32, V_WINDOW1, "v_window1")]
+        nc.sync.dma_start(v_windows[1][:], vT[P:DV, :])
 
         k_grouped = sbuf([P, N, PACK], BF16, "k_grouped")
         nc.vector.tensor_copy(by_slot(k_grouped[:, :, 0]), k_planes[0][:].indirect(k_list[:]))
@@ -177,7 +183,8 @@ def tile_attend_mod_sorted_kernel(tc, xq, kT, vT, vs, offs, qoffs, out):
         q3 = quantize(q_chunks(3, 1), mx_tiles(P, "q3"))
         scores.append(product("bank3", columns(q3, 0, P), keys))
 
-        neg_max = [sbuf([P, 1], F32, "neg_max%d" % b)[:] for b in range(Q_CHUNKS)]
+        neg_max = [sbuf([P, 1], F32, "neg_max%d" % b)[:] for b in range(Q_CHUNKS - 1)]
+        neg_max.append(placed([P, 1], F32, V_RUN1 + 2 * ALIGN, "neg_max3")[:])
 
         def maximum(b):
             nc.vector.tensor_reduce(neg_max[b], scores[b][:], AXIS_X, MAX, negate=True)
@@ -210,71 +217,71 @@ def tile_attend_mod_sorted_kernel(tc, xq, kT, vT, vs, offs, qoffs, out):
 
         def spread(h, bank):
             for i in range(CHUNKS_PER_HALF):
-                b = h * CHUNKS_PER_HALF + i
-                nc.tensor.transpose(bank[:, i, :], inv_total[:, b : b + 1].to_broadcast([P, P]), ident[:])
+                nc.tensor.transpose(bank[:, i, :], inv_total[h][:, i : i + 1].to_broadcast([P, P]), ident[:])
             return bank.rearrange("p b q -> p (b q)")
 
-        v0_run = sbuf([P, N], BF16, "v0_run")
+        v0_run = placed([P, N], BF16, V_RUN1 + 3 * ALIGN, "v0_run")
         nc.scalar.activation(v0_run[:], values_at(0, 0, N), COPY)
         total = sbuf([P, Q_CHUNKS], F32, "v_window0")
         for b in range(Q_CHUNKS):
             maximum(b)
 
-        def multiply_on_gpsimd(prob, name):
-            weights = sbuf([P, N], BF16, name)
-            nc.gpsimd.tensor_tensor(weights[:], prob[:], vs_row[:], MULT)
-            return weights
+        inv_total = [sbuf([P, CHUNKS_PER_HALF], F32, "inv_total%d" % h) for h in range(HALVES)]
+
+        def reciprocal(h):
+            nc.vector.reciprocal(inv_total[h][:], total[:, h * CHUNKS_PER_HALF : (h + 1) * CHUNKS_PER_HALF])
 
         def window(e, h):
             return out_windows[e][:].indirect(entries(q_list, h * HALF_Q, HALF_Q))
 
-        def divided(bank, h, name):
-            result = sbuf([P, HALF_Q], F32, name)
+        def divide(result, bank, h):
             nc.vector.tensor_tensor(result[:], bank[:], inverse[h][:], MULT)
             return result
 
-        weights0 = multiply_on_gpsimd(probabilities(0, "u s e"), "weights0")
-        turned1 = turn_probs(probabilities(1, "u e s"), "bank6")
-        weights2 = multiply_on_gpsimd(probabilities(2, "u s e"), "weights2")
+        turned0 = turn_probs(probabilities(0, "u e s"), "bank4")
+        turned1 = turn_probs(probabilities(1, "u e s"), "bank5")
+        reciprocal(0)
+        spread0 = spread(0, pair_bank("bank6"))
+        weights2 = sbuf([P, N], BF16, "weights2")
+        nc.gpsimd.tensor_tensor(weights2[:], probabilities(2, "u s e")[:], vs_row[:], MULT)
         prob3 = probabilities(3, "u e s")
 
         v_grouped = [sbuf([P, P, PACK], BF16, "v_grouped%d" % e) for e in range(V_CHUNKS)]
-        w_grouped = [sbuf([P, HALF_Q, PACK], BF16, "w_grouped%d" % h) for h in range(HALVES)]
-        w_halves = [mx_tiles(HALF_Q, "w_half%d" % h) for h in range(HALVES)]
-        whole_halves = [columns(half, 0, HALF_Q) for half in w_halves]
-        v1_paired = sbuf([P, N], BF16, "v1_paired")
-        nc.vector.tensor_copy(by_slot(v1_paired[:]), values_at(1, 0, N))
-        v0_turned = turn_pairs(v0_run[:], pair_bank("bank7"), True)
-        copy_pairs(nc.scalar.copy, turn_pairs(weights0[:], pair_bank("bank1")), w_grouped[0][:, 0:P, :])
-        copy_pairs(nc.scalar.copy, v0_turned, v_grouped[0][:])
-        multiply_on_vector(turned1, w_grouped[0][:, P:HALF_Q, :])
-        inv_total = sbuf([P, Q_CHUNKS], F32, "v_window1")
-        nc.vector.reciprocal(inv_total[:], total[:])
-        turned3 = turn_probs(prob3, "bank5")
-        nc.scalar.copy(inverse[0][:], spread(0, pair_bank("bank0")))
-        copy_pairs(nc.scalar.copy, turn_pairs(weights2[:], pair_bank("bank1")), w_grouped[1][:, 0:P, :])
-        quantize(w_grouped[0][:], w_halves[0])
-        values0 = columns(quantize(v_grouped[0][:], mx_tiles(P, "v0", "neg_max3")), 0, P)
-        sums00 = product("bank2", values0, whole_halves[0])
-        multiply_on_vector(turned3, w_grouped[1][:, P:HALF_Q, :])
-        result00 = divided(sums00, 0, "result00")
+        w01_grouped = sbuf([P, HALF_Q, PACK], BF16, "w01_grouped")
+        multiply_on_vector(turned0, w01_grouped[:, 0:P, :])
+        multiply_on_vector(turned1, w01_grouped[:, P:HALF_Q, :])
+        copy_pairs(nc.scalar.copy, turn_pairs(v0_run[:], pair_bank("bank2"), True), v_grouped[0][:])
+        v1_run = placed([P, N], BF16, V_RUN1, "v1_run")
+        nc.scalar.activation(v1_run[:], values_at(1, 0, N), COPY)
+        nc.vector.tensor_copy(inverse[0][:], spread0)
+        turned3 = turn_probs(prob3, "bank7")
+        reciprocal(1)
+        spread1 = spread(1, pair_bank("bank3"))
+        w01 = columns(quantize(w01_grouped[:], mx_tiles(HALF_Q, "w01")), 0, HALF_Q)
+        values0 = columns(quantize(v_grouped[0][:], mx_tiles(P, "v0")), 0, P)
+        sums00 = product("bank1", values0, w01)
+        w2_grouped = placed([P, P, PACK], BF16, V_WINDOW1, "w2_grouped")
+        copy_pairs(nc.scalar.copy, turn_pairs(weights2[:], pair_bank("bank0")), w2_grouped[:])
+        nc.scalar.copy(inverse[1][:], spread1)
+        w3_grouped = sbuf([P, P, PACK], BF16, "w3_grouped")
+        multiply_on_vector(turned3, w3_grouped[:])
+        v1_turned = turn_pairs(v1_run[:], pair_bank("bank4"), True)
+        result00 = divide(placed([P, HALF_Q], F32, V_WINDOW1 + 4 * ALIGN, "result00"), sums00, 0)
         nc.scalar.activation(window(0, 0), result00[:], COPY)
-        late_bank = psum.tile([P, 2 * PAIR, P], F32, name="bank5")
-        v1_turned = turn_pairs(v1_paired[:], late_bank[:, 0:PAIR, :])
-        spread1 = spread(1, late_bank[:, PAIR : 2 * PAIR, :])
-        quantize(w_grouped[1][:], w_halves[1])
-        sums01 = product("bank6", values0, whole_halves[1])
         copy_pairs(nc.vector.tensor_copy, v1_turned, v_grouped[1][:])
-        nc.vector.tensor_copy(inverse[1][:], spread1)
+        w23_tiles = (sbuf([P, HALF_Q], U32, "w23_codes"), placed([P, HALF_Q], U8, V_RUN1 + ALIGN, "w23_scales"))
+        quantize(w3_grouped[:], columns(w23_tiles, P, P))
+        quantize(w2_grouped[:], columns(w23_tiles, 0, P))
+        w23 = columns(w23_tiles, 0, HALF_Q)
+        sums01 = product("bank5", values0, w23)
         values1 = columns(quantize(v_grouped[1][:], mx_tiles(P, "v1")), 0, P)
-        sums10 = product("bank7", values1, whole_halves[0])
-        sums11 = product("bank4", values1, whole_halves[1])
-        result01 = divided(sums01, 1, "result01")
-        result10 = divided(sums10, 0, "result10")
+        sums10 = product("bank6", values1, w01)
+        sums11 = product("bank7", values1, w23)
+        result01 = divide(sbuf([P, HALF_Q], F32, "result01"), sums01, 1)
         nc.scalar.activation(window(0, 1), result01[:], COPY)
         nc.sync.dma_start(out[0:P, :], out_windows[0][:])
-        undivided = sbuf([P, HALF_Q], F32, "result01")
-        nc.scalar.copy(undivided[:], sums11[:])
+        result10 = divide(sbuf([P, HALF_Q], F32, "result10"), sums10, 0)
+        result11 = divide(sbuf([P, HALF_Q], F32, "result11"), sums11, 1)
         nc.vector.tensor_copy(window(1, 0), result10[:])
-        nc.vector.tensor_tensor(window(1, 1), undivided[:], inverse[1][:], MULT)
+        nc.vector.tensor_copy(window(1, 1), result11[:])
         nc.sync.dma_start(out[P:DV, :], out_windows[1][:])

@@ -31,8 +31,7 @@ HALF_Q = NQ // HALVES
 HALF_N = N // HALVES
 CHUNKS_PER_HALF = Q_CHUNKS // HALVES
 ALIGN = 256
-V_WINDOW1 = 4 * T
-V_RUN1 = V_WINDOW1 + 4 * T
+V_RUN1 = 4 * T + 4 * ALIGN
 SIDE_BY_SIDE = "p t x -> p x t"
 
 FLOPS = 2 * NQ * N * D + 2 * NQ * N * DV
@@ -131,8 +130,7 @@ def tile_attend_mod_sorted_kernel(tc, xq, kT, vT, vs, offs, qoffs, out):
         q_planes.append(on_plane2([P, T], F32, 0, "q_plane2"))
         nc.sync.dma_start(q_planes[2][:], q_rows[:, 2, :])
         q_planes.append(load(q_rows[:, 3, :], "q_plane3"))
-        v_windows = [load(vT[0:P, :], "v_window0"), placed([P, T], F32, V_WINDOW1, "v_window1")]
-        nc.sync.dma_start(v_windows[1][:], vT[P:DV, :])
+        v_windows = [load(vT[e * P : (e + 1) * P, :], "v_window%d" % e) for e in range(V_CHUNKS)]
 
         k_grouped = sbuf([P, N, PACK], BF16, "k_grouped")
         nc.vector.tensor_copy(by_slot(k_grouped[:, :, 0]), k_planes[0][:].indirect(k_list[:]))
@@ -183,8 +181,8 @@ def tile_attend_mod_sorted_kernel(tc, xq, kT, vT, vs, offs, qoffs, out):
         q3 = quantize(q_chunks(3, 1), mx_tiles(P, "q3"))
         scores.append(product("bank3", columns(q3, 0, P), keys))
 
-        neg_max = [sbuf([P, 1], F32, "neg_max%d" % b)[:] for b in range(Q_CHUNKS - 1)]
-        neg_max.append(placed([P, 1], F32, V_RUN1 + 2 * ALIGN, "neg_max3")[:])
+        neg_max = [sbuf([P, 1], F32, "neg_max%d" % b)[:] for b in range(Q_CHUNKS)]
+        neg_max[2] = placed([P, P], F32, V_RUN1 - ALIGN, "neg_max2_wide")[:, 0:1]
 
         def maximum(b):
             nc.vector.tensor_reduce(neg_max[b], scores[b][:], AXIS_X, MAX, negate=True)
@@ -220,8 +218,9 @@ def tile_attend_mod_sorted_kernel(tc, xq, kT, vT, vs, offs, qoffs, out):
                 nc.tensor.transpose(bank[:, i, :], inv_total[h][:, i : i + 1].to_broadcast([P, P]), ident[:])
             return bank.rearrange("p b q -> p (b q)")
 
-        v0_run = placed([P, N], BF16, V_RUN1 + 3 * ALIGN, "v0_run")
+        v0_run = sbuf([P, N], BF16, "v0_run")
         nc.scalar.activation(v0_run[:], values_at(0, 0, N), COPY)
+        v0_turned = turn_pairs(v0_run[:], pair_bank("bank6"), True)
         total = sbuf([P, Q_CHUNKS], F32, "v_window0")
         for b in range(Q_CHUNKS):
             maximum(b)
@@ -241,46 +240,46 @@ def tile_attend_mod_sorted_kernel(tc, xq, kT, vT, vs, offs, qoffs, out):
         turned0 = turn_probs(probabilities(0, "u e s"), "bank4")
         turned1 = turn_probs(probabilities(1, "u e s"), "bank5")
         reciprocal(0)
-        spread0 = spread(0, pair_bank("bank6"))
+        spread0 = spread(0, pair_bank("bank0"))
         weights2 = sbuf([P, N], BF16, "weights2")
         nc.gpsimd.tensor_tensor(weights2[:], probabilities(2, "u s e")[:], vs_row[:], MULT)
         prob3 = probabilities(3, "u e s")
 
-        v_grouped = [sbuf([P, P, PACK], BF16, "v_grouped%d" % e) for e in range(V_CHUNKS)]
+        v_grouped = [placed([P, P, PACK], BF16, V_RUN1 - 4 * ALIGN, "v_grouped0"), sbuf([P, P, PACK], BF16, "v_grouped1")]
         w01_grouped = sbuf([P, HALF_Q, PACK], BF16, "w01_grouped")
         multiply_on_vector(turned0, w01_grouped[:, 0:P, :])
         multiply_on_vector(turned1, w01_grouped[:, P:HALF_Q, :])
-        copy_pairs(nc.scalar.copy, turn_pairs(v0_run[:], pair_bank("bank2"), True), v_grouped[0][:])
+        copy_pairs(nc.scalar.copy, v0_turned, v_grouped[0][:])
         v1_run = placed([P, N], BF16, V_RUN1, "v1_run")
         nc.scalar.activation(v1_run[:], values_at(1, 0, N), COPY)
         nc.vector.tensor_copy(inverse[0][:], spread0)
         turned3 = turn_probs(prob3, "bank7")
         reciprocal(1)
-        spread1 = spread(1, pair_bank("bank3"))
         w01 = columns(quantize(w01_grouped[:], mx_tiles(HALF_Q, "w01")), 0, HALF_Q)
         values0 = columns(quantize(v_grouped[0][:], mx_tiles(P, "v0")), 0, P)
+        w2_grouped = sbuf([P, P, PACK], BF16, "w2_grouped")
+        copy_pairs(nc.scalar.copy, turn_pairs(weights2[:], pair_bank("bank2")), w2_grouped[:])
         sums00 = product("bank1", values0, w01)
-        w2_grouped = placed([P, P, PACK], BF16, V_WINDOW1, "w2_grouped")
-        copy_pairs(nc.scalar.copy, turn_pairs(weights2[:], pair_bank("bank0")), w2_grouped[:])
-        nc.scalar.copy(inverse[1][:], spread1)
         w3_grouped = sbuf([P, P, PACK], BF16, "w3_grouped")
         multiply_on_vector(turned3, w3_grouped[:])
-        v1_turned = turn_pairs(v1_run[:], pair_bank("bank4"), True)
-        result00 = divide(placed([P, HALF_Q], F32, V_WINDOW1 + 4 * ALIGN, "result00"), sums00, 0)
+        v1_turned = turn_pairs(v1_run[:], pair_bank("bank7"), True)
+        result00 = divide(sbuf([P, HALF_Q], F32, "result00"), sums00, 0)
         nc.scalar.activation(window(0, 0), result00[:], COPY)
-        copy_pairs(nc.vector.tensor_copy, v1_turned, v_grouped[1][:])
-        w23_tiles = (sbuf([P, HALF_Q], U32, "w23_codes"), placed([P, HALF_Q], U8, V_RUN1 + ALIGN, "w23_scales"))
+        spread1 = spread(1, pair_bank("bank1"))
+        w23_tiles = mx_tiles(HALF_Q, "w23")
         quantize(w3_grouped[:], columns(w23_tiles, P, P))
         quantize(w2_grouped[:], columns(w23_tiles, 0, P))
         w23 = columns(w23_tiles, 0, HALF_Q)
         sums01 = product("bank5", values0, w23)
+        copy_pairs(nc.vector.tensor_copy, v1_turned, v_grouped[1][:])
+        nc.vector.tensor_copy(inverse[1][:], spread1)
         values1 = columns(quantize(v_grouped[1][:], mx_tiles(P, "v1")), 0, P)
-        sums10 = product("bank6", values1, w01)
-        sums11 = product("bank7", values1, w23)
+        sums10 = product("bank4", values1, w01)
+        sums11 = product("bank6", values1, w23)
         result01 = divide(sbuf([P, HALF_Q], F32, "result01"), sums01, 1)
         nc.scalar.activation(window(0, 1), result01[:], COPY)
         nc.sync.dma_start(out[0:P, :], out_windows[0][:])
-        result10 = divide(sbuf([P, HALF_Q], F32, "result10"), sums10, 0)
+        result10 = divide(sbuf([P, HALF_Q], F32, "v1_codes"), sums10, 0)
         result11 = divide(sbuf([P, HALF_Q], F32, "result11"), sums11, 1)
         nc.vector.tensor_copy(window(1, 0), result10[:])
         nc.vector.tensor_copy(window(1, 1), result11[:])

@@ -31,7 +31,6 @@ HALF_Q = NQ // HALVES
 HALF_N = N // HALVES
 CHUNKS_PER_HALF = Q_CHUNKS // HALVES
 ALIGN = 256
-V_RUN1 = 4 * T + 4 * ALIGN
 SIDE_BY_SIDE = "p t x -> p x t"
 
 FLOPS = 2 * NQ * N * D + 2 * NQ * N * DV
@@ -49,9 +48,6 @@ def tile_attend_mod_sorted_kernel(tc, xq, kT, vT, vs, offs, qoffs, out):
             return keep.tile(shape, dtype, align_bytes=ALIGN, name=name)
 
         def on_plane2(shape, dtype, offset, name):
-            return shared.tile(shape, dtype, align_bytes=ALIGN, offset=offset, name=name)
-
-        def placed(shape, dtype, offset, name):
             return shared.tile(shape, dtype, align_bytes=ALIGN, offset=offset, name=name)
 
         def load(rows, name):
@@ -182,7 +178,6 @@ def tile_attend_mod_sorted_kernel(tc, xq, kT, vT, vs, offs, qoffs, out):
         scores.append(product("bank3", columns(q3, 0, P), keys))
 
         neg_max = [sbuf([P, 1], F32, "neg_max%d" % b)[:] for b in range(Q_CHUNKS)]
-        neg_max[2] = placed([P, P], F32, V_RUN1 - ALIGN, "neg_max2_wide")[:, 0:1]
 
         def maximum(b):
             nc.vector.tensor_reduce(neg_max[b], scores[b][:], AXIS_X, MAX, negate=True)
@@ -245,12 +240,12 @@ def tile_attend_mod_sorted_kernel(tc, xq, kT, vT, vs, offs, qoffs, out):
         nc.gpsimd.tensor_tensor(weights2[:], probabilities(2, "u s e")[:], vs_row[:], MULT)
         prob3 = probabilities(3, "u e s")
 
-        v_grouped = [placed([P, P, PACK], BF16, V_RUN1 - 4 * ALIGN, "v_grouped0"), sbuf([P, P, PACK], BF16, "v_grouped1")]
+        v_grouped = [sbuf([P, P, PACK], BF16, "neg_max2"), sbuf([P, P, PACK], BF16, "v_grouped1")]
         w01_grouped = sbuf([P, HALF_Q, PACK], BF16, "w01_grouped")
         multiply_on_vector(turned0, w01_grouped[:, 0:P, :])
         multiply_on_vector(turned1, w01_grouped[:, P:HALF_Q, :])
         copy_pairs(nc.scalar.copy, v0_turned, v_grouped[0][:])
-        v1_run = placed([P, N], BF16, V_RUN1, "v1_run")
+        v1_run = sbuf([P, N], BF16, "prob2")
         nc.scalar.activation(v1_run[:], values_at(1, 0, N), COPY)
         nc.vector.tensor_copy(inverse[0][:], spread0)
         turned3 = turn_probs(prob3, "bank7")
@@ -279,7 +274,7 @@ def tile_attend_mod_sorted_kernel(tc, xq, kT, vT, vs, offs, qoffs, out):
         result01 = divide(sbuf([P, HALF_Q], F32, "result01"), sums01, 1)
         nc.scalar.activation(window(0, 1), result01[:], COPY)
         nc.sync.dma_start(out[0:P, :], out_windows[0][:])
-        result10 = divide(sbuf([P, HALF_Q], F32, "v1_codes"), sums10, 0)
+        result10 = divide(sbuf([P, HALF_Q], F32, "result10"), sums10, 0)
         result11 = divide(sbuf([P, HALF_Q], F32, "result11"), sums11, 1)
         nc.vector.tensor_copy(window(1, 0), result10[:])
         nc.vector.tensor_copy(window(1, 1), result11[:])

@@ -220,9 +220,10 @@ def tile_attend_mod_sorted_kernel(tc, xq, kT, vT, vs, offs, qoffs, out):
         for b in range(Q_CHUNKS):
             maximum(b)
 
-        inv_total = [sbuf([P, CHUNKS_PER_HALF], F32, "inv_total%d" % h) for h in range(HALVES)]
+        inv_total = []
 
-        def reciprocal(h):
+        def reciprocal(h, name):
+            inv_total.append(sbuf([P, CHUNKS_PER_HALF], F32, name))
             nc.vector.reciprocal(inv_total[h][:], total[:, h * CHUNKS_PER_HALF : (h + 1) * CHUNKS_PER_HALF])
 
         def window(e, h):
@@ -234,7 +235,7 @@ def tile_attend_mod_sorted_kernel(tc, xq, kT, vT, vs, offs, qoffs, out):
 
         turned0 = turn_probs(probabilities(0, "u e s"), "bank4")
         turned1 = turn_probs(probabilities(1, "u e s"), "bank5")
-        reciprocal(0)
+        reciprocal(0, "inv_total0")
         spread0 = spread(0, pair_bank("bank0"))
         weights2 = sbuf([P, N], BF16, "weights2")
         nc.gpsimd.tensor_tensor(weights2[:], probabilities(2, "u s e")[:], vs_row[:], MULT)
@@ -245,11 +246,10 @@ def tile_attend_mod_sorted_kernel(tc, xq, kT, vT, vs, offs, qoffs, out):
         multiply_on_vector(turned0, w01_grouped[:, 0:P, :])
         multiply_on_vector(turned1, w01_grouped[:, P:HALF_Q, :])
         copy_pairs(nc.scalar.copy, v0_turned, v_grouped[0][:])
-        v1_run = sbuf([P, N], BF16, "prob2")
+        nc.scalar.copy(inverse[0][:], spread0)
+        v1_run = sbuf([P, N], BF16, "prob1")
         nc.scalar.activation(v1_run[:], values_at(1, 0, N), COPY)
-        nc.vector.tensor_copy(inverse[0][:], spread0)
         turned3 = turn_probs(prob3, "bank7")
-        reciprocal(1)
         w01 = columns(quantize(w01_grouped[:], mx_tiles(HALF_Q, "w01")), 0, HALF_Q)
         values0 = columns(quantize(v_grouped[0][:], mx_tiles(P, "v0")), 0, P)
         w2_grouped = sbuf([P, P, PACK], BF16, "w2_grouped")
@@ -258,11 +258,12 @@ def tile_attend_mod_sorted_kernel(tc, xq, kT, vT, vs, offs, qoffs, out):
         w3_grouped = sbuf([P, P, PACK], BF16, "w3_grouped")
         multiply_on_vector(turned3, w3_grouped[:])
         v1_turned = turn_pairs(v1_run[:], pair_bank("bank7"), True)
-        result00 = divide(sbuf([P, HALF_Q], F32, "result00"), sums00, 0)
-        nc.scalar.activation(window(0, 0), result00[:], COPY)
-        spread1 = spread(1, pair_bank("bank1"))
+        reciprocal(1, "prob3")
+        spread1 = spread(1, pair_bank("bank3"))
         w23_tiles = mx_tiles(HALF_Q, "w23")
         quantize(w3_grouped[:], columns(w23_tiles, P, P))
+        result00 = divide(sbuf([P, HALF_Q], F32, "result00"), sums00, 0)
+        nc.scalar.activation(window(0, 0), result00[:], COPY)
         quantize(w2_grouped[:], columns(w23_tiles, 0, P))
         w23 = columns(w23_tiles, 0, HALF_Q)
         sums01 = product("bank5", values0, w23)

@@ -278,5 +278,5 @@ def tile_attend_mod_sorted_kernel(tc, xq, kT, vT, vs, offs, qoffs, out):
         result10 = divide(sbuf([P, HALF_Q], F32, "result10"), sums10, 0)
         result11 = divide(sbuf([P, HALF_Q], F32, "result11"), sums11, 1)
         nc.vector.tensor_copy(window(1, 0), result10[:])
-        nc.vector.tensor_copy(window(1, 1), result11[:])
+        nc.scalar.activation(window(1, 1), result11[:], COPY)
         nc.sync.dma_start(out[P:DV, :], out_windows[1][:])

@@ -31,6 +31,7 @@ HALF_Q = NQ // HALVES
 HALF_N = N // HALVES
 CHUNKS_PER_HALF = Q_CHUNKS // HALVES
 ALIGN = 256
+PROB1 = 8 * ALIGN
 SIDE_BY_SIDE = "p t x -> p x t"
 
 FLOPS = 2 * NQ * N * D + 2 * NQ * N * DV
@@ -74,10 +75,9 @@ def tile_attend_mod_sorted_kernel(tc, xq, kT, vT, vs, offs, qoffs, out):
             )
             return quantised
 
-        def product(bank_name, stationary, moving):
-            bank = psum.tile([P, moving[0].shape[1]], F32, name=bank_name)
+        def multiply(sums, stationary, moving):
             nc.tensor.matmul_mx(
-                out=bank[:],
+                out=sums,
                 lhsT=stationary[0].bitcast(FP8X4),
                 lhsT_scale=stationary[1],
                 rhs=moving[0].bitcast(FP8X4),
@@ -85,6 +85,10 @@ def tile_attend_mod_sorted_kernel(tc, xq, kT, vT, vs, offs, qoffs, out):
                 start=True,
                 stop=True,
             )
+
+        def product(bank_name, stationary, moving):
+            bank = psum.tile([P, moving[0].shape[1]], F32, name=bank_name)
+            multiply(bank[:], stationary, moving)
             return bank
 
         def pair_bank(bank_name):
@@ -183,7 +187,7 @@ def tile_attend_mod_sorted_kernel(tc, xq, kT, vT, vs, offs, qoffs, out):
             nc.vector.tensor_reduce(neg_max[b], scores[b][:], AXIS_X, MAX, negate=True)
 
         def probabilities(b, order):
-            prob = sbuf([P, N], F32, "prob%d" % b)
+            prob = on_plane2([P, N], F32, PROB1, "prob1") if b == 1 else sbuf([P, N], F32, "prob%d" % b)
             nc.scalar.activation(
                 prob[:].rearrange("p (%s) -> p %s" % (order, order), u=PAIR, e=PAIR),
                 scores[b][:].rearrange("p (u s e) -> p %s" % order, u=PAIR, e=PAIR),
@@ -241,20 +245,25 @@ def tile_attend_mod_sorted_kernel(tc, xq, kT, vT, vs, offs, qoffs, out):
         nc.gpsimd.tensor_tensor(weights2[:], probabilities(2, "u s e")[:], vs_row[:], MULT)
         prob3 = probabilities(3, "u e s")
 
-        v_grouped = [sbuf([P, P, PACK], BF16, "neg_max2"), sbuf([P, P, PACK], BF16, "v_grouped1")]
+        v_grouped = [sbuf([P, P, PACK], BF16, "prob0"), sbuf([P, P, PACK], BF16, "v_grouped1")]
         w01_grouped = sbuf([P, HALF_Q, PACK], BF16, "w01_grouped")
         multiply_on_vector(turned0, w01_grouped[:, 0:P, :])
+        copy_pairs(nc.vector.tensor_copy, v0_turned, v_grouped[0][:])
         multiply_on_vector(turned1, w01_grouped[:, P:HALF_Q, :])
-        copy_pairs(nc.scalar.copy, v0_turned, v_grouped[0][:])
         nc.scalar.copy(inverse[0][:], spread0)
-        v1_run = sbuf([P, N], BF16, "prob1")
+        v1_run = on_plane2([P, N], BF16, PROB1 + 4 * ALIGN, "v1_run")
         nc.scalar.activation(v1_run[:], values_at(1, 0, N), COPY)
         turned3 = turn_probs(prob3, "bank7")
-        w01 = columns(quantize(w01_grouped[:], mx_tiles(HALF_Q, "w01")), 0, HALF_Q)
-        values0 = columns(quantize(v_grouped[0][:], mx_tiles(P, "v0")), 0, P)
+        values0 = columns(quantize(v_grouped[0][:], (sbuf([P, P], U32, "v0_codes"), on_plane2([P, P], U8, PROB1, "v0_scales"))), 0, P)
+        w01_tiles = (sbuf([P, HALF_Q], U32, "w01_codes"), on_plane2([P, HALF_Q], U8, PROB1 + ALIGN, "w01_scales"))
+        for i in range(CHUNKS_PER_HALF):
+            quantize(w01_grouped[:, i * P : (i + 1) * P, :], columns(w01_tiles, i * P, P))
+        w01 = columns(w01_tiles, 0, HALF_Q)
         w2_grouped = sbuf([P, P, PACK], BF16, "w2_grouped")
         copy_pairs(nc.scalar.copy, turn_pairs(weights2[:], pair_bank("bank2")), w2_grouped[:])
-        sums00 = product("bank1", values0, w01)
+        sums00 = psum.tile([P, HALF_Q], F32, name="bank1")
+        for i in range(CHUNKS_PER_HALF):
+            multiply(sums00[:, i * P : (i + 1) * P], values0, columns(w01_tiles, i * P, P))
         w3_grouped = sbuf([P, P, PACK], BF16, "w3_grouped")
         multiply_on_vector(turned3, w3_grouped[:])
         v1_turned = turn_pairs(v1_run[:], pair_bank("bank7"), True)

@@ -256,14 +256,10 @@ def tile_attend_mod_sorted_kernel(tc, xq, kT, vT, vs, offs, qoffs, out):
         turned3 = turn_probs(prob3, "bank7")
         values0 = columns(quantize(v_grouped[0][:], (sbuf([P, P], U32, "v0_codes"), on_plane2([P, P], U8, PROB1, "v0_scales"))), 0, P)
         w01_tiles = (sbuf([P, HALF_Q], U32, "w01_codes"), on_plane2([P, HALF_Q], U8, PROB1 + ALIGN, "w01_scales"))
-        for i in range(CHUNKS_PER_HALF):
-            quantize(w01_grouped[:, i * P : (i + 1) * P, :], columns(w01_tiles, i * P, P))
-        w01 = columns(w01_tiles, 0, HALF_Q)
+        w01 = columns(quantize(w01_grouped[:], w01_tiles), 0, HALF_Q)
         w2_grouped = sbuf([P, P, PACK], BF16, "w2_grouped")
         copy_pairs(nc.scalar.copy, turn_pairs(weights2[:], pair_bank("bank2")), w2_grouped[:])
-        sums00 = psum.tile([P, HALF_Q], F32, name="bank1")
-        for i in range(CHUNKS_PER_HALF):
-            multiply(sums00[:, i * P : (i + 1) * P], values0, columns(w01_tiles, i * P, P))
+        sums00 = product("bank1", values0, w01)
         w3_grouped = sbuf([P, P, PACK], BF16, "w3_grouped")
         multiply_on_vector(turned3, w3_grouped[:])
         v1_turned = turn_pairs(v1_run[:], pair_bank("bank7"), True)

@@ -245,10 +245,10 @@ def tile_attend_mod_sorted_kernel(tc, xq, kT, vT, vs, offs, qoffs, out):
         nc.gpsimd.tensor_tensor(weights2[:], probabilities(2, "u s e")[:], vs_row[:], MULT)
         prob3 = probabilities(3, "u e s")
 
-        v_grouped = [sbuf([P, P, PACK], BF16, "prob0"), sbuf([P, P, PACK], BF16, "v_grouped1")]
+        v_grouped = [sbuf([P, P, PACK], BF16, "neg_max1"), sbuf([P, P, PACK], BF16, "v_grouped1")]
         w01_grouped = sbuf([P, HALF_Q, PACK], BF16, "w01_grouped")
-        multiply_on_vector(turned0, w01_grouped[:, 0:P, :])
         copy_pairs(nc.vector.tensor_copy, v0_turned, v_grouped[0][:])
+        multiply_on_vector(turned0, w01_grouped[:, 0:P, :])
         multiply_on_vector(turned1, w01_grouped[:, P:HALF_Q, :])
         nc.scalar.copy(inverse[0][:], spread0)
         v1_run = on_plane2([P, N], BF16, PROB1 + 4 * ALIGN, "v1_run")

@@ -238,20 +238,28 @@ def tile_attend_mod_sorted_kernel(tc, xq, kT, vT, vs, offs, qoffs, out):
             return result
 
         turned0 = turn_probs(probabilities(0, "u e s"), "bank4")
-        turned1 = turn_probs(probabilities(1, "u e s"), "bank5")
+        prob1 = probabilities(1, "u s e")
         reciprocal(0, "inv_total0")
         spread0 = spread(0, pair_bank("bank0"))
+        weights1 = sbuf([P, N], BF16, "weights1")
+        nc.vector.tensor_tensor(
+            weights1[:].rearrange("p (u s e) -> p u s e", u=PAIR, e=PAIR),
+            prob1[:].rearrange("p (u s e) -> p u s e", u=PAIR, e=PAIR),
+            row_bank[:].rearrange("p (u e) s -> p u s e", e=PAIR),
+            MULT,
+        )
+        w1_turned = turn_pairs(weights1[:], pair_bank("bank5"))
         weights2 = sbuf([P, N], BF16, "weights2")
         nc.gpsimd.tensor_tensor(weights2[:], probabilities(2, "u s e")[:], vs_row[:], MULT)
         prob3 = probabilities(3, "u e s")
 
         v_grouped = [sbuf([P, P, PACK], BF16, "neg_max1"), sbuf([P, P, PACK], BF16, "v_grouped1")]
         w01_grouped = sbuf([P, HALF_Q, PACK], BF16, "w01_grouped")
-        copy_pairs(nc.vector.tensor_copy, v0_turned, v_grouped[0][:])
         multiply_on_vector(turned0, w01_grouped[:, 0:P, :])
-        multiply_on_vector(turned1, w01_grouped[:, P:HALF_Q, :])
+        copy_pairs(nc.vector.tensor_copy, v0_turned, v_grouped[0][:])
         nc.scalar.copy(inverse[0][:], spread0)
-        v1_run = on_plane2([P, N], BF16, PROB1 + 4 * ALIGN, "v1_run")
+        copy_pairs(nc.scalar.copy, w1_turned, w01_grouped[:, P:HALF_Q, :])
+        v1_run = sbuf([P, N], BF16, "weights1")
         nc.scalar.activation(v1_run[:], values_at(1, 0, N), COPY)
         turned3 = turn_probs(prob3, "bank7")
         values0 = columns(quantize(v_grouped[0][:], (sbuf([P, P], U32, "v0_codes"), on_plane2([P, P], U8, PROB1, "v0_scales"))), 0, P)
@@ -260,7 +268,7 @@ def tile_attend_mod_sorted_kernel(tc, xq, kT, vT, vs, offs, qoffs, out):
         w2_grouped = sbuf([P, P, PACK], BF16, "w2_grouped")
         copy_pairs(nc.scalar.copy, turn_pairs(weights2[:], pair_bank("bank2")), w2_grouped[:])
         sums00 = product("bank1", values0, w01)
-        w3_grouped = sbuf([P, P, PACK], BF16, "w3_grouped")
+        w3_grouped = sbuf([P, P, PACK], BF16, "neg_max1")
         multiply_on_vector(turned3, w3_grouped[:])
         v1_turned = turn_pairs(v1_run[:], pair_bank("bank7"), True)
         reciprocal(1, "prob3")

@@ -217,12 +217,8 @@ def tile_attend_mod_sorted_kernel(tc, xq, kT, vT, vs, offs, qoffs, out):
                 nc.tensor.transpose(bank[:, i, :], inv_total[h][:, i : i + 1].to_broadcast([P, P]), ident[:])
             return bank.rearrange("p b q -> p (b q)")
 
-        v0_run = sbuf([P, N], BF16, "v0_run")
-        nc.scalar.activation(v0_run[:], values_at(0, 0, N), COPY)
-        v0_turned = turn_pairs(v0_run[:], pair_bank("bank6"), True)
-        total = sbuf([P, Q_CHUNKS], F32, "v_window0")
-        for b in range(Q_CHUNKS):
-            maximum(b)
+        def window(e, first, count):
+            return out_windows[e][:].indirect(entries(q_list, first, count))
 
         inv_total = []
 
@@ -230,66 +226,62 @@ def tile_attend_mod_sorted_kernel(tc, xq, kT, vT, vs, offs, qoffs, out):
             inv_total.append(sbuf([P, CHUNKS_PER_HALF], F32, name))
             nc.vector.reciprocal(inv_total[h][:], total[:, h * CHUNKS_PER_HALF : (h + 1) * CHUNKS_PER_HALF])
 
-        def window(e, h):
-            return out_windows[e][:].indirect(entries(q_list, h * HALF_Q, HALF_Q))
-
         def divide(result, bank, h):
-            nc.vector.tensor_tensor(result[:], bank[:], inverse[h][:], MULT)
-            return result
+            nc.vector.tensor_tensor(result, bank[:], inverse[h][:], MULT)
+
+        v0_run = sbuf([P, N], BF16, "v0_run")
+        nc.scalar.activation(v0_run[:], values_at(0, 0, N), COPY)
+        total = sbuf([P, Q_CHUNKS], F32, "v_window0")
+        for b in range(Q_CHUNKS):
+            maximum(b)
 
         turned0 = turn_probs(probabilities(0, "u e s"), "bank4")
-        prob1 = probabilities(1, "u s e")
+        turned1 = turn_probs(probabilities(1, "u e s"), "bank5")
+        v0_turned = turn_pairs(v0_run[:], pair_bank("bank1"), True)
         reciprocal(0, "inv_total0")
-        spread0 = spread(0, pair_bank("bank0"))
-        weights1 = sbuf([P, N], BF16, "weights1")
-        nc.vector.tensor_tensor(
-            weights1[:].rearrange("p (u s e) -> p u s e", u=PAIR, e=PAIR),
-            prob1[:].rearrange("p (u s e) -> p u s e", u=PAIR, e=PAIR),
-            row_bank[:].rearrange("p (u e) s -> p u s e", e=PAIR),
-            MULT,
-        )
-        w1_turned = turn_pairs(weights1[:], pair_bank("bank5"))
         weights2 = sbuf([P, N], BF16, "weights2")
         nc.gpsimd.tensor_tensor(weights2[:], probabilities(2, "u s e")[:], vs_row[:], MULT)
         prob3 = probabilities(3, "u e s")
-
-        v_grouped = [sbuf([P, P, PACK], BF16, "neg_max1"), sbuf([P, P, PACK], BF16, "v_grouped1")]
-        w01_grouped = sbuf([P, HALF_Q, PACK], BF16, "w01_grouped")
-        multiply_on_vector(turned0, w01_grouped[:, 0:P, :])
-        copy_pairs(nc.vector.tensor_copy, v0_turned, v_grouped[0][:])
-        nc.scalar.copy(inverse[0][:], spread0)
-        copy_pairs(nc.scalar.copy, w1_turned, w01_grouped[:, P:HALF_Q, :])
-        v1_run = sbuf([P, N], BF16, "weights1")
+        v1_run = sbuf([P, N], BF16, "neg_max3")
         nc.scalar.activation(v1_run[:], values_at(1, 0, N), COPY)
         turned3 = turn_probs(prob3, "bank7")
-        values0 = columns(quantize(v_grouped[0][:], (sbuf([P, P], U32, "v0_codes"), on_plane2([P, P], U8, PROB1, "v0_scales"))), 0, P)
-        w01_tiles = (sbuf([P, HALF_Q], U32, "w01_codes"), on_plane2([P, HALF_Q], U8, PROB1 + ALIGN, "w01_scales"))
-        w01 = columns(quantize(w01_grouped[:], w01_tiles), 0, HALF_Q)
+        spread0 = spread(0, pair_bank("bank0"))
+
+        w01_grouped = sbuf([P, HALF_Q, PACK], BF16, "w01_grouped")
+        multiply_on_vector(turned0, w01_grouped[:, 0:P, :])
+        multiply_on_vector(turned1, w01_grouped[:, P:HALF_Q, :])
+        v_grouped = [sbuf([P, P, PACK], BF16, "v_grouped%d" % e) for e in range(V_CHUNKS)]
+        copy_pairs(nc.vector.tensor_copy, v0_turned, v_grouped[0][:])
+        w01 = columns(quantize(w01_grouped[:], mx_tiles(HALF_Q, "w01")), 0, HALF_Q)
+        values0 = columns(quantize(v_grouped[0][:], mx_tiles(P, "v0")), 0, P)
+        nc.scalar.copy(inverse[0][:], spread0)
         w2_grouped = sbuf([P, P, PACK], BF16, "w2_grouped")
         copy_pairs(nc.scalar.copy, turn_pairs(weights2[:], pair_bank("bank2")), w2_grouped[:])
-        sums00 = product("bank1", values0, w01)
-        w3_grouped = sbuf([P, P, PACK], BF16, "neg_max1")
+        sums00 = product("bank6", values0, w01)
+        w3_grouped = sbuf([P, P, PACK], BF16, "v_grouped0")
         multiply_on_vector(turned3, w3_grouped[:])
         v1_turned = turn_pairs(v1_run[:], pair_bank("bank7"), True)
         reciprocal(1, "prob3")
         spread1 = spread(1, pair_bank("bank3"))
         w23_tiles = mx_tiles(HALF_Q, "w23")
-        quantize(w3_grouped[:], columns(w23_tiles, P, P))
-        result00 = divide(sbuf([P, HALF_Q], F32, "result00"), sums00, 0)
-        nc.scalar.activation(window(0, 0), result00[:], COPY)
         quantize(w2_grouped[:], columns(w23_tiles, 0, P))
+        result00 = sbuf([P, HALF_Q], F32, "result00")
+        divide(result00[:], sums00, 0)
+        nc.scalar.activation(window(0, 0, HALF_Q), result00[:], COPY)
+        quantize(w3_grouped[:], columns(w23_tiles, P, P))
         w23 = columns(w23_tiles, 0, HALF_Q)
         sums01 = product("bank5", values0, w23)
         copy_pairs(nc.vector.tensor_copy, v1_turned, v_grouped[1][:])
         nc.vector.tensor_copy(inverse[1][:], spread1)
         values1 = columns(quantize(v_grouped[1][:], mx_tiles(P, "v1")), 0, P)
         sums10 = product("bank4", values1, w01)
-        sums11 = product("bank6", values1, w23)
-        result01 = divide(sbuf([P, HALF_Q], F32, "result01"), sums01, 1)
-        nc.scalar.activation(window(0, 1), result01[:], COPY)
+        sums11 = product("bank1", values1, w23)
+        result01 = sbuf([P, HALF_Q], F32, "result01")
+        divide(result01[:], sums01, 1)
+        nc.scalar.activation(window(0, HALF_Q, HALF_Q), result01[:], COPY)
         nc.sync.dma_start(out[0:P, :], out_windows[0][:])
-        result10 = divide(sbuf([P, HALF_Q], F32, "result10"), sums10, 0)
-        result11 = divide(sbuf([P, HALF_Q], F32, "result11"), sums11, 1)
-        nc.vector.tensor_copy(window(1, 0), result10[:])
-        nc.scalar.activation(window(1, 1), result11[:], COPY)
+        result1 = sbuf([P, NQ], F32, "result1")
+        divide(result1[:, 0:HALF_Q], sums10, 0)
+        divide(result1[:, HALF_Q:NQ], sums11, 1)
+        nc.vector.tensor_copy(window(1, 0, NQ), result1[:])
         nc.sync.dma_start(out[P:DV, :], out_windows[1][:])

@@ -32,6 +32,7 @@ HALF_N = N // HALVES
 CHUNKS_PER_HALF = Q_CHUNKS // HALVES
 ALIGN = 256
 PROB1 = 8 * ALIGN
+VALUES0 = 20 * ALIGN
 SIDE_BY_SIDE = "p t x -> p x t"
 
 FLOPS = 2 * NQ * N * D + 2 * NQ * N * DV
@@ -181,7 +182,9 @@ def tile_attend_mod_sorted_kernel(tc, xq, kT, vT, vs, offs, qoffs, out):
         q3 = quantize(q_chunks(3, 1), mx_tiles(P, "q3"))
         scores.append(product("bank3", columns(q3, 0, P), keys))
 
-        neg_max = [sbuf([P, 1], F32, "neg_max%d" % b)[:] for b in range(Q_CHUNKS)]
+        neg_max = [sbuf([P, 1], F32, "neg_max%d" % b)[:] for b in (0, 1)]
+        neg_max.append(on_plane2([P, 1], F32, VALUES0, "neg_max2")[:])
+        neg_max.append(sbuf([P, 1], F32, "neg_max3")[:])
 
         def maximum(b):
             nc.vector.tensor_reduce(neg_max[b], scores[b][:], AXIS_X, MAX, negate=True)
@@ -231,17 +234,19 @@ def tile_attend_mod_sorted_kernel(tc, xq, kT, vT, vs, offs, qoffs, out):
 
         v0_run = sbuf([P, N], BF16, "v0_run")
         nc.scalar.activation(v0_run[:], values_at(0, 0, N), COPY)
+        v0_turned = turn_pairs(v0_run[:], pair_bank("bank6"), True)
         total = sbuf([P, Q_CHUNKS], F32, "v_window0")
         for b in range(Q_CHUNKS):
             maximum(b)
 
         turned0 = turn_probs(probabilities(0, "u e s"), "bank4")
         turned1 = turn_probs(probabilities(1, "u e s"), "bank5")
-        v0_turned = turn_pairs(v0_run[:], pair_bank("bank1"), True)
         reciprocal(0, "inv_total0")
         weights2 = sbuf([P, N], BF16, "weights2")
         nc.gpsimd.tensor_tensor(weights2[:], probabilities(2, "u s e")[:], vs_row[:], MULT)
         prob3 = probabilities(3, "u e s")
+        v_grouped = [on_plane2([P, P, PACK], BF16, VALUES0, "v_grouped0"), sbuf([P, P, PACK], BF16, "v_grouped1")]
+        copy_pairs(nc.scalar.copy, v0_turned, v_grouped[0][:])
         v1_run = sbuf([P, N], BF16, "neg_max3")
         nc.scalar.activation(v1_run[:], values_at(1, 0, N), COPY)
         turned3 = turn_probs(prob3, "bank7")
@@ -250,32 +255,26 @@ def tile_attend_mod_sorted_kernel(tc, xq, kT, vT, vs, offs, qoffs, out):
         w01_grouped = sbuf([P, HALF_Q, PACK], BF16, "w01_grouped")
         multiply_on_vector(turned0, w01_grouped[:, 0:P, :])
         multiply_on_vector(turned1, w01_grouped[:, P:HALF_Q, :])
-        v_grouped = [sbuf([P, P, PACK], BF16, "v_grouped%d" % e) for e in range(V_CHUNKS)]
-        copy_pairs(nc.vector.tensor_copy, v0_turned, v_grouped[0][:])
+        values0 = columns(quantize(v_grouped[0][:], mx_tiles(P, "v0", "v0_codes")), 0, P)
         w01 = columns(quantize(w01_grouped[:], mx_tiles(HALF_Q, "w01")), 0, HALF_Q)
-        values0 = columns(quantize(v_grouped[0][:], mx_tiles(P, "v0")), 0, P)
-        nc.scalar.copy(inverse[0][:], spread0)
-        w2_grouped = sbuf([P, P, PACK], BF16, "w2_grouped")
-        copy_pairs(nc.scalar.copy, turn_pairs(weights2[:], pair_bank("bank2")), w2_grouped[:])
-        sums00 = product("bank6", values0, w01)
-        w3_grouped = sbuf([P, P, PACK], BF16, "v_grouped0")
-        multiply_on_vector(turned3, w3_grouped[:])
+        w23_grouped = on_plane2([P, HALF_Q, PACK], BF16, VALUES0, "w23_grouped")
+        copy_pairs(nc.scalar.copy, turn_pairs(weights2[:], pair_bank("bank2")), w23_grouped[:, 0:P, :])
+        sums00 = product("bank1", values0, w01)
+        nc.vector.tensor_copy(inverse[0][:], spread0)
+        multiply_on_vector(turned3, w23_grouped[:, P:HALF_Q, :])
         v1_turned = turn_pairs(v1_run[:], pair_bank("bank7"), True)
         reciprocal(1, "prob3")
         spread1 = spread(1, pair_bank("bank3"))
-        w23_tiles = mx_tiles(HALF_Q, "w23")
-        quantize(w2_grouped[:], columns(w23_tiles, 0, P))
         result00 = sbuf([P, HALF_Q], F32, "result00")
         divide(result00[:], sums00, 0)
         nc.scalar.activation(window(0, 0, HALF_Q), result00[:], COPY)
-        quantize(w3_grouped[:], columns(w23_tiles, P, P))
-        w23 = columns(w23_tiles, 0, HALF_Q)
+        w23 = columns(quantize(w23_grouped[:], mx_tiles(HALF_Q, "w23")), 0, HALF_Q)
         sums01 = product("bank5", values0, w23)
         copy_pairs(nc.vector.tensor_copy, v1_turned, v_grouped[1][:])
         nc.vector.tensor_copy(inverse[1][:], spread1)
         values1 = columns(quantize(v_grouped[1][:], mx_tiles(P, "v1")), 0, P)
         sums10 = product("bank4", values1, w01)
-        sums11 = product("bank1", values1, w23)
+        sums11 = product("bank6", values1, w23)
         result01 = sbuf([P, HALF_Q], F32, "result01")
         divide(result01[:], sums01, 1)
         nc.scalar.activation(window(0, HALF_Q, HALF_Q), result01[:], COPY)

from contextlib import ExitStack

import concourse.mybir as mybir
from concourse.masks import make_identity

F32 = mybir.dt.float32
BF16 = mybir.dt.bfloat16
U32 = mybir.dt.uint32
U16 = mybir.dt.uint16
U8 = mybir.dt.uint8
FP8X4 = mybir.dt.float8_e4m3fn_x4
EXP = mybir.ActivationFunctionType.Exp
MULT = mybir.AluOpType.mult
MAX = mybir.AluOpType.max
COPY = mybir.ActivationFunctionType.Copy
AXIS_X = mybir.AxisListType.X

P = 128
PACK = 4
PAIR = 2
T = 2048
D = 512
DV = 256
N = 512
NQ = 512
PER_LIST_COLUMN = 16
Q_CHUNKS = NQ // P
V_CHUNKS = DV // P
HALVES = 2
HALF_Q = NQ // HALVES
HALF_N = N // HALVES
CHUNKS_PER_HALF = Q_CHUNKS // HALVES
ALIGN = 256
PROB1 = 8 * ALIGN
VALUES0 = 20 * ALIGN
SIDE_BY_SIDE = "p t x -> p x t"

FLOPS = 2 * NQ * N * D + 2 * NQ * N * DV
BYTES = 4 * (2 * D * T + DV * T + T + DV * T) + 2 * P * (N + NQ) // PER_LIST_COLUMN


def tile_attend_mod_sorted_kernel(tc, xq, kT, vT, vs, offs, qoffs, out):
    nc = tc.nc
    with ExitStack() as ctx:
        keep = ctx.enter_context(tc.tile_pool(name="keep", bufs=1))
        shared = ctx.enter_context(tc.tile_pool(name="shared", bufs=1))
        psum = ctx.enter_context(tc.psum_pool(name="psum", bufs=1))

        def sbuf(shape, dtype, name):
            return keep.tile(shape, dtype, align_bytes=ALIGN, name=name)

        def on_plane2(shape, dtype, offset, name):
            return shared.tile(shape, dtype, align_bytes=ALIGN, offset=offset, name=name)

        def load(rows, name):
            tile = sbuf(list(rows.shape), F32, name)
            nc.sync.dma_start(tile[:], rows)
            return tile

        def entries(listed, first, count):
            return listed[:, first // PER_LIST_COLUMN : (first + count) // PER_LIST_COLUMN]

        def by_slot(paired):
            return paired.rearrange("p (u s e) -> p s u e", u=PAIR, e=PAIR)

        def mx_tiles(width, name, codes_name=None):
            return sbuf([P, width], U32, codes_name or name + "_codes"), sbuf([P, width], U8, name + "_scales")

        def columns(quantised, first, count):
            return [tile[:, first : first + count] for tile in quantised]

        def quantize(grouped, quantised):
            codes, scales = quantised
            nc.vector.quantize_mx(
                out=codes[:].bitcast(FP8X4), scales=scales[:], in_=grouped.rearrange("p c t -> p (c t)")
            )
            return quantised

        def multiply(sums, stationary, moving):
            nc.tensor.matmul_mx(
                out=sums,
                lhsT=stationary[0].bitcast(FP8X4),
                lhsT_scale=stationary[1],
                rhs=moving[0].bitcast(FP8X4),
                rhs_scale=moving[1],
                start=True,
                stop=True,
            )

        def product(bank_name, stationary, moving):
            bank = psum.tile([P, moving[0].shape[1]], F32, name=bank_name)
            multiply(bank[:], stationary, moving)
            return bank

        def pair_bank(bank_name):
            return psum.tile([P, PAIR, P], F32, name=bank_name)[:]

        def turn_pairs(paired, bank, in_slot_order=False):
            words = paired.bitcast(F32)
            for u in range(PAIR):
                run = words[:, u::PAIR] if in_slot_order else words[:, u * P : (u + 1) * P]
                nc.tensor.transpose(bank[:, u, :], run, ident[:])
            return bank

        def copy_pairs(copy, turned, grouped):
            grouped_words = grouped.rearrange("p x t -> p (x t)").bitcast(F32).rearrange("p (x u) -> p x u", u=PAIR)
            copy(grouped_words, turned.rearrange(SIDE_BY_SIDE))

        k_list = sbuf([P, N // PER_LIST_COLUMN], U16, "k_list")
        q_list = sbuf([P, NQ // PER_LIST_COLUMN], U16, "q_list")
        k_rows = kT.rearrange("(p t) c -> p t c", t=PACK)
        q_rows = xq.rearrange("(p t) c -> p t c", t=PACK)
        k_planes = [sbuf([P, T], F32, "k_plane0")]
        nc.sync.dma_start(k_planes[0][:, 0 : T // 2], k_rows[:, 0, 0 : T // 2])
        nc.scalar.dma_start(k_planes[0][:, T // 2 : T], k_rows[:, 0, T // 2 : T])
        nc.sync.dma_start(k_list[:], offs)
        k_planes.append(load(k_rows[:, 1, :], "k_plane1"))

        vs_window = sbuf([P, T], F32, "vs_window")
        nc.vector.memset(vs_window[:], 0.0)
        ident = sbuf([P, P], F32, "ident")
        make_identity(nc, ident[:])
        out_windows = [sbuf([P, T], F32, "out_window%d" % e) for e in range(V_CHUNKS)]
        for window in out_windows:
            nc.gpsimd.memset(window[:], 0.0)

        nc.sync.dma_start(vs_window[0:1, :], vs[0:1, :])
        k_planes.extend([load(k_rows[:, t, :], "k_plane%d" % t) for t in range(2, PACK)])
        nc.sync.dma_start(q_list[:], qoffs)
        q_planes = [load(q_rows[:, t, :], "q_plane%d" % t) for t in range(2)]
        q_planes.append(on_plane2([P, T], F32, 0, "q_plane2"))
        nc.sync.dma_start(q_planes[2][:], q_rows[:, 2, :])
        q_planes.append(load(q_rows[:, 3, :], "q_plane3"))
        v_windows = [load(vT[e * P : (e + 1) * P, :], "v_window%d" % e) for e in range(V_CHUNKS)]

        k_grouped = sbuf([P, N, PACK], BF16, "k_grouped")
        nc.vector.tensor_copy(by_slot(k_grouped[:, :, 0]), k_planes[0][:].indirect(k_list[:]))

        vs_picked = sbuf([P, N], F32, "vs_picked")
        nc.vector.tensor_copy(vs_picked[:], vs_window[:].indirect(k_list[:]))
        column_bank = psum.tile([P, PACK, P], F32, name="bank4")
        for t in range(PACK):
            nc.tensor.transpose(column_bank[:, t, :], vs_picked[:, t::PACK], ident[:])
        vs_column = sbuf([P, PACK], F32, "vs_column")
        nc.scalar.copy(vs_column[:], column_bank[:, :, 0])
        row_bank = psum.tile([P, PACK, P], F32, name="bank5")
        for t in range(PACK):
            nc.tensor.transpose(row_bank[:, t, :], vs_column[:, t : t + 1].to_broadcast([P, P]), ident[:])
        vs_row = sbuf([P, N], F32, "vs_row")
        nc.scalar.copy(
            vs_row[:].rearrange("p (u s e) -> p u s e", u=PAIR, e=PAIR),
            row_bank[:].rearrange("p (u e) s -> p u s e", e=PAIR),
        )

        for t in range(1, PACK):
            nc.vector.tensor_copy(by_slot(k_grouped[:, :, t]), k_planes[t][:].indirect(k_list[:]))
        keys = columns(quantize(k_grouped[:], mx_tiles(N, "k")), 0, N)

        q_grouped = sbuf([P, NQ, PACK], BF16, "q_grouped")
        for t in range(PACK - 1):
            nc.vector.tensor_copy(q_grouped[:, :, t], q_planes[t][:].indirect(q_list[:]))

        def last_plane(first, count):
            return q_planes[PACK - 1][:].indirect(entries(q_list, first, count))

        def q_chunks(first, count):
            return q_grouped[:, first * P : (first + count) * P, :]

        run0 = [on_plane2([P, P // 2], BF16, i * ALIGN, "run0_%d" % i) for i in range(2)]
        for i in range(2):
            nc.scalar.activation(run0[i][:], last_plane(i * P // 2, P // 2), COPY)
        for i in range(2):
            nc.scalar.copy(q_grouped[:, i * P // 2 : (i + 1) * P // 2, PACK - 1], run0[i][:])
        nc.vector.tensor_copy(q_chunks(1, 2)[:, :, PACK - 1], last_plane(P, 2 * P))
        q0 = quantize(q_chunks(0, 1), mx_tiles(P, "q0"))
        scores = [product("bank0", columns(q0, 0, P), keys)]
        run3 = on_plane2([P, P], BF16, 0, "run3")
        nc.scalar.activation(run3[:], last_plane(3 * P, P), COPY)
        nc.scalar.copy(q_chunks(3, 1)[:, :, PACK - 1], run3[:])
        q12 = quantize(q_chunks(1, 2), (sbuf([P, 2 * P], U32, "q12_codes"), on_plane2([P, 2 * P], U8, ALIGN, "q12_scales")))
        scores.extend([product("bank%d" % (1 + i), columns(q12, i * P, P), keys) for i in range(2)])
        q3 = quantize(q_chunks(3, 1), mx_tiles(P, "q3"))
        scores.append(product("bank3", columns(q3, 0, P), keys))

        neg_max = [sbuf([P, 1], F32, "neg_max%d" % b)[:] for b in (0, 1)]
        neg_max.append(on_plane2([P, 1], F32, VALUES0, "neg_max2")[:])
        neg_max.append(sbuf([P, 1], F32, "neg_max3")[:])

        def maximum(b):
            nc.vector.tensor_reduce(neg_max[b], scores[b][:], AXIS_X, MAX, negate=True)

        def probabilities(b, order):
            prob = on_plane2([P, N], F32, PROB1, "prob1") if b == 1 else sbuf([P, N], F32, "prob%d" % b)
            nc.scalar.activation(
                prob[:].rearrange("p (%s) -> p %s" % (order, order), u=PAIR, e=PAIR),
                scores[b][:].rearrange("p (u s e) -> p %s" % order, u=PAIR, e=PAIR),
                EXP,
                bias=neg_max[b],
                accum_out=total[:, b : b + 1],
            )
            return prob

        def turn_probs(prob, bank_name):
            bank = psum.tile([P, PACK, P], F32, name=bank_name)
            for t in range(PACK):
                nc.tensor.transpose(bank[:, t, :], prob[:, t * P : (t + 1) * P], ident[:])
            return bank

        def multiply_on_vector(turned, grouped):
            scales = vs_column[:].unsqueeze(1).to_broadcast([P, P, PACK])
            nc.vector.tensor_tensor(grouped, turned[:].rearrange(SIDE_BY_SIDE), scales, MULT)

        def values_at(e, first, count):
            return v_windows[e][:].indirect(entries(k_list, first, count))

        inverse = [sbuf([P, HALF_Q], F32, "inverse%d" % h) for h in range(HALVES)]

        def spread(h, bank):
            for i in range(CHUNKS_PER_HALF):
                nc.tensor.transpose(bank[:, i, :], inv_total[h][:, i : i + 1].to_broadcast([P, P]), ident[:])
            return bank.rearrange("p b q -> p (b q)")

        def window(e, first, count):
            return out_windows[e][:].indirect(entries(q_list, first, count))

        inv_total = []

        def reciprocal(h, name):
            inv_total.append(sbuf([P, CHUNKS_PER_HALF], F32, name))
            nc.vector.reciprocal(inv_total[h][:], total[:, h * CHUNKS_PER_HALF : (h + 1) * CHUNKS_PER_HALF])

        def divide(result, bank, h):
            nc.vector.tensor_tensor(result, bank[:], inverse[h][:], MULT)

        v0_run = sbuf([P, N], BF16, "v0_run")
        nc.scalar.activation(v0_run[:], values_at(0, 0, N), COPY)
        v0_turned = turn_pairs(v0_run[:], pair_bank("bank6"), True)
        total = sbuf([P, Q_CHUNKS], F32, "v_window0")
        for b in range(Q_CHUNKS):
            maximum(b)

        turned0 = turn_probs(probabilities(0, "u e s"), "bank4")
        turned1 = turn_probs(probabilities(1, "u e s"), "bank5")
        reciprocal(0, "inv_total0")
        weights2 = sbuf([P, N], BF16, "weights2")
        nc.gpsimd.tensor_tensor(weights2[:], probabilities(2, "u s e")[:], vs_row[:], MULT)
        prob3 = probabilities(3, "u e s")
        v_grouped = [on_plane2([P, P, PACK], BF16, VALUES0, "v_grouped0"), sbuf([P, P, PACK], BF16, "v_grouped1")]
        copy_pairs(nc.scalar.copy, v0_turned, v_grouped[0][:])
        v1_run = sbuf([P, N], BF16, "neg_max3")
        nc.scalar.activation(v1_run[:], values_at(1, 0, N), COPY)
        turned3 = turn_probs(prob3, "bank7")
        spread0 = spread(0, pair_bank("bank0"))

        w01_grouped = sbuf([P, HALF_Q, PACK], BF16, "w01_grouped")
        multiply_on_vector(turned0, w01_grouped[:, 0:P, :])
        multiply_on_vector(turned1, w01_grouped[:, P:HALF_Q, :])
        values0 = columns(quantize(v_grouped[0][:], mx_tiles(P, "v0", "v0_codes")), 0, P)
        w01 = columns(quantize(w01_grouped[:], mx_tiles(HALF_Q, "w01")), 0, HALF_Q)
        w23_grouped = on_plane2([P, HALF_Q, PACK], BF16, VALUES0, "w23_grouped")
        copy_pairs(nc.scalar.copy, turn_pairs(weights2[:], pair_bank("bank2")), w23_grouped[:, 0:P, :])
        sums00 = product("bank1", values0, w01)
        nc.vector.tensor_copy(inverse[0][:], spread0)
        multiply_on_vector(turned3, w23_grouped[:, P:HALF_Q, :])
        v1_turned = turn_pairs(v1_run[:], pair_bank("bank7"), True)
        reciprocal(1, "prob3")
        spread1 = spread(1, pair_bank("bank3"))
        result00 = sbuf([P, HALF_Q], F32, "result00")
        divide(result00[:], sums00, 0)
        nc.scalar.activation(window(0, 0, HALF_Q), result00[:], COPY)
        w23 = columns(quantize(w23_grouped[:], mx_tiles(HALF_Q, "w23")), 0, HALF_Q)
        sums01 = product("bank5", values0, w23)
        copy_pairs(nc.vector.tensor_copy, v1_turned, v_grouped[1][:])
        nc.vector.tensor_copy(inverse[1][:], spread1)
        values1 = columns(quantize(v_grouped[1][:], mx_tiles(P, "v1")), 0, P)
        sums10 = product("bank4", values1, w01)
        sums11 = product("bank6", values1, w23)
        result01 = sbuf([P, HALF_Q], F32, "result01")
        divide(result01[:], sums01, 1)
        nc.scalar.activation(window(0, HALF_Q, HALF_Q), result01[:], COPY)
        nc.sync.dma_start(out[0:P, :], out_windows[0][:])
        result1 = sbuf([P, NQ], F32, "result1")
        divide(result1[:, 0:HALF_Q], sums10, 0)
        divide(result1[:, HALF_Q:NQ], sums11, 1)
        nc.vector.tensor_copy(window(1, 0, NQ), result1[:])
        nc.sync.dma_start(out[P:DV, :], out_windows[1][:])
